import numpy as np, ml_dtypes
CORES = [40,41,42,43,44,45,46,47]
N = 8
BF = ml_dtypes.bfloat16
W, A, T, M, RO, EPS, TH = 4096, 1024, 192, 5, 4, 40, 800
WT = 15 * np.arange(16) + 7
RI, GI = np.arange(N)[:, None, None], np.arange(8)[None, :, None]
def clue(d):
    return np.add.reduce(d * WT, axis=-1)
def side(v):
    return (5 * v + (v >> 2)) & (A - 1)
def apart(cand, used):
    v = clue(cand); p, c = v & (A - 1), side(v)
    return cand[np.argmax((p != c) & ~np.isin(p, used) & ~np.isin(c, used))]
def rows128(a):
    return np.ascontiguousarray(np.swapaxes(a, 2, 3)).reshape(N, 128, -1)
def pack(X, S, K, z, l):
    return {"x0": rows128(X).astype(np.float32).astype(BF), "asc": rows128(S).astype(np.int32), "kw": rows128(K).astype(np.int32), "z0": rows128(z).astype(np.float32).astype(BF), "l0": np.ascontiguousarray(l).astype(np.int32)}
def parts(rng):
    mid = rng.integers(0, 256, (8, 32, 16)); order = np.argsort(rng.random((N, 8, W)), axis=-1); h = W >> 1
    X = rng.integers(0, 256, (N, 8, W, 16))
    X[RI, GI, order[:, :, :h]] = np.clip(mid[None, :, np.arange(h) % 32] + rng.integers(-20, 21, (N, 8, h, 16)), 0, 255)
    c = rng.integers(0, 32, (N, 8, T)); m = rng.random((N, 8, T, 1))
    z = np.clip(mid[GI, c] + rng.integers(-20, 21, (N, 8, T, 16)), 0, 255)
    z = np.where(m < 0.5, z, np.where(m < 0.8, rng.integers(0, 256, z.shape), rng.integers(96, 160, z.shape)))
    own = order[RI[..., None], GI[..., None], c[..., None] + 32 * rng.integers(0, W >> 6, (N, 8, T, 16))]
    share = rng.choice(np.array([0.0, 0.15, 0.5]), (N, 8, T, 1))
    K = np.where(rng.random((N, 8, T, 16)) < share, own, rng.integers(0, W, (N, 8, T, 16)))
    S = rng.integers(0, W, (N, 8, A, 16)); l = rng.choice(np.array([0, 0, 1, 1, 2, 3, 5, 8, 14, 15]), (N, 8, T))
    return X, S, K, z, l
def setup_inputs(rng):
    return pack(*parts(rng))
def setup_inputs_corners(rng):
    X, S, K, z, l = parts(rng)
    X[:, 6, 0] = 0; X[:, 6, W - 1] = 255
    S[:, 1] = (W - 1) * rng.integers(0, 2, (N, A, 16)); S[:, 3] = S[:, 3, :, :1].copy(); S[:, 5] = np.arange(A)[:, None]; S[:, 7] = rng.choice(np.array([0, 1, W - 2, W - 1]), (N, A, 16))
    mode = rng.integers(0, 8, (N, 8, T)); mo = mode[..., None]
    K = np.where((mo == 0) | (mo == 3), K[..., :1], np.where(mo == 1, (W - 1) * rng.integers(0, 2, K.shape), K))
    own = np.take_along_axis(K, rng.integers(0, 16, (N, 8, T, 1)), 3)[..., 0]
    z = np.where((mo == 2) | (mo == 3), X[RI, GI, own], np.where(mo == 7, 255 * rng.integers(0, 2, z.shape), z))
    l = np.where((mode == 4) | (mode == 7), 15, np.where(mode == 5, 14, np.where(mode == 6, 0, l)))
    zc = rng.integers(0, 256, 16); X[:, 2, W - 1] = zc; S[:, 2, 0] = rng.integers(0, W - 1, (N, 16)); S[::2, 2, 0, 15] = W - 1
    for t, n in ((0, 15), (T - 1, 14)):
        z[:, 2, t] = zc; K[:, 2, t] = W - 1; l[:, 2, t] = n
    lane = np.arange(T); bq = (np.arange(N)[:, None] + 1 + lane % M) % N; even = np.arange(N) % 2 == 0
    dl = rng.integers(1, 60, 16); z[:, 0] = rng.integers(64, 192, (N, T, 16)); z[:, 0, :, 0] = 0
    X[:, 0, :T] = z[:, 0] + dl * (2 * rng.integers(0, 2, (N, T, 16)) - 1); X[:, 0, :T, 0] = rng.permutation(T); K[:, 0] = lane[:, None]
    pat = rng.integers(0, 256, (16, 16))
    for m in range(4): X[:, 0, W - 64 + 16 * m:W - 48 + 16 * m] = pat
    S[:, 0] = W - 64 + 16 * (np.arange(N) % 4)[:, None, None] + np.argsort(rng.random((N, A, 16)), axis=-1)
    dl = rng.integers(0, 11, 16); z[:, 4] = np.where(bq % 2 == 0, 120, 135)[:, :, None] + rng.integers(-3, 4, (N, T, 16)); z[:, 4, :, 0] = 0
    X[:, 4] = np.where(even, 40, 215)[:, None, None] + rng.integers(-3, 4, (N, W, 16)); X[:, 4, :, 0] = 0
    X[:, 4, :T] = z[:, 4] + dl; X[:, 4, :T, 0] = rng.permutation(T); K[:, 4] = lane[:, None]
    S[:, 4] = T + np.argsort(rng.random((N, A, 1)), axis=1)
    lev = np.where(even, 100, 150); X[:, 5, :W - T] = lev[:, None, None] + rng.integers(-3, 4, (N, W - T, 16))
    z[:, 5] = lev[bq][:, :, None] + rng.integers(-3, 4, (N, T, 16)); X[:, 5, W - T:] = z[:, 5] + rng.integers(0, 11, (N, T, 16)); K[:, 5] = W - T + lane[:, None]
    return pack(X, S, K, z, l)
def setup_inputs_crowd(rng):
    X, S, K, z, l = parts(rng); lane = np.arange(T); bq = (np.arange(N)[:, None] + 1 + lane % M) % N
    for g in (0, 4):
        pat = rng.integers(40, 200, (16, 16)); pat[15] = rng.integers(0, 20, 16)
        if (clue(pat[15]) & (A - 1)) == side(clue(pat[15])): pat[15, 0] += 1
        X[:, g] = pat[np.arange(W) & 15]
        S[:, g] = np.argsort(rng.random((N, A, 16)), axis=-1) + 16 * rng.integers(0, W >> 4, (N, A, 16))
        z[:, g] = 0; l[:, g] = 0; K[:, g] = rng.integers(0, W, (N, T, 16)); K[:, g, :, 0] = (K[:, g, :, 0] >> 4) << 4
        if g == 4:
            K[:, g, 5] = 15 + 16 * rng.integers(0, W >> 4, (N, 16)); c = int(side(clue(pat[15])))
            S[:, g, c] = np.where((S[:, g, c] & 15) == 15, S[:, g, c] - 15, S[:, g, c])
    for g in (1, 5):
        dl = rng.integers(1, 60, 16)
        if (clue(dl) & (A - 1)) == 0: dl[0] += 1
        z[:, g] = rng.integers(64, 192, (N, T, 16)); X[:, g, :T] = z[:, g] + dl * (2 * rng.integers(0, 2, (N, T, 16)) - 1); K[:, g] = lane[:, None]
        pat = rng.integers(0, 256, (16, 16))
        for m in range(4): X[:, g, W - 64 + 16 * m:W - 48 + 16 * m] = pat
        S[:, g] = W - 64 + 16 * (np.arange(N) % 4)[:, None, None] + np.argsort(rng.random((N, 1, 16)), axis=-1)
        if g == 5: X[:, g, T] = z[:, g, 7]; K[:, g, 7] = T
    for g in (2, 6):
        X[:, g, W - 1] = np.where(np.arange(N) % 2 == 0, 40, 215)[:, None] + rng.integers(-3, 4, (N, 16)); S[:, g] = W - 1
        z[:, g] = np.where(bq % 2 == 0, 120, 135)[:, :, None] + rng.integers(-3, 4, (N, T, 16))
        X[:, g, :T] = z[:, g] + rng.integers(0, 21, (N, T, 16)); K[:, g] = lane[:, None]
        if g == 6: z[:, g, 9] = X[bq[:, 9], g, W - 1]; X[:, g, 9] = z[:, g, 9]
    for g in (3, 7):
        pat = rng.integers(0, 31, (16, 16)); pat[4] = rng.integers(185, 221, 16); pat[7] = 255; pat[8] = 0
        for q in range(3):
            e = rng.permutation(64); s = clue(pat[q]) + 7 * (e - pat[q, 0])
            pat[q, 0] = e[np.argmax(((s >> 2) & 15) == ((1 - 4 * q) & 15))]
        v = clue(pat[:3]); pat[3] = apart(rng.integers(0, 31, (64, 16)), np.concatenate([v & (A - 1), side(v)]))
        v = clue(pat[:4]); pat[6] = apart(rng.integers(0, 31, (64, 16)), np.concatenate([v & (A - 1), side(v)]))
        v3, v6 = int(clue(pat[3])), int(clue(pat[6])); a = ((RO - 1) * (T - (1 if g == 7 else 0))) & 31
        if g == 3: dl = np.concatenate([np.array([1, 2, 31]), rng.integers(1, 32, N - 3)])
        else: dl = np.concatenate([np.array([a - 1, a, a + 1]), a + rng.integers(-1, 3, N - 3)])
        dl = rng.permutation(dl)
        X[:, g] = pat[np.arange(W) & 15]; X[:, g, 5::16] = pat[4]; X[:, g, 5::16, 15] += dl[:, None]
        S[:, g] = 4 + 16 * rng.integers(0, W >> 4, (N, A, 16))
        S[:, g, side(v3)] += 1; S[:, g, v6 & (A - 1)] += 4; S[:, g, side(v6)] += 3
        z[:, g] = 0; K[:, g] = 4 - RO + 16 * rng.integers(0, W >> 4, (N, T, 16))
        if g == 7: K[:, g, T - 1] = 6 + 16 * rng.integers(0, W >> 4, (N, 16))
    return pack(X, S, K, z, l)
def setup_inputs_ends(rng):
    X = 255 * rng.integers(0, 2, (N, 8, W, 16)); pal = 255 * rng.integers(0, 2, (8, 8, 16)); pal[:, 0] = 0; pal[:, 1] = 255
    X = np.where(rng.random((N, 8, W, 1)) < 0.5, pal[GI, rng.integers(0, 8, (N, 8, W))], X)
    z = np.where(rng.random((N, 8, T, 1)) < 0.6, pal[GI, rng.integers(0, 8, (N, 8, T))], 255 * rng.integers(0, 2, (N, 8, T, 16)))
    S = np.where((np.arange(A) % 4 == 3)[:, None], rng.integers(0, W, (N, 8, A, 16)), (W - 1) * rng.integers(0, 2, (N, 8, A, 16)))
    K = np.where((np.arange(T) % 4 == 3)[:, None], rng.integers(0, W, (N, 8, T, 16)), (W - 1) * rng.integers(0, 2, (N, 8, T, 16)))
    l = 15 * rng.integers(0, 2, (N, 8, T)); top = int(clue(np.full(16, 255))); c1, c2 = top & (A - 1), int(side(top))
    for g in (0, 7):
        X[:, g, 0] = 0; X[:, g, W - 1] = 255
        for t in (0, T - 1): z[:, g, t] = 0; l[:, g, t] = 0; K[:, g, t] = 0; K[:, g, t, 1] = W - 1; K[:, g, t, 15] = W - 1
        for t in (1, T - 2): z[:, g, t] = 0; l[:, g, t] = 15; K[:, g, t] = 0; K[:, g, t, ::2] = W - 1
        for t in (2, T - 3): z[:, g, t] = 255; l[:, g, t] = 15; K[:, g, t] = 0
        for q in range(N):
            S[q, g, c1] = 0; S[q, g, c2] = 0; S[q, g, 0] = W - 1
            if q % 2 == 1: S[q, g, c1, 1] = W - 1; S[q, g, c1, 15] = W - 1
            if q % 3 == 1: S[q, g, c2, 2] = W - 1; S[q, g, c2, 15] = W - 1
            if q % 2 == 0: S[q, g, 0, 3] = 0; S[q, g, 0, 14] = 0
    return pack(X, S, K, z, l)
def setup_inputs_spread(rng):
    X = (np.exp2(8 * rng.random((N, 8, W, 1))) * rng.random((N, 8, W, 16))).astype(np.int64) * (rng.random((N, 8, W, 1)) > 0.0625)
    z = (np.exp2(8 * rng.random((N, 8, T, 1))) * rng.random((N, 8, T, 16))).astype(np.int64)
    X = np.where(rng.random((N, 8, W, 1)) < 0.3, 255 - X, X); z = np.where(rng.random((N, 8, T, 1)) < 0.5, 255 - z, z)
    S = (W * rng.random((N, 8, A, 16)) ** 3).astype(np.int64); K = (W * rng.random((N, 8, T, 16)) ** 4).astype(np.int64); l = (16 * rng.random((N, 8, T)) ** 3).astype(np.int64)
    return pack(X, S, K, z, l)
def setup_inputs_ties(rng):
    X, S, K, z, l = parts(rng); few = np.array([0, EPS, EPS + 1, 2 * EPS, 255])
    for g in (0, 2, 4, 6):
        s = few[:3] if g < 4 else few
        X[:, g] = rng.choice(s, (N, W, 16)); z[:, g] = rng.choice(s, (N, T, 16))
    for g, e in ((1, 1), (3, 31), (7, 32)):
        y = np.full((N, 16), 100); y[1::2, 15] += e; X[:, g, W - 1] = y; S[:, g] = W - 1
        dev = np.full((N, T, 16), TH >> 4); dev[..., 0] += rng.integers(-2, 3, (N, T))
        z[:, g] = 100 + (2 * rng.integers(0, 2, (N, T, 1)) - 1) * dev; X[:, g, :T] = z[:, g]; K[:, g] = np.arange(T)[:, None]
    lane = np.arange(T); bq = (np.arange(N)[:, None] + 1 + lane % M) % N; cq = (bq[:, 0] + 1) % N
    own = rng.integers(0, 251, (N, 16)); own[:, 0] = 30 * np.arange(N)
    order = rng.permutation(N); dl = rng.integers(1, 5, N); dl[order[:4]] = np.array([1, 2, 3, 1])
    near = np.roll(own, 1, axis=0); near[:, 15] += dl
    X[:, 5, W - 1] = own; X[:, 5, W - 2] = near
    S[:, 5, 0] = W - 1 - (np.argsort(rng.random((N, 16)), axis=-1) & 1)
    z[:, 5] = own[bq]; z[:, 5, 0] = np.where((cq != order[3])[:, None], near[cq], own[bq[:, 0]])
    X[:, 5, :T] = z[:, 5]; K[:, 5] = lane[:, None]
    return pack(X, S, K, z, l)
def check_inputs(d):
    bad = []
    for k, lo, hi in (("x0", 0, 255), ("asc", 0, W - 1), ("kw", 0, W - 1), ("z0", 0, 255), ("l0", 0, 15)):
        v = np.asarray(d[k]).astype(np.float64)
        if not (np.min(v) >= lo and np.max(v) <= hi): bad.append("range of " + k)
        elif np.any(v != np.floor(v)): bad.append("whole numbers of " + k)
    return bad
def reference(x0, asc, kw, z0, l0):
    def turn(a):
        return np.ascontiguousarray(np.swapaxes(a.astype(np.float32).astype(np.int32).reshape(N, 8, 16, -1), 2, 3))
    X, S, K, z, l = turn(x0), turn(asc), turn(kw), turn(z0), l0.astype(np.int32)
    ri, gi = np.arange(N)[:, None, None], np.arange(8)[None, :, None]; i16 = np.arange(16); wt = (15 * np.arange(16) + 7).astype(np.int32)
    b = (np.arange(N)[:, None] + 1 + np.arange(T)[None, :] % M) % N; c = (b + 1) % N
    al = np.zeros((N, 8), np.int32)
    def look(q, col, aim, dl):
        p = S[q[:, None, :], gi, col]; y = X[q[:, None, :, None], gi[..., None], p]
        e = np.add.reduce(np.abs(np.abs(y - aim[:, :, :, None]) - dl[:, :, :, None]), axis=-1); j = np.argmin(e, axis=-1)
        return p, j, np.take_along_axis(e, j[..., None], 3)[..., 0], np.take_along_axis(y, j[..., None, None], 3)[:, :, :, 0]
    for rnd in range(RO):
        x = X[ri[..., None], gi[..., None], K]; dx = np.abs(x - z[:, :, :, None])
        fit = ~np.any((dx > EPS) & (i16 < l[..., None])[:, :, :, None], axis=-1)
        may = fit | ~np.any(fit, axis=-1, keepdims=True)
        k = np.argmax(np.where(may, np.add.reduce(dx, axis=-1), -1), axis=-1)[..., None, None]
        de = np.take_along_axis(dx, k, 3)[:, :, :, 0]; xs = np.take_along_axis(x, k, 3)[:, :, :, 0]
        v = np.add.reduce(de * wt, axis=-1); cb = v & (A - 1); cc = (5 * v + (v >> 2)) & (A - 1)
        p, j, eb, y = look(b, cb, z, de); pg, g, ec, yg = look(c, cc, z, de)
        hit = ec <= eb + (al[c[:, None, :], gi] & 31); con = ~hit & (eb < TH); nei = ~hit & ~con
        zn = np.where(con[..., None], y, np.where(nei[..., None], (z + xs) >> 1, z)); ln = np.where(con, (l + 1) & 15, l)
        off = np.any((np.abs(x - zn[:, :, :, None]) > EPS) & (i16 < ln[..., None])[:, :, :, None], axis=-1)
        K = np.where(hit[..., None], (5 * K + (v >> 2)[..., None]) & (W - 1), np.where(con[..., None] & off, p, K))
        word = np.take_along_axis(p, j[..., None], 3)[..., 0]; new = (y + de) >> 1
        column = np.where(i16 == j[..., None], np.take_along_axis(pg, g[..., None], 3), p)
        for t in range(T):
            r, h = np.nonzero(nei[:, :, t]); X[b[r, t], h, word[r, h, t]] = new[r, h, t]
            r, h = np.nonzero(hit[:, :, t]); S[b[r, t], h, cb[r, h, t]] = column[r, h, t]
            al[c[:, t]] += hit[:, :, t]
        z, l = zn, ln
    def back(a):
        return np.ascontiguousarray(np.swapaxes(a, 2, 3)).reshape(N, 128, -1).astype(np.float32)
    return {"yx": back(X).astype(BF), "ya": back(S), "yk": back(K), "yz": back(z).astype(BF), "yl": l.astype(np.float32)}

@@ -1,0 +1,794 @@
+from concourse.bass import DstId, RemoteDMATransfer
+from concourse.mybir import AluOpType as OP, AxisListType, ActivationFunctionType as AF
+
+N, W, A, LN, RO = 8, 4096, 1024, 192, 4
+NH = 2
+LW = LN // NH
+NB = LW // 16
+BIG = 16 * LW
+KG = 4
+XCH = 2
+SOFF = 256
+HK0 = W + 256
+NKEY = HK0 + A
+MAGIC = 1.5 * 2.0 ** 30
+ROUND = 1.5 * 2.0 ** 23
+CS = 1.578125
+H16 = "float16"
+HO = [1, 0]
+ORDER = "H1 H0 B1 P1 C1 D1 B0 P0 C0 O1 D0 O0"
+OFFMODE = "ssss"
+GENG = ["xx", "xx", "xx"]
+FUSE = ""
+ZENG = "x"
+JOIN = True
+LV2 = False
+CY, PCY, FIX, HOP, GCY, TT2 = 1.0, 0.48, 60.0, 120.0, 1.35, 2.0
+VB, LAM, NOISE, SEED = 1.0, 600.0, 800.0, 1
+
+
+def _sb(n, d):
+    return ("sbuf", [128, n], d)
+
+
+SCRATCH = {"UZ": _sb(400, "bfloat16"), "CK": _sb(LW, H16), "CKs": _sb(LW, H16), "I12": _sb(128, H16),
+           "X": _sb(W + LN, "bfloat16"), "S": _sb(SOFF + A, "float32"), "Si": _sb(A, "int32"),
+           "XN": _sb(W + LN, "bfloat16"), "SN": _sb(SOFF + A, "float32"), "MW": _sb(408, "float32"), "MO": _sb(408, "float32"),
+           "KC": _sb(3 * LN, "int32"), "ZC": _sb(3 * LN, "bfloat16"), "TW": _sb(3 * LN, "float32"), "PGu": _sb(2 * LN, "uint16"),
+           "zs": _sb(2 * LN, "bfloat16"), "Ds": _sb(2 * LN, "bfloat16"), "Ku": _sb(LN, "uint16"), "dd": _sb(12 * LN, "float32"),
+           "sf": _sb(16 * 40, "float32"), "si": _sb(16 * 12, "int32"), "su": _sb(16 * 12, "uint16"), "sh": _sb(16 * 4, "bfloat16"),
+           "cI": _sb(16, "int32"), "col": _sb(32, "float32"), "coli": _sb(16, "int32"), "PERM": _sb(5 * 128, "bfloat16"),
+           "OH": _sb(BIG, "bfloat16"), "IO": _sb(NKEY, "float32"), "C2k": _sb(LW, H16), "TFh": _sb(12, H16),
+           "ZIh": _sb(256, H16), "ZWh": _sb(256, H16), "NIh": _sb(128, H16), "BOh": _sb(128, H16)}
+for _names, _n, _d in (("xg dx gt yB aB mB yC aC mC ab2" + "".join(" zr" + _s for _s in FUSE), 16 * LN, "bfloat16"),
+                       ("Zn us D thrR ohj ohm yj nw dl Lb Lr", LN, "bfloat16"), ("Kp vi Li", LN, "int32"), ("Ph Gh ohP ohG", LN, H16),
+                       ("K20 fit key thrK To Pf GB rr dPK kr2 Kf tR", LN, "float32"), ("cJ c1 c2", 256, "float32"),
+                       ("ZI ZW1 ZWd ZWp ZWw ZW2 ZWm Z8", 256, "bfloat16"), ("NI CI NCI HI BO BOw", 128, "bfloat16"),
+                       ("CQ", LW, "bfloat16"), ("TBL TB2 TBN", 32, "float32")):
+    for _x in _names.split():
+        SCRATCH[_x] = _sb(_n, _d)
+for _x, _n, _d in [("I", 24, "int32"), ("Z", 24, "bfloat16"), ("A", 128, "int32"), ("N", 512, "bfloat16"), ("S", 128, "float32"), ("W", 51, "float32"),
+                   ("K", 24, "float32"), ("L", 48, "bfloat16")] + [("X%d" % _c, 512 // XCH, "bfloat16") for _c in range(XCH)]:
+    SCRATCH["st" + _x] = ("dram", [N, 128, _n], _d)
+    SCRATCH["ld" + _x] = ("dram", [N, 128, _n], _d)
+SCRATCH["stP"] = ("dram", [128, 12], "int32")
+SCRATCH["ldP"] = ("dram", [N, 128, 12], "int32")
+for _b in ("PB0", "PB1", "PB2", "PS0", "PS1", "PD", "PM0", "PM1"):
+    SCRATCH[_b] = ("psum", [128, 512], "float32")
+SEMAPHORES = ["ev", "es", "ep", "eg"] + ["d%d" % _i for _i in range(40)] + ["r%d" % _i for _i in range(12)] + ["l%d" % _i for _i in range(12)]
+ESEM = {"v": "ev", "s": "es", "p": "ep", "g": "eg"}
+REPORT = {}
+
+
+def build(g, core, T, topo):
+    rank = T.rank_of(core)
+    ops, stg = [], [0]
+    Q = {"v": g.vector, "s": g.scalar, "p": g.tensor, "g": g, "y": g.sync}
+
+    def dt(n):
+        return SCRATCH[n][2]
+
+    def a(n, c0=0, c1=None, st=None, p=None):
+        c1 = SCRATCH[n][1][1] if c1 is None else c1
+        ps = slice(None) if p is None else slice(p[0], p[1])
+        cs = slice(c0, c1) if st is None else slice(c0, c1, st)
+        return {"ap": T[n][ps, cs], "reg": [(n, c0, c1)], "n": len(range(c0, c1, st or 1)), "nm": n}
+
+    def ind(w, o):
+        return {"ap": w["ap"].indirect(o["ap"]), "reg": w["reg"], "xr": o["reg"], "n": 16 * o["n"], "nm": w["nm"], "ind": 1}
+
+    def d(ap, n):
+        return {"ap": ap, "reg": [(n, 0, N)] if n else [], "n": 0, "nm": n}
+
+    def val(x):
+        return x["ap"] if isinstance(x, dict) else x
+
+    def add(alts, outs, ins, **k):
+        rd = [r for x in ins if isinstance(x, dict) for r in x["reg"] + x.get("xr", [])] + [r for x in outs for r in x.get("xr", [])]
+        o = {"alts": alts, "w": [r for x in outs for r in x["reg"]], "r": rd, "st": stg[0]}
+        o.update(k)
+        ops.append(o)
+        return len(ops) - 1
+
+    def two(*xs):
+        return all(dt(x["nm"]) in ("bfloat16", "float16", "uint16") for x in xs)
+
+    def vcost(out, in0, per):
+        if "ind" in in0:
+            return 50 + GCY * in0["n"]
+        if "ind" in out:
+            return 50 + 3.2 * out["n"]
+        return max(FIX, per * CY * in0["n"])
+
+    def tt(out, i0, i1, op):
+        ps = SCRATCH[i0["nm"]][0] == "psum" or SCRATCH[i1["nm"]][0] == "psum"
+        add({"v": (vcost(out, i0, 1 if ps else TT2), lambda: g.vector.tensor_tensor(out["ap"], i0["ap"], i1["ap"], op))}, [out], [i0, i1])
+
+    def ts(out, i0, s1, op0, s2=None, op1=None):
+        if s2 is None:
+            f = lambda: g.vector.tensor_scalar(out["ap"], i0["ap"], val(s1), None, op0)
+        else:
+            f = lambda: g.vector.tensor_scalar(out["ap"], i0["ap"], val(s1), val(s2), op0, op1)
+        add({"v": (vcost(out, i0, 0.5 if two(out, i0) else 1), f)}, [out], [i0, s1, s2])
+
+    def cp(out, i0, eng="v"):
+        alts = {}
+        if "v" in eng:
+            alts["v"] = (vcost(out, i0, 0.5 if two(out, i0) else 1), lambda: g.vector.tensor_copy(out["ap"], i0["ap"]))
+        if "s" in eng:
+            alts["s"] = (vcost(out, i0, 1) + 15, lambda: g.scalar.activation(out["ap"], i0["ap"], AF.Copy))
+        add(alts, [out], [i0])
+
+    def act(out, i0, fn, bias=None):
+        if bias is None:
+            f = lambda: g.scalar.activation(out["ap"], i0["ap"], fn)
+        else:
+            f = lambda: g.scalar.activation(out["ap"], i0["ap"], fn, bias=bias["ap"])
+        add({"s": (vcost(out, i0, 1), f)}, [out], [i0, bias])
+
+    def lin(out, i0, sc, bi):
+        add({"v": (vcost(out, i0, 1), lambda: g.vector.tensor_scalar(out["ap"], i0["ap"], sc, bi, OP.mult, OP.add)),
+             "s": (vcost(out, i0, 1) + 15, lambda: g.scalar.activation(out["ap"], i0["ap"], AF.Identity, bias=bi, scale=sc))}, [out], [i0])
+
+    def red(out, i0, op):
+        add({"v": (vcost(out, i0, 1), lambda: g.vector.tensor_reduce(out["ap"], i0["ap"], AxisListType.X, op))}, [out], [i0])
+
+    def mset(out, v):
+        add({"v": (FIX, lambda: g.vector.memset(out["ap"], v))}, [out], [])
+
+    def mm(out, l, r, st=True, sp=True):
+        add({"p": (max(64, r["n"]) * PCY, lambda: g.tensor.matmul(out["ap"], l["ap"], r["ap"], st, sp))}, [out], [l, r])
+
+    def iota(out, pat, base, cm, **k):
+        if dt(out["nm"]) == "int32":
+            f = lambda: g.iota(out["ap"], pat, base, cm)
+        else:
+            f = lambda: g.iota(out["ap"], pat, base, cm, allow_small_or_imprecise_dtypes=True)
+        add({"g": (130 + 2 * out["n"], f)}, [out], [], **k)
+
+    nd = [0]
+
+    def dma(q, pairs, nbytes, behind=None):
+        sem = "d%d" % nd[0]
+        nd[0] += 1
+
+        def f():
+            for o, i in pairs:
+                Q[q].dma_start(o["ap"], i["ap"]).then_inc(T.sem[sem], 16)
+        add({q: ((600 if q == "g" else 80) * len(pairs), f)}, [o for o, i in pairs] + ([d(None, behind)] if behind else []), [i for o, i in pairs],
+            sem=(sem, 16 * len(pairs)), lat=1800 + nbytes / 250.0)
+
+    peers = [r for r in range(N) if r != rank]
+    far = [r for r in peers if topo.die(T.cores[r]) != topo.die(core)]
+    near = [r for r in peers if r not in far]
+    nr = [0]
+
+    def exchange(names, nbytes):
+        k = nr[0]
+        nr[0] += 1
+        per = 2 // len(names)
+        trs = []
+        for j, x in enumerate(names):
+            st, ld = "st" + x, "ld" + x
+            for cls, lst in ((0, far), (1, near)):
+                for i, r in enumerate(lst):
+                    en = topo.engines(core, T.cores[r])[cls::2]
+                    m = 0
+                    for e in en[2 * i + j * per:2 * i + (j + 1) * per]:
+                        m |= 1 << e
+                    rid, pid, _ = topo.addr(T.cores[r])
+                    trs.append(RemoteDMATransfer(dst_ids=[DstId(rid=rid, pnc=pid)], dma_engine_mask=m, remote_sem=T.sem["r%d" % k],
+                                                 src=T[st][r] if len(SCRATCH[st][1]) == 3 else T[st][:], dst=T[ld][rank]))
+        tot = per * len(trs)
+        s = add({"g": (1000, lambda: g.remote_dma_fused(trs, local_sem=T.sem["l%d" % k]))}, [], [d(None, "st" + x) for x in names],
+                sem=("l%d" % k, tot), lat=2200 + nbytes / 200.0)
+        add({}, [d(None, "ld" + x + "R") for x in names], [], sem=("r%d" % k, tot), lat=2500 + nbytes / 200.0, after=s)
+        return s
+
+    def land(x, r0=0, r1=128):
+        y = d(T["ld" + x][:, r0:r1, :], "ld" + x)
+        y["reg"] = y["reg"] + [("ld" + x + "R", 0, N)]
+        return y
+
+    def stage(x, src, r0=0, r1=128):
+        st, ld, pr = "st" + x, "ld" + x, []
+        if rank > 0:
+            pr.append((d(T[st][0:rank, r0:r1, :], st), src(0, 16 * rank)))
+        if rank < N - 1:
+            pr.append((d(T[st][rank + 1:N, r0:r1, :], st), src(16 * (rank + 1), 16 * N)))
+        return pr, [(d(T[ld][rank, r0:r1, :], ld), src(16 * rank, 16 * (rank + 1)))]
+
+    def inp(t, c0, c1):
+        return lambda r0, r1: d(t[r0:r1, c0:c1], None)
+
+    def sbs(n, c0, c1):
+        return lambda r0, r1: a(n, c0, c1, p=(r0, r1))
+
+    k1, k2 = stage("I", inp(T.kw, 0, LN))
+    l1, l2 = [(d(T.stP[:], "stP"), d(T.l0[:], None))], [(d(T.ldP[rank], "ldP"), d(T.l0[:], None))]
+    z1, z2 = stage("Z", inp(T.z0, 0, LN))
+    xw = W // XCH
+    xs = [stage("X%d" % c, inp(T.x0, c * xw, (c + 1) * xw)) for c in range(XCH)]
+    dma("s", k1, 1e5)
+    dma("y", xs[0][0], 2 ** 20 / XCH)
+    dma("s", l1 + z1, 1e5)
+    for c in range(1, XCH):
+        dma("y", xs[c][0], 2 ** 20 / XCH * (c + 1))
+    dma("s", k2 + l2 + z2, 1e5)
+    for c in range(XCH):
+        dma("s", xs[c][1], 2 ** 20)
+    exchange(["I"], 1e5)
+    exchange(["Z", "P"], 1e5)
+    for c in range(XCH):
+        exchange(["X%d" % c], 2 ** 20 / XCH)
+    dma("y", [(a("KC", LN, 2 * LN), land("I"))], 1e5)
+    dma("y", [(a("Zn"), land("Z"))], 1e5)
+    dma("y", [(a("Li", p=(0, N)), land("P", 16 * rank, 16 * rank + 16))], 1e5)
+    for c in range(XCH):
+        dma("y", [(a("X", c * xw, (c + 1) * xw), land("X%d" % c))], 2 ** 20 / XCH)
+    a1, a2 = stage("A", inp(T.asc, 0, A))
+    dma("s", a1, 2 ** 19, "stX0")
+    dma("s", a2, 2 ** 19)
+    sent = exchange(["A"], 2 ** 19)
+    dma("y", [(a("Si"), land("A"))], 2 ** 19)
+
+    def col(i):
+        return a("col", i, i + 1)
+
+    def small(buf):
+        return lambda i, h=None: a(buf, 16 * i, 16 * i + 12) if h is None else a(buf, 16 * i + NB * h, 16 * i + NB * (h + 1))
+    sf, si, su, sh = small("sf"), small("si"), small("su"), small("sh")
+    PID, CI_, CQ16, CW, CPW, CQ128, CI16, AM, CP128, CZ8, PC = 0, 1, 2, 3, 4, 5, 6, 7, 8, 9, 16
+    iota(a("coli", 0, 1), [[0, 1]], 0, 1)
+    iota(a("cJ"), [[1, 256]], 0, 0)
+    cp(col(PID), a("coli", 0, 1))
+    ts(a("coli", 1, 2), a("coli", 0, 1), 15, OP.bitwise_and)
+    cp(col(CI_), a("coli", 1, 2))
+    tt(col(CQ16), col(PID), col(CI_), OP.subtract)
+    ts(col(CQ128), col(CQ16), 128.0, OP.add)
+    ts(col(CP128), col(PID), 128.0, OP.add)
+    ts(col(CW), col(CI_), 15.0, OP.mult, 7.0, OP.add)
+    ts(col(CI16), col(CI_), 16.0, OP.mult)
+    ts(col(CZ8), col(PID), 16.0, OP.mult, 128.0, OP.add)
+    mset(col(AM), 2048.0)
+    ts(a("c1"), a("cJ"), col(PID), OP.is_equal)
+    ts(a("c2"), a("cJ"), col(CP128), OP.is_equal)
+    tt(a("ZI"), a("c1"), a("c2"), OP.add)
+    cp(a("ZIh"), a("ZI"))
+    I = a("ZI", 0, 128)
+    for n, v in (("NI", -1.0), ("NIh", -1.0), ("HI", 0.5), ("CI", CS), ("NCI", -CS), ("I12", 2.0 ** -12)):
+        ts(a(n), I, v, OP.mult)
+    mset(a("CQ"), -0.25)
+    ts(a("C2k"), a("CQ"), 0.0, OP.mult, 2048.0, OP.add)
+    mset(a("c1", 0, 16), 0.5)
+    mset(a("c2", 0, 16), 0.0)
+    add({"v": (FIX, lambda: g.vector.tensor_tensor_scan(T.TBL[:, 0:16], T.c1[:, 0:16], T.c2[:, 0:16], 131072.0, OP.mult, OP.add))},
+        [a("TBL", 0, 16)], [a("c1", 0, 16), a("c2", 0, 16)])
+    cp(a("TBL", 16, 32), a("TBL", 0, 16))
+    cp(a("TBN", 0, 31), a("TBL", 1, 32))
+    mset(a("TBN", 31, 32), 1.0)
+    mset(a("TW", 0, 2 * LN), 2.0 ** 20)
+    cp(a("TB2", 0, 16), a("cJ", 0, 16))
+    cp(a("TB2", 16, 32), a("cJ", 0, 16))
+    ts(a("c1", 0, 16), a("cJ", 0, 16), col(CI_), OP.is_equal, 0.5, OP.mult)
+    tt(a("c2", 0, 16), a("c1", 0, 16), a("TBL", 0, 16), OP.mult)
+    red(col(CPW), a("c2", 0, 16), OP.add)
+    ts(a("c1"), a("cJ"), col(CQ16), OP.is_equal)
+    ts(a("c2"), a("cJ"), col(CQ128), OP.is_equal)
+    tt(a("ZW1"), a("c1"), a("c2"), OP.add)
+    for n, v in (("ZWd", -2.0 ** -12), ("ZWp", col(CPW)), ("ZWw", col(CW)), ("ZW2", 4096.0), ("ZWm", 2048.0 if LV2 else -2048.0), ("ZWh", 1.0)):
+        ts(a(n), a("ZW1"), v, OP.mult)
+    ts(a("Z8"), a("cJ"), col(CZ8), OP.is_equal)
+    ts(a("c1", 0, 128), a("cJ", 0, 128), col(CQ16), OP.subtract, 0.0, OP.is_ge)
+    ts(a("c2", 0, 128), a("cJ", 0, 128), col(CQ16), OP.subtract, 16.0, OP.is_lt)
+    tt(a("BO"), a("c1", 0, 128), a("c2", 0, 128), OP.mult)
+    cp(a("BOh"), a("BO"))
+    ts(a("BOw"), a("BO"), col(CW), OP.mult)
+    ts(a("c1", 0, 5), a("cJ", 0, 5), col(CI_), OP.add)
+    ts(a("cI", 0, 5), a("c1", 0, 5), -2.0, OP.add, 0.2, OP.mult)
+    ts(a("c2", 0, 5), a("cI", 0, 5), -5.0, OP.mult)
+    tt(a("c1", 0, 5), a("c1", 0, 5), a("c2", 0, 5), OP.add)
+    ts(a("c1", 0, 5), a("c1", 0, 5), -16.0, OP.mult, col(CP128), OP.add)
+    ts(a("cI", 0, 5), a("c1", 0, 5), -16.0, OP.add)
+    ts(a("cI", 0, 5), a("cI", 0, 5), 127, OP.bitwise_and)
+    cp(a("col", PC, PC + 5), a("cI", 0, 5))
+    for c in range(5):
+        ts(a("PERM", 128 * c, 128 * c + 128), a("cJ", 0, 128), col(PC + c), OP.is_equal)
+    iota(a("c1", 0, LW), [[1, 16], [256, NB]], 0, 0)
+    ts(a("CK"), a("c1", 0, LW), col(CI16), OP.add)
+    ts(a("CKs"), a("CK"), 2.0 ** -11, OP.mult)
+    TOF, DUM, HKT, BB, LO, THO, TMP, DUF, MUL = 0, 1, 2, 3, 5, 6, 7, 9, 36
+    ts(sf(TOF), a("cJ", 0, 12), 16.0, OP.mult, col(CI_), OP.add)
+    cp(sh(0), sf(TOF))
+    ts(a("sf", 16 * BB, 16 * BB + 12), sf(TOF), float(W), OP.add)
+    ts(a("sf", 16 * BB + 12, 16 * BB + 24), sf(TOF), -1.0, OP.mult)
+    ts(sf(HKT), sf(TOF), 1.0 / 256, OP.mult, float(HK0), OP.add)
+    ts(a("TFh"), sf(TOF), 1.0 / 256, OP.mult)
+    ts(sf(DUF), sf(TOF), 1.0 + 1.0 / 256, OP.mult, float(W), OP.add)
+    mset(a("sf", 16 * MUL, 16 * MUL + NB), 4.0)
+    mset(a("sf", 16 * MUL + NB, 16 * MUL + 2 * NB), 21.0)
+    ts(si(0, 0), sf(TOF, 0), -(NB - 1) / 2.0, OP.add, 1.0 / NB, OP.mult)
+    ts(sf(TMP, 0), si(0, 0), -float(NB), OP.mult)
+    tt(sf(TMP, 0), sf(TMP, 0), sf(TOF, 0), OP.add)
+    for h in range(NH):
+        ts(su(0, h), sf(TMP, 0), float(NB * h), OP.add)
+    ts(a("tR"), a("cJ", 0, LN), 1.0 / 256, OP.mult)
+    mset(si(11), 0)
+    mset(a("sf", 16 * THO, 16 * THO + 16), 0.0)
+    for n in ("X", "XN"):
+        mset(a(n, W, W + LN), 0.0)
+    for n in ("S", "SN"):
+        mset(a(n, 0, SOFF), 0.0)
+    ts(a("OH", 0, 16), a("cJ", 0, 16), col(CI_), OP.is_equal)
+    c = 16
+    while c < BIG:
+        cp(a("OH", c, min(2 * c, BIG)), a("OH", 0, min(c, BIG - c)))
+        c *= 2
+    for c in range(0, NKEY, 896):
+        iota(a("IO", c, c + 896), [[1, 896]], c, 0, after=sent)
+
+    def SH(n, s):
+        return a(n, 128 - 16 * (s % N), 256 - 16 * (s % N))
+
+    def WW(n, s, i):
+        return a(n, 128 - 16 * (s % N) - i, 256 - 16 * (s % N) - i)
+
+    mset(a("UZ"), 0.0)
+
+    def hs(n, h, base=0):
+        if n == "us" and JOIN:
+            return a("UZ", 200 * h, 200 * h + LW)
+        return a(n, base + LW * h, base + LW * (h + 1))
+
+    def shift(ps, pc, mat, sign, extra, src, h, acc=False):
+        t0 = LW * h
+        for m in range(5):
+            f = (m - t0) % 5
+            mm(a(ps, pc + f, pc + LW, 5), SH(mat, sign * (1 + m + extra)), a(src, t0 + f, t0 + LW, 5), not acc, not acc or m == 4)
+
+    def osum(out, mat, s, src, c0, c1, first=True, last=True):
+        for i in range(16):
+            mm(out, WW(mat, s, i), a(src, c0 + i, c1, 16), first and i == 0, last and i == 15)
+
+    nb = [0]
+
+    def sub(src, h, kg, zz, pos, neg, keep=False):
+        nb[0] += 1
+        b = ("PB0", "PB1", "PB2", "PD")[nb[0] % (4 if LV2 else 3)]
+        for kk in range(KG):
+            o = a(b, kk * LW, (kk + 1) * LW)
+            mm(o, pos, a(src, BIG * h + kg * KG + kk, BIG * (h + 1), 16), kk == 0 or not keep, False)
+            mm(o, neg, zz, False, not keep or kk == KG - 1)
+        return a(b, 0, KG * LW)
+
+    def big(n, h, kg):
+        return a(n, BIG * h + kg * KG * LW, BIG * h + (kg + 1) * KG * LW)
+
+    def words(dst, h, lst, base, j):
+        eng, s = GENG[j], "HBC"[j]
+        w = LW // len(eng)
+        for c, e in enumerate(eng):
+            c0 = LW * h + c * w
+            o, i = a(dst, 16 * c0, 16 * (c0 + w)), ind(a("X", 0, W), a(lst, base + c0, base + c0 + w))
+            if s in FUSE:
+                tt(o, i, a("zr" + s, 16 * c0, 16 * (c0 + w)), OP.subtract)
+            else:
+                cp(o, i, e.replace("x", "vs"))
+
+    def absolute(dst, src, h, kg):
+        for k in range(kg * KG, (kg + 1) * KG):
+            act(a(dst, BIG * h + k * LW, BIG * h + (k + 1) * LW), a(src, BIG * h + k, BIG * (h + 1), 16), AF.Abs)
+
+    def halve(out, pm, c, x, y, wy):
+        o = a(pm, c, c + LW)
+        mm(o, a("HI"), x, True, False)
+        mm(o, wy, y, False, False)
+        mm(o, I, a("CQ"), False, True)
+        ts(out, o, ROUND, OP.add, ROUND, OP.subtract)
+
+    def thresholds(step, last):
+        if step:
+            ts(sf(TMP), su(3), float(2 * LN), OP.is_ge)
+            tt(sf(LO), sf(LO), sf(TMP), OP.add)
+        cp(su(1), sf(LO))
+        if last:
+            cp(a("Lr"), ind(a("TB2"), su(1)), "vs")
+            return
+        cp(a("TW", 2 * LN, 3 * LN), ind(a("TBN"), su(1)), "vs")
+        cp(a("thrR"), ind(a("TBL"), su(1)), "vs")
+        osum(a("PM0", 0, 12), "ZW1", 0, "thrR", 0, LN)
+        lin(sf(THO), a("PM0", 0, 12), 1.0 / 16, 0.0)
+        for h in HO:
+            cp(hs("thrK", h), ind(a("sf", 16 * THO, 16 * THO + 16), su(0, h)), "vs")
+
+    def zshift(h):
+        pm, c = "PM%d" % h, 2 * LW * h
+        if JOIN:
+            cp(a("UZ", 200 * h + 100, 200 * h + 100 + LW), hs("Zn", h), "vs")
+        else:
+            shift(pm, 0, "ZI", 1, 0, "Zn", h)
+            shift(pm, LW, "ZI", 1, 1, "Zn", h)
+            cp(a("zs", c, c + 2 * LW), a(pm, 0, 2 * LW), "s")
+        cp(hs("ZC", h), hs("Zn", h), "vs")
+        for s in FUSE:
+            z = {"H": hs("Zn", h), "B": a("zs", c, c + LW), "C": a("zs", c + LW, c + 2 * LW)}[s]
+            for k in range(16):
+                cp(a("zr" + s, BIG * h + k, BIG * (h + 1), 16), z, ZENG[k % len(ZENG)].replace("x", "vs"))
+
+    cp(a("Lb", p=(0, N)), a("Li", p=(0, N)))
+    for i in range(16):
+        mm(a("PM0", 0, 12), a("Z8", 128 - i, 256 - i, p=(0, N)), a("Lb", i, LN, 16, p=(0, N)), i == 0, i == 15)
+    cp(sf(LO), a("PM0", 0, 12))
+    cp(a("Ku"), a("KC", LN, 2 * LN))
+    thresholds(False, False)
+    for h in HO:
+        zshift(h)
+    cp(a("S", SOFF, SOFF + A), a("Si"))
+
+    MH, T8, HK, ME, MF, THE, LT, CC, U1, U2, KD, NB2, AA, MN, PEN, RR, CNT = 10, 11, 12, 15, 16, 17, 18, 19, 20, 21, 22, 23, 24, 26, 27, 29, 34
+
+    def pair(buf, i, h):
+        return a(buf, 16 * i + 2 * NB * h, 16 * i + 2 * NB * (h + 1))
+
+    def half(buf, i, h, j):
+        return a(buf, 16 * i + 2 * NB * h + NB * j, 16 * i + 2 * NB * h + NB * (j + 1))
+
+    def least(slot, h, src, c):
+        for b in range(NB):
+            red(a("sf", 16 * slot + NB * h + b, 16 * slot + NB * h + b + 1), a(src, c + b, c + LW, NB), OP.min)
+
+    def home(h, last):
+        ps, pm, db = "PS%d" % h, "PM%d" % h, 2 * LW * h
+        words("xg", h, "Ku", 0, 0)
+        for kg in range(16 // KG):
+            if "H" in FUSE:
+                absolute("dx", "xg", h, kg)
+            else:
+                act(big("dx", h, kg), sub("xg", h, kg, hs("Zn", h), I, a("NI")), AF.Abs)
+            ts(big("gt", h, kg), big("dx", h, kg), 40.0, OP.is_gt)
+        cp(hs("KC", h, 2 * LN), hs("KC", h, LN))
+        ts(hs("K20", h), hs("KC", h, LN), 20.0, OP.mult)
+        mm(a(ps, 0, LW), a("I12"), a("CKs"), True, False)
+        osum(a(ps, 0, LW), "ZWd", 0, "dx", BIG * h, BIG * (h + 1), False, True)
+        osum(a(ps, LW, 2 * LW), "ZWp", 0, "gt", BIG * h, BIG * (h + 1))
+        tt(hs("fit", h), a(ps, LW, 2 * LW), hs("thrK", h), OP.is_lt)
+        tt(hs("key", h), a(ps, 0, LW), hs("fit", h), OP.subtract)
+        least(MH, h, "key", LW * h)
+        ts(si(0, h), sf(MH, h), 2.0 ** 23, OP.mult)
+        ts(si(1, h), si(0, h), 2047, OP.bitwise_and)
+        cp(su(2, h), si(1, h))
+        spk = ind(a("xg", BIG * h, BIG * (h + 1)), su(2, h))
+        if "H" in FUSE:
+            cp(hs("us", h), spk, "vs")
+        else:
+            tt(hs("us", h), spk, hs("Zn", h), OP.subtract)
+        if JOIN:
+            for j in range(2):
+                for m in range(5):
+                    f = (m - LW * h) % 5
+                    mm(a(pm, 100 + 200 * j + f, 300 + 200 * j, 5), SH("ZI", 1 + m + j), a("UZ", 200 * h + f, 200 * h + 200, 5))
+            for j in range(2):
+                act(a("Ds", db + LW * j, db + LW * (j + 1)), a(pm, 100 + 200 * j, 100 + 200 * j + LW), AF.Abs)
+            for j in range(2):
+                act(a("PD", db + LW * j, db + LW * (j + 1)), a(pm, 100 + 200 * j, 100 + 200 * j + LW), AF.Abs)
+                cp(a("zs", db + LW * j, db + LW * (j + 1)), a(pm, 200 + 200 * j, 200 + 200 * j + LW), "s")
+        else:
+            shift("PD", db, "ZI", 1, 0, "us", h)
+            shift("PD", db + LW, "ZI", 1, 1, "us", h)
+            pd = a("PD", db, db + 2 * LW)
+            act(a("Ds", db, db + 2 * LW), pd, AF.Abs)
+            act(pd, pd, AF.Abs)
+        osum(a("PS%d" % h, 4 * LW, 4 * LW + 2 * NB) if JOIN else a(pm, 0, 2 * NB), "ZWw", 0, "Ds", db, db + 2 * LW)
+        tt(pair("si", 2, h), a("PS%d" % h, 4 * LW, 4 * LW + 2 * NB) if JOIN else a(pm, 0, 2 * NB), a("sf", 16 * MUL, 16 * MUL + 2 * NB), OP.mult)
+        ts(pair("si", 4, h), pair("si", 2, h), 2, OP.arith_shift_right, A - 1, OP.bitwise_and)
+        cp(pair("su", 4, h), pair("si", 4, h))
+        for j in range(2):
+            cp(hs("PGu", h, LN * j), ind(a("S", SOFF, SOFF + A), half("su", 4, h, j)))
+        act(hs("D", h), hs("us", h), AF.Abs)
+        if not LV2:
+            osum(a(pm, 16, 16 + NB), "ZW1", 0, "Ds", db, db + LW)
+        mm(a(pm, 32, 32 + LW), a("BOw"), hs("D", h))
+        if not LV2:
+            lin(sf(T8, h), a(pm, 16, 16 + NB), 2048.0, 800.0 * 2048)
+        tt(hs("vi", h), a(pm, 32, 32 + LW), hs("K20", h), OP.add)
+        ts(hs("KC", h), hs("vi", h), 2, OP.arith_shift_right, W - 1, OP.bitwise_and)
+        halve(hs("ZC", h, LN), pm, 128, hs("us", h), hs("Zn", h), I)
+        tt(sf(HK, h), half("si", 4, h, 0), sf(HKT, h), OP.add)
+        ts(hs("Ph", h), hs("PGu", h), -2048.0, OP.add)
+        ts(hs("Gh", h), hs("PGu", h, LN), -2048.0, OP.add)
+        cp(hs("Pf", h), hs("PGu", h))
+        mm(a(pm, 256, 256 + LW), SH("ZIh", -1), hs("Gh", h))
+        cp(hs("GB", h), a(pm, 256, 256 + LW), "s")
+
+    def look(h, j):
+        ps = "PS%d" % h
+        y, aa, mx = (("yB", "aB", "mB"), ("yC", "aC", "mC"))[j]
+        words(y, h, "PGu", LN * j, 1 + j)
+        c = 2 * LW * h + LW * j
+        for kg in range(16 // KG):
+            if "BC"[j] in FUSE:
+                absolute(aa, y, h, kg)
+            else:
+                b = sub(y, h, kg, a("zs", c, c + LW), I, a("NI"), LV2)
+                if LV2:
+                    act(b, b, AF.Abs)
+                    for kk in range(KG):
+                        mm(a(b["nm"], kk * LW, (kk + 1) * LW), a("NI"), a("Ds", c, c + LW), False, kk == KG - 1)
+                act(big(aa, h, kg), b, AF.Abs)
+            for kk in range(0 if LV2 else KG):
+                c0 = BIG * h + (kg * KG + kk) * LW
+                tt(a(mx, c0, c0 + LW), a(aa, c0, c0 + LW), a("PD", c, c + LW), OP.max)
+        o = a(ps, (2 + j) * LW, (3 + j) * LW)
+        mm(o, a("ZIh", 0, 128), a("CK"), True, False)
+        osum(o, "ZWm", -j, aa, BIG * h, BIG * (h + 1), False, LV2)
+        if not LV2:
+            osum(o, "ZW2", -j, mx, BIG * h, BIG * (h + 1), False, True)
+        least((ME, MF)[j], h, ps, (2 + j) * LW)
+
+    def partner(h, last):
+        pm = "PM%d" % h
+        cp(si(6, h), sf(ME, h))
+        ts(si(7, h), si(6, h), 2047, OP.bitwise_and)
+        cp(su(6, h), si(7, h))
+        if LV2:
+            ts(sf(LT, h), sf(ME, h), 800.0 * 2048, OP.is_lt)
+        else:
+            tt(sf(LT, h), sf(ME, h), sf(T8, h), OP.is_lt)
+        tt(sf(THE, h), sf(ME, h), si(7, h), OP.subtract)
+        ts(sf(THE, h), sf(THE, h), col(AM), OP.add)
+        lin(sf(CC, h), sf(LT, h), float(LN), float(LN))
+        best = ind(a("yB", BIG * h, BIG * (h + 1)), su(6, h))
+        if "B" in FUSE:
+            tt(hs("yj", h), best, a("zs", 2 * LW * h, 2 * LW * h + LW), OP.add)
+        else:
+            cp(hs("yj", h), best, "vs")
+        cp(hs("ohj", h), ind(a("OH"), su(6, h)), "vs")
+        tt(hs("ohP", h), hs("ohj", h), hs("Ph", h), OP.mult)
+        mm(a(pm, 16, 16 + NB), a("ZIh", 0, 128), a("C2k", 0, NB), True, False)
+        mm(a(pm, 16, 16 + NB), a("ZIh", 0, 128), a("TFh", NB * h, NB * (h + 1)), False, False)
+        osum(a(pm, 16, 16 + NB), "ZWh", 0, "ohP", LW * h, LW * (h + 1), False, True)
+        tt(sf(U2, h), sf(DUF, h), sf(LT, h), OP.mult)
+        shift(pm, 128, "ZI", -1, 0, "yj", h)
+        tt(sf(U1, h), a(pm, 16, 16 + NB), sf(U2, h), OP.max)
+        cp(hs("ZC", h, 2 * LN), a(pm, 128, 128 + LW), "vs")
+        tt(sf(KD, h), sf(U1, h), sf(HK, h), OP.subtract)
+        halve(hs("MW" if last else "nw", h), pm, 256, hs("yj", h), a("Ds", 2 * LW * h, 2 * LW * h + LW), a("HI"))
+
+    def decide(h, last):
+        pm = "PM%d" % h
+        key = a("sf", 16 * AA + NB * h, 16 * AA + NB * (h + 1))
+        tt(sh(1, h), sf(MF, h), sf(THE, h), OP.is_ge)
+        tt(sh(2, h), sf(CC, h), sh(1, h), OP.mult)
+        tt(key, sf(KD, h), sh(1, h), OP.mult)
+        tt(key, key, sf(HK, h), OP.add)
+        ts(su(8, h), key, -0.375, OP.add)
+        tt(hs("kr2", h), ind(a("IO"), su(8, h)), hs("tR", h), OP.add)
+        lin(sf(NB2, h), key, -1.0, -0.375)
+        lin(a("sf", 16 * AA + 12 + NB * h, 16 * AA + 12 + NB * (h + 1)), key, -1.0, float(HK0 - SOFF))
+        mm(a(pm, 0, NB), I, sh(0, h), True, False)
+        for c in range(5):
+            f = (c - NB * h) % 5
+            mm(a(pm, f, NB, 5), a("PERM", 128 * c, 128 * c + 128), a("sh", 32 + NB * h + f, 32 + NB * (h + 1), 5), False, c == 4)
+        cp(su(3, h), a(pm, 0, NB))
+        cp(hs("Zn", h), ind(a("ZC"), su(3, h)), "vs")
+        cp(si(8, h), sf(MF, h))
+        ts(si(9, h), si(8, h), 2047, OP.bitwise_and)
+        cp(su(7, h), si(9, h))
+        cp(hs("ohm", h), ind(a("OH"), su(7, h)), "vs")
+        tt(hs("ohG", h), hs("ohm", h), hs("GB", h), OP.mult)
+        mm(a(pm, 256, 256 + LW), a("BOh"), hs("ohG", h), True, False)
+        mm(a(pm, 256, 256 + LW), a("NIh"), hs("Ph", h), False, True)
+        mm(a(pm, 128, 128 + LW), a("ZIh", 0, 128), a("C2k"), True, False)
+        shift(pm, 128, "ZIh", -1, 0, "Ph", h, True)
+        tt(hs("rr", h), a(pm, 256, 256 + LW), hs("ohj", h), OP.mult)
+        if last:
+            tt(hs("MW", h, LN), hs("rr", h), hs("Pf", h), OP.add)
+        cp(hs("Kp", h), ind(a("KC"), su(3, h)))
+        tt(hs("dPK", h), a(pm, 128, 128 + LW), hs("Kp", h), OP.subtract)
+        cp(hs("To", h), ind(a("TW"), su(3, h)), "vs")
+
+    def off(h, last):
+        o = a("PS%d" % h, 4 * LW, 5 * LW)
+        if "H" in FUSE:
+            tt(hs("dl", h), hs("Zn", h), hs("ZC", h), OP.subtract)
+        for kg in range(16 // KG):
+            b = sub("xg", h, kg, hs("dl" if "H" in FUSE else "Zn", h), a("CI"), a("NCI"))
+            if OFFMODE[kg] == "v":
+                ts(big("gt", h, kg), b, MAGIC, OP.add, MAGIC, OP.not_equal)
+            else:
+                act(big("ab2", h, kg), b, AF.Abs)
+                ts(big("gt", h, kg), big("ab2", h, kg), 64.0, OP.is_gt)
+        for k in range(16):
+            mm(o, WW("ZWp", 0, k), a("gt", BIG * h + k * LW, BIG * h + (k + 1) * LW), k == 0, k == 15)
+        tt(o, o, hs("To", h), OP.is_ge)
+        tt(o, o, hs("dPK", h), OP.mult)
+        if last:
+            tt(hs("Kf", h), o, hs("Kp", h), OP.add)
+        else:
+            tt(hs("KC", h, LN), o, hs("Kp", h), OP.add)
+            cp(hs("Ku", h), hs("KC", h, LN))
+            zshift(h)
+
+    def settle(last):
+        for b in range(11, -1, -1):
+            o = a("dd", LN * b + 16 * b, LN * (b + 1))
+            act(o, a("kr2", 16 * b, LN), AF.Abs, a("sf", 16 * NB2 + b, 16 * NB2 + b + 1))
+            red(a("sf", 16 * MN + b, 16 * MN + b + 1), o, OP.min)
+        for j in range(2):
+            ts(a("sf", 16 * PEN + 12 * j, 16 * PEN + 12 * j + 12), sf(MN), 0.375, OP.is_lt, 8192.0, OP.mult)
+        r24 = a("sf", 16 * RR, 16 * RR + 24)
+        tt(r24, a("sf", 16 * AA, 16 * AA + 24), a("sf", 16 * PEN, 16 * PEN + 24), OP.add)
+        tt(a("MW", 2 * LN, 2 * LN + 24) if last else r24, r24, a("sf", 16 * BB, 16 * BB + 24), OP.min)
+        if last:
+            thresholds(True, True)
+            return
+        ts(su(10), a("sf", 16 * RR, 16 * RR + 12), -0.375, OP.add)
+        ts(su(11), a("sf", 16 * RR + 12, 16 * RR + 24), -1.0, OP.mult, -0.375, OP.add)
+        cp(ind(a("X"), su(10)), a("nw"))
+        tt(ind(a("S"), su(11)), a("rr"), a("Pf"), OP.add)
+        thresholds(True, False)
+        mm(a("PM0", 400, 412), a("BO"), sh(1))
+        red(a("sf", 16 * CNT, 16 * CNT + 1), a("PM0", 400, 412), OP.add)
+        tt(a("si", 16 * 11, 16 * 11 + 1), a("si", 16 * 11, 16 * 11 + 1), a("sf", 16 * CNT, 16 * CNT + 1), OP.subtract)
+        ts(a("si", 16 * 11 + 4, 16 * 11 + 5), a("si", 16 * 11, 16 * 11 + 1), 31, OP.bitwise_and)
+        ts(col(AM), a("si", 16 * 11 + 4, 16 * 11 + 5), 2048.0, OP.mult, 2048.0, OP.add)
+
+    steps = {"H": home, "B": lambda h, last: look(h, 0), "C": lambda h, last: look(h, 1), "P": partner, "D": decide, "O": off}
+    for rnd in range(RO):
+        last = rnd == RO - 1
+        if last:
+            n1, n2 = stage("N", sbs("X", 0, W))
+            s1, s2 = stage("S", sbs("S", SOFF, SOFF + A))
+            dma("y", n1, 2 ** 20)
+            dma("y", s1, 2 ** 20)
+            dma("y", n2 + s2, 2 ** 20)
+            exchange(["N"], 2 ** 20)
+            exchange(["S"], 2 ** 20)
+            dma("y", [(a("XN", 0, W), land("N"))], 2 ** 20)
+            dma("y", [(a("SN", SOFF, SOFF + A), land("S"))], 2 ** 20)
+        for w in ORDER.split():
+            stg[0] += 1
+            steps[w[0]](int(w[1]), last)
+        settle(last)
+
+    w1, w2 = stage("W", sbs("MW", 0, 408))
+    dma("y", w1, 2e5)
+    dma("y", w2, 2e5)
+    exchange(["W"], 2e5)
+    k1, k2 = stage("K", sbs("Kf", 0, LN))
+    z1, z2 = stage("L", sbs("Zn", 0, LN), 0, 64)
+    l1, l2 = stage("L", sbs("Lr", 0, LN), 64, 128)
+    dma("s", k1 + z1 + l1, 2e5)
+    dma("s", k2 + z2 + l2, 2e5)
+    exchange(["K", "L"], 2e5)
+    dma("y", [(a("MO"), land("W"))], 2e5)
+    ts(su(10), a("MO", 2 * LN, 2 * LN + 12), -0.375, OP.add)
+    ts(su(11), a("MO", 2 * LN + 12, 2 * LN + 24), -1.0, OP.mult, -0.375, OP.add)
+    cp(ind(a("XN"), su(10)), a("MO", 0, LN))
+    dma("y", [(d(T.yx[:], None), a("XN", 0, W))], 2 ** 20)
+    cp(ind(a("SN"), su(11)), a("MO", LN, 2 * LN))
+    dma("s", [(d(T.ya[:], None), a("SN", SOFF, SOFF + A))], 2 ** 20)
+    dma("s", [(d(T.yk[:], None), land("K")), (d(T.yz[:], None), land("L", 0, 64))], 2e5)
+    dma("g", [(d(T.yl[:], None), land("L", 64, 68))], 1e4)
+    return ops, Q
+
+
+def depend(ops):
+    recs, banks = {}, {}
+    for i, o in enumerate(ops):
+        dp, od = set(), set()
+        eng = list(o["alts"])[0] if len(o["alts"]) == 1 else i
+        for wr, regs in ((0, o["r"]), (1, o["w"])):
+            for n, c0, c1 in regs:
+                if n in SCRATCH and SCRATCH[n][0] == "psum":
+                    st = banks.setdefault(n, [None, [], []])
+                    if st[0] != eng:
+                        st[0], st[1], st[2] = eng, [], [x[0] for x in st[1]]
+                    dp.update(st[2])
+                    if eng == "p":
+                        od.update(x[0] for x in st[1][-1:])
+                    else:
+                        dp.update(x[0] for x in st[1] if (wr or x[3]) and x[1] < c1 and c0 < x[2])
+                    st[1].append((i, c0, c1, wr))
+                    continue
+                lst = recs.setdefault(n, [])
+                dp.update(x[0] for x in lst if (wr or x[3]) and x[1] < c1 and c0 < x[2])
+                if wr:
+                    lst[:] = [x for x in lst if not (c0 <= x[1] and x[2] <= c1)]
+                lst.append((i, c0, c1, wr))
+        dp.discard(i)
+        od.discard(i)
+        if "after" in o:
+            od.add(o["after"])
+        o["dp"], o["od"] = dp, od - dp
+
+
+def schedule(ops):
+    n = len(ops)
+    succ = [[] for _ in range(n)]
+    left = [0] * n
+    for i, o in enumerate(ops):
+        for j in o["dp"] | o["od"]:
+            succ[j].append(i)
+            left[i] += 1
+    prio = [0.0] * n
+    for i in range(n - 1, -1, -1):
+        o = ops[i]
+        c = min([x[0] for x in o["alts"].values()] or [0]) + o.get("lat", 0)
+        prio[i] = c + max([prio[j] + (HOP if i in ops[j]["dp"] else 0) for j in succ[i]] or [0])
+    x = SEED
+    for i in range(n):
+        x = (x * 1103515245 + 12345) % 2147483648
+        prio[i] += NOISE * (x / 2147483648.0) - LAM * ops[i]["st"]
+    free = {"v": 0.0, "s": 0.0, "p": 0.0, "g": 0.0, "y": 0.0}
+    busy = dict(free)
+    issue, done, rdy, order = [0.0] * n, [0.0] * n, {}, []
+    for i in range(n):
+        if left[i] == 0:
+            rdy[i] = 0.0
+    while rdy:
+        cand = []
+        for i, t in rdy.items():
+            al = ops[i]["alts"]
+            if not al:
+                cand.append((-1.0, i, None))
+                continue
+            e = min(al, key=lambda q: max(t, free[q]) + al[q][0] * (VB if q == "v" else 1))
+            cand.append((max(t, free[e]), i, e))
+        t0 = min(c[0] for c in cand)
+        t, i, e = max((c for c in cand if c[0] <= t0 + 1.0), key=lambda c: prio[c[1]])
+        o = ops[i]
+        t = max(t, rdy.pop(i))
+        c = o["alts"][e][0] if e else 0.0
+        if e:
+            free[e] = t + c
+            busy[e] += c
+        o["e"], o["t"] = e, t
+        issue[i], done[i] = t + c, t + c + o.get("lat", 0)
+        order.append(i)
+        for j in succ[i]:
+            left[j] -= 1
+            if left[j] == 0:
+                rdy[j] = max([done[k] + HOP for k in ops[j]["dp"]] + [issue[k] for k in ops[j]["od"]])
+    REPORT.update(end=max(done), busy=busy, ops=ops)
+    return order, succ
+
+
+def rank_program(g, core, T, topo):
+    if T.rank_of(core) is None:
+        return
+    ops, Q = build(g, core, T, topo)
+    depend(ops)
+    order, succ = schedule(ops)
+    count, final = {}, {}
+    known = {q: {} for q in Q}
+    for i in order:
+        o = ops[i]
+        e = o["e"]
+        if e is None:
+            o["tok"], o["clk"] = o["sem"], {}
+            final[o["sem"][0]] = o["sem"][1]
+            continue
+        kn = known[e]
+        for j in sorted(o["dp"], key=lambda k: -ops[k]["t"]):
+            s, v = ops[j]["tok"]
+            if kn.get(s, 0) < v:
+                Q[e].wait_ge(T.sem[s], v)
+                kn[s] = v
+            for s2, v2 in ops[j]["clk"].items():
+                if kn.get(s2, 0) < v2:
+                    kn[s2] = v2
+        o["clk"] = dict(kn)
+        ins = o["alts"][e][1]()
+        if "sem" in o:
+            o["tok"] = o["sem"]
+            final[o["sem"][0]] = o["sem"][1]
+        elif any(i in ops[j]["dp"] for j in succ[i]):
+            s = ESEM[e]
+            count[s] = count.get(s, 0) + 1
+            ins.then_inc(T.sem[s], 1)
+            o["tok"] = (s, count[s])
+            final[s] = count[s]
+    for s, v in final.items():
+        if known["g"].get(s, 0) < v:
+            g.wait_ge(T.sem[s], v)

@@ -8,61 +8,80 @@ NB = LW // 16
 BIG = 16 * LW
 KG = 4
 XCH = 2
-SOFF = 256
-HK0 = W + 256
-NKEY = HK0 + A
+X0 = A
+KCON = X0 + W
+KDUM = KCON + 16
+NK = KDUM + LN
+CODE = 128
+ZA, UA = 160, 60
+MWH = 200
+MUH = 304
 MAGIC = 1.5 * 2.0 ** 30
 ROUND = 1.5 * 2.0 ** 23
 CS = 1.578125
+FAR = 2.0 ** 60
 H16 = "float16"
-HO = [1, 0]
-ORDER = "H1 H0 B1 P1 C1 D1 B0 P0 C0 O1 D0 O0"
-OFFMODE = "ssss"
-GENG = ["xx", "xx", "xx"]
+ORDER = "H0 H1 B0 C0 P0 D0 B1 C1 P1 S0 O0 D1 S1 W0 W1 O1"
+OFFMODE = "ssss ssss"
+GENG = "xxx xxx xxx xxx xxx xxx"
+LEVEL = "vv vv"
 FUSE = ""
-ZENG = "x"
-JOIN = True
-LV2 = False
-CY, PCY, FIX, HOP, GCY, TT2 = 1.0, 0.48, 60.0, 120.0, 1.35, 2.0
-VB, LAM, NOISE, SEED = 1.0, 600.0, 800.0, 1
+HOMEH = False
+VSUM, PJSUM = False, False
+ONS = None
+LATE = {'W0': -1500, 'D0': -500, 'C1': -1000, 'P0': 2000, 'S0': 4000, 'B0': -2000, 'W1': 2000, 'O1': -500, 'R': -500, 'B1': 500, 'C0': -1000, 'D1': -1000, 'O0': 1000}
+SPARE = False
+SX = "vs"
+CY, PCY, FIX, HOP, GCY, SCY, SA = 0.83, 0.42, 55.0, 130.0, 1.3, 3.2, 60.0
+VB, LAM, PASSES = 1.4, 1000.0, 2
 
 
 def _sb(n, d):
     return ("sbuf", [128, n], d)
 
 
-SCRATCH = {"UZ": _sb(400, "bfloat16"), "CK": _sb(LW, H16), "CKs": _sb(LW, H16), "I12": _sb(128, H16),
-           "X": _sb(W + LN, "bfloat16"), "S": _sb(SOFF + A, "float32"), "Si": _sb(A, "int32"),
-           "XN": _sb(W + LN, "bfloat16"), "SN": _sb(SOFF + A, "float32"), "MW": _sb(408, "float32"), "MO": _sb(408, "float32"),
-           "KC": _sb(3 * LN, "int32"), "ZC": _sb(3 * LN, "bfloat16"), "TW": _sb(3 * LN, "float32"), "PGu": _sb(2 * LN, "uint16"),
-           "zs": _sb(2 * LN, "bfloat16"), "Ds": _sb(2 * LN, "bfloat16"), "Ku": _sb(LN, "uint16"), "dd": _sb(12 * LN, "float32"),
-           "sf": _sb(16 * 40, "float32"), "si": _sb(16 * 12, "int32"), "su": _sb(16 * 12, "uint16"), "sh": _sb(16 * 4, "bfloat16"),
+SCRATCH = {"CK": _sb(LW, H16), "X": _sb(NK, "bfloat16"), "S": _sb(NK, "float32"), "Si": _sb(A, "int32"),
+           "XN": _sb(NK, "bfloat16"), "SN": _sb(NK, "float32"), "MW": _sb(NH * MWH, "float32"), "MO": _sb(NH * MWH, "float32"),
+           "WK": _sb(NH * 3 * CODE, "int32"), "TT": _sb(3 * CODE, "float32"), "PGu": _sb(2 * LN, "uint16"),
+           "Ds": _sb(NH * 400, "bfloat16"), "Ku": _sb(LN, "uint16"), "YP": _sb(NH * 304, H16),
+           "sf": _sb(16 * 24, "float32"), "si": _sb(16 * 16, "int32"), "su": _sb(16 * 16, "uint16"), "sh": _sb(16 * 4, "bfloat16"),
            "cI": _sb(16, "int32"), "col": _sb(32, "float32"), "coli": _sb(16, "int32"), "PERM": _sb(5 * 128, "bfloat16"),
-           "OH": _sb(BIG, "bfloat16"), "IO": _sb(NKEY, "float32"), "C2k": _sb(LW, H16), "TFh": _sb(12, H16),
-           "ZIh": _sb(256, H16), "ZWh": _sb(256, H16), "NIh": _sb(128, H16), "BOh": _sb(128, H16)}
-for _names, _n, _d in (("xg dx gt yB aB mB yC aC mC ab2" + "".join(" zr" + _s for _s in FUSE), 16 * LN, "bfloat16"),
-                       ("Zn us D thrR ohj ohm yj nw dl Lb Lr", LN, "bfloat16"), ("Kp vi Li", LN, "int32"), ("Ph Gh ohP ohG", LN, H16),
-                       ("K20 fit key thrK To Pf GB rr dPK kr2 Kf tR", LN, "float32"), ("cJ c1 c2", 256, "float32"),
-                       ("ZI ZW1 ZWd ZWp ZWw ZW2 ZWm Z8", 256, "bfloat16"), ("NI CI NCI HI BO BOw", 128, "bfloat16"),
-                       ("CQ", LW, "bfloat16"), ("TBL TB2 TBN", 32, "float32")):
+           "OH": _sb(BIG, "bfloat16"), "IO": _sb(KDUM, "float32"), "MK": _sb(3 * LW, "bfloat16"), "MK2": _sb(LW, "bfloat16"),
+           "MK3": _sb(LW, "bfloat16"), "kr": _sb(LN, "uint16"), "EQ": _sb(NH * NB * LW, "bfloat16"), "PW": _sb(LW, "float32"),
+           "MU": _sb(NH * MUH, H16), "MI": _sb(NH * MUH, H16)}
+for _names, _n, _d in (("xg xh yB yC zr", 16 * LN, "bfloat16"), ("ZZ00 ZZ01 ZZ10 ZZ11", ZA + 3 * CODE, "bfloat16"),
+                       ("Zi Zf D thrR ohj nw fit Lb Lr ze", LN, "bfloat16"), ("Ki vi Li", LN, "int32"), ("ohP ohG GB", LN, H16),
+                       ("K20 thrK To Pf rr dl Kf", LN, "float32"), ("cJ c1 c2", 256, "float32"),
+                       ("ZI ZW1 ZWd ZWp ZW2 ZWt ZWw Z8", 256, "bfloat16"), ("NI CI NCI HI NF BO BOw", 128, "bfloat16"),
+                       ("CQ", LW, "bfloat16"), ("C3k", NB, "bfloat16"), ("TBL TB2", 32, "float32")):
     for _x in _names.split():
         SCRATCH[_x] = _sb(_n, _d)
-for _x, _n, _d in [("I", 24, "int32"), ("Z", 24, "bfloat16"), ("A", 128, "int32"), ("N", 512, "bfloat16"), ("S", 128, "float32"), ("W", 51, "float32"),
-                   ("K", 24, "float32"), ("L", 48, "bfloat16")] + [("X%d" % _c, 512 // XCH, "bfloat16") for _c in range(XCH)]:
+for _x in "dx gt aB mB aC mC ab2".split():
+    SCRATCH[_x] = ("sbuf", [128, LN, 16], "bfloat16")
+for _x, _n, _d in [("I", 24, "int32"), ("Z", 24, "bfloat16"), ("A", 128, "int32"), ("N", 512, "bfloat16"), ("S", 128, "float32"),
+                   ("W", NH * MWH // N, "float32"), ("K", 24, "float32"), ("L", 48, "bfloat16"), ("U0", MUH // N, H16), ("U1", MUH // N, H16),
+                   ("G", 2 * LN, "bfloat16")] + [("X%d" % _c, 512 // XCH, "bfloat16") for _c in range(XCH)]:
     SCRATCH["st" + _x] = ("dram", [N, 128, _n], _d)
     SCRATCH["ld" + _x] = ("dram", [N, 128, _n], _d)
 SCRATCH["stP"] = ("dram", [128, 12], "int32")
 SCRATCH["ldP"] = ("dram", [N, 128, 12], "int32")
-for _b in ("PB0", "PB1", "PB2", "PS0", "PS1", "PD", "PM0", "PM1"):
+for _b in ("PB0", "PB1", "PB2"):
+    SCRATCH[_b] = ("psum", [128, 128, KG], "float32")
+for _b in ("PS0", "PS1"):
+    SCRATCH[_b] = ("psum", [128, 32, 16], "float32")
+for _b in ("PD", "PM0", "PM1"):
     SCRATCH[_b] = ("psum", [128, 512], "float32")
-SEMAPHORES = ["ev", "es", "ep", "eg"] + ["d%d" % _i for _i in range(40)] + ["r%d" % _i for _i in range(12)] + ["l%d" % _i for _i in range(12)]
+ALL = dict(SCRATCH)
+for _x in (("stI ldI stZ ldZ stP ldP" if HOMEH else "stU0 ldU0 stU1 ldU1 stG ldG MI xh") + ("" if FUSE else " zr ze")).split():
+    del SCRATCH[_x]
+SEMAPHORES = ["ev", "es", "ep", "eg"] + ["d%d" % _i for _i in range(48)] + ["r%d" % _i for _i in range(12)] + ["l%d" % _i for _i in range(12)]
 ESEM = {"v": "ev", "s": "es", "p": "ep", "g": "eg"}
 REPORT = {}
 
 
 def build(g, core, T, topo):
     rank = T.rank_of(core)
-    ops, stg = [], [0]
+    ops, stg, seen = [], [0, ""], {}
     Q = {"v": g.vector, "s": g.scalar, "p": g.tensor, "g": g, "y": g.sync}
 
     def dt(n):
@@ -72,20 +91,34 @@ def build(g, core, T, topo):
         c1 = SCRATCH[n][1][1] if c1 is None else c1
         ps = slice(None) if p is None else slice(p[0], p[1])
         cs = slice(c0, c1) if st is None else slice(c0, c1, st)
-        return {"ap": T[n][ps, cs], "reg": [(n, c0, c1)], "n": len(range(c0, c1, st or 1)), "nm": n}
+        return {"ap": T[n][ps, cs], "reg": [(n, c0, c1, 0, 1)], "n": len(range(c0, c1, st or 1)), "nm": n}
+
+    def a3(n, r0, r1, c0=0, c1=None, st=1):
+        c1 = SCRATCH[n][1][2] if c1 is None else c1
+        return {"ap": T[n][:, r0:r1:st, c0:c1], "reg": [(n, r0, r1, c0, c1)], "n": len(range(r0, r1, st)) * (c1 - c0), "nm": n}
+
+    def one(n, r0, r1, c):
+        return {"ap": T[n][:, r0:r1, c], "reg": [(n, r0, r1, c, c + 1)], "n": r1 - r0, "nm": n}
 
     def ind(w, o):
         return {"ap": w["ap"].indirect(o["ap"]), "reg": w["reg"], "xr": o["reg"], "n": 16 * o["n"], "nm": w["nm"], "ind": 1}
 
     def d(ap, n):
-        return {"ap": ap, "reg": [(n, 0, N)] if n else [], "n": 0, "nm": n}
+        return {"ap": ap, "reg": [(n, 0, N, 0, 1)] if n else [], "n": 0, "nm": n}
 
     def val(x):
         return x["ap"] if isinstance(x, dict) else x
 
     def add(alts, outs, ins, **k):
+        if len(alts) > 1:
+            name = stg[1] + outs[0]["nm"]
+            seen[name] = seen.get(name, -1) + 1
+            name += str(seen[name])
+            k["name"] = name
+        k["tag"] = stg[1]
         rd = [r for x in ins if isinstance(x, dict) for r in x["reg"] + x.get("xr", [])] + [r for x in outs for r in x.get("xr", [])]
-        o = {"alts": alts, "w": [r for x in outs for r in x["reg"]], "r": rd, "st": stg[0]}
+        o = {"alts": alts, "w": [r for x in outs for r in x["reg"]], "r": rd, "st": stg[0],
+             "gn": sum(x["n"] for x in ins if isinstance(x, dict) and "ind" in x), "sn": sum(x["n"] for x in outs if "ind" in x)}
         o.update(k)
         ops.append(o)
         return len(ops) - 1
@@ -97,12 +130,15 @@ def build(g, core, T, topo):
         if "ind" in in0:
             return 50 + GCY * in0["n"]
         if "ind" in out:
-            return 50 + 3.2 * out["n"]
+            return 50 + SCY * out["n"]
         return max(FIX, per * CY * in0["n"])
+
+    def scost(out, in0):
+        return vcost(out, in0, 1) + (15 if "ind" in in0 else SA)
 
     def tt(out, i0, i1, op):
         ps = SCRATCH[i0["nm"]][0] == "psum" or SCRATCH[i1["nm"]][0] == "psum"
-        add({"v": (vcost(out, i0, 1 if ps else TT2), lambda: g.vector.tensor_tensor(out["ap"], i0["ap"], i1["ap"], op))}, [out], [i0, i1])
+        add({"v": (vcost(out, i0, 1 if ps else 2), lambda: g.vector.tensor_tensor(out["ap"], i0["ap"], i1["ap"], op))}, [out], [i0, i1])
 
     def ts(out, i0, s1, op0, s2=None, op1=None):
         if s2 is None:
@@ -116,25 +152,28 @@ def build(g, core, T, topo):
         if "v" in eng:
             alts["v"] = (vcost(out, i0, 0.5 if two(out, i0) else 1), lambda: g.vector.tensor_copy(out["ap"], i0["ap"]))
         if "s" in eng:
-            alts["s"] = (vcost(out, i0, 1) + 15, lambda: g.scalar.activation(out["ap"], i0["ap"], AF.Copy))
+            alts["s"] = (scost(out, i0), lambda: g.scalar.activation(out["ap"], i0["ap"], AF.Copy))
         add(alts, [out], [i0])
 
-    def act(out, i0, fn, bias=None):
-        if bias is None:
-            f = lambda: g.scalar.activation(out["ap"], i0["ap"], fn)
-        else:
-            f = lambda: g.scalar.activation(out["ap"], i0["ap"], fn, bias=bias["ap"])
-        add({"s": (vcost(out, i0, 1), f)}, [out], [i0, bias])
+    def act(out, i0, fn):
+        add({"s": (scost(out, i0), lambda: g.scalar.activation(out["ap"], i0["ap"], fn))}, [out], [i0])
 
-    def lin(out, i0, sc, bi):
-        add({"v": (vcost(out, i0, 1), lambda: g.vector.tensor_scalar(out["ap"], i0["ap"], sc, bi, OP.mult, OP.add)),
-             "s": (vcost(out, i0, 1) + 15, lambda: g.scalar.activation(out["ap"], i0["ap"], AF.Identity, bias=bi, scale=sc))}, [out], [i0])
+    def lin(out, i0, sc, bi, eng="vs"):
+        alts = {}
+        if "v" in eng:
+            alts["v"] = (vcost(out, i0, 0.5 if two(out, i0) else 1), lambda: g.vector.tensor_scalar(out["ap"], i0["ap"], sc, val(bi), OP.mult, OP.add))
+        if "s" in eng:
+            alts["s"] = (scost(out, i0), lambda: g.scalar.activation(out["ap"], i0["ap"], AF.Identity, bias=val(bi), scale=sc))
+        add(alts, [out], [i0, bi])
 
     def red(out, i0, op):
         add({"v": (vcost(out, i0, 1), lambda: g.vector.tensor_reduce(out["ap"], i0["ap"], AxisListType.X, op))}, [out], [i0])
 
+    def scan(out, d0, d1, init, op0, op1):
+        add({"v": (vcost(out, d0, 1), lambda: g.vector.tensor_tensor_scan(out["ap"], d0["ap"], d1["ap"], init, op0, op1))}, [out], [d0, d1])
+
     def mset(out, v):
-        add({"v": (FIX, lambda: g.vector.memset(out["ap"], v))}, [out], [])
+        add({"v": (vcost(out, out, 0.5 if two(out) else 1), lambda: g.vector.memset(out["ap"], v))}, [out], [])
 
     def mm(out, l, r, st=True, sp=True):
         add({"p": (max(64, r["n"]) * PCY, lambda: g.tensor.matmul(out["ap"], l["ap"], r["ap"], st, sp))}, [out], [l, r])
@@ -144,26 +183,29 @@ def build(g, core, T, topo):
             f = lambda: g.iota(out["ap"], pat, base, cm)
         else:
             f = lambda: g.iota(out["ap"], pat, base, cm, allow_small_or_imprecise_dtypes=True)
-        add({"g": (130 + 2 * out["n"], f)}, [out], [], **k)
+        add({"g": (130 + 2 * CY * out["n"], f)}, [out], [], **k)
+
+    def gcp(out, i0):
+        add({"g": (170 + 2 * CY * i0["n"], lambda: g.affine_select(out["ap"], i0["ap"], [[0, i0["n"]]], OP.is_ge, 0.0, 1, 0))}, [out], [i0])
 
     nd = [0]
 
-    def dma(q, pairs, nbytes, behind=None):
+    def dma(q, pairs, nbytes, behind=None, **k):
         sem = "d%d" % nd[0]
         nd[0] += 1
 
         def f():
             for o, i in pairs:
                 Q[q].dma_start(o["ap"], i["ap"]).then_inc(T.sem[sem], 16)
-        add({q: ((600 if q == "g" else 80) * len(pairs), f)}, [o for o, i in pairs] + ([d(None, behind)] if behind else []), [i for o, i in pairs],
-            sem=(sem, 16 * len(pairs)), lat=1800 + nbytes / 250.0)
+        return add({q: ((600 if q == "g" else 160), f)}, [o for o, i in pairs] + ([d(None, behind)] if behind else []), [i for o, i in pairs],
+                   sem=(sem, 16 * len(pairs)), lat=1800 + nbytes / 250.0, **k)
 
     peers = [r for r in range(N) if r != rank]
     far = [r for r in peers if topo.die(T.cores[r]) != topo.die(core)]
     near = [r for r in peers if r not in far]
     nr = [0]
 
-    def exchange(names, nbytes):
+    def exchange(names, nbytes, **kw):
         k = nr[0]
         nr[0] += 1
         per = 2 // len(names)
@@ -181,13 +223,13 @@ def build(g, core, T, topo):
                                                  src=T[st][r] if len(SCRATCH[st][1]) == 3 else T[st][:], dst=T[ld][rank]))
         tot = per * len(trs)
         s = add({"g": (1000, lambda: g.remote_dma_fused(trs, local_sem=T.sem["l%d" % k]))}, [], [d(None, "st" + x) for x in names],
-                sem=("l%d" % k, tot), lat=2200 + nbytes / 200.0)
+                sem=("l%d" % k, tot), lat=2200 + nbytes / 200.0, **kw)
         add({}, [d(None, "ld" + x + "R") for x in names], [], sem=("r%d" % k, tot), lat=2500 + nbytes / 200.0, after=s)
         return s
 
     def land(x, r0=0, r1=128):
         y = d(T["ld" + x][:, r0:r1, :], "ld" + x)
-        y["reg"] = y["reg"] + [("ld" + x + "R", 0, N)]
+        y["reg"] = y["reg"] + [("ld" + x + "R", 0, N, 0, 1)]
         return y
 
     def stage(x, src, r0=0, r1=128):
@@ -204,33 +246,46 @@ def build(g, core, T, topo):
     def sbs(n, c0, c1):
         return lambda r0, r1: a(n, c0, c1, p=(r0, r1))
 
-    k1, k2 = stage("I", inp(T.kw, 0, LN))
-    l1, l2 = [(d(T.stP[:], "stP"), d(T.l0[:], None))], [(d(T.ldP[rank], "ldP"), d(T.l0[:], None))]
-    z1, z2 = stage("Z", inp(T.z0, 0, LN))
     xw = W // XCH
     xs = [stage("X%d" % c, inp(T.x0, c * xw, (c + 1) * xw)) for c in range(XCH)]
-    dma("s", k1, 1e5)
-    dma("y", xs[0][0], 2 ** 20 / XCH)
-    dma("s", l1 + z1, 1e5)
-    for c in range(1, XCH):
-        dma("y", xs[c][0], 2 ** 20 / XCH * (c + 1))
-    dma("s", k2 + l2 + z2, 1e5)
-    for c in range(XCH):
-        dma("s", xs[c][1], 2 ** 20)
-    exchange(["I"], 1e5)
-    exchange(["Z", "P"], 1e5)
-    for c in range(XCH):
-        exchange(["X%d" % c], 2 ** 20 / XCH)
-    dma("y", [(a("KC", LN, 2 * LN), land("I"))], 1e5)
-    dma("y", [(a("Zn"), land("Z"))], 1e5)
-    dma("y", [(a("Li", p=(0, N)), land("P", 16 * rank, 16 * rank + 16))], 1e5)
-    for c in range(XCH):
-        dma("y", [(a("X", c * xw, (c + 1) * xw), land("X%d" % c))], 2 ** 20 / XCH)
     a1, a2 = stage("A", inp(T.asc, 0, A))
-    dma("s", a1, 2 ** 19, "stX0")
-    dma("s", a2, 2 ** 19)
-    sent = exchange(["A"], 2 ** 19)
-    dma("y", [(a("Si"), land("A"))], 2 ** 19)
+    if HOMEH:
+        dma("s", [(a("Ki"), d(T.kw[:], None)), (a("Zi"), d(T.z0[:], None)), (a("Li", p=(0, N)), d(T.l0[:], None))], 1e5)
+        prev = dma("y", [(a("XN", X0, X0 + W), d(T.x0[:], None))], 2 ** 20)
+        for c in range(XCH):
+            prev = dma("y", xs[c][0] + xs[c][1], 2 ** 20 + 2 ** 20 / XCH * (c + 1), after=prev)
+        prev = dma("y", a1 + a2, 2.5 * 2 ** 20, after=prev)
+        sent = exchange(["X0"], 2 ** 20 / XCH)
+        for c in range(1, XCH):
+            sent = exchange(["X%d" % c], 2 ** 20 / XCH, after=sent)
+        sent = exchange(["A"], 2 ** 19, after=sent)
+        for c in range(XCH):
+            prev = dma("y", [(a("X", X0 + c * xw, X0 + (c + 1) * xw), land("X%d" % c))], 2 ** 20 / XCH, after=prev)
+        dma("y", [(a("Si"), land("A"))], 2 ** 19, after=prev)
+    else:
+        k1, k2 = stage("I", inp(T.kw, 0, LN))
+        l1, l2 = [(d(T.stP[:], "stP"), d(T.l0[:], None))], [(d(T.ldP[rank], "ldP"), d(T.l0[:], None))]
+        z1, z2 = stage("Z", inp(T.z0, 0, LN))
+        ps_ = dma("s", k1, 1e5)
+        py_ = dma("y", xs[0][0], 2 ** 20 / XCH)
+        ps_ = dma("s", l1 + z1, 1e5, after=ps_)
+        for c in range(1, XCH):
+            py_ = dma("y", xs[c][0], 2 ** 20 / XCH * (c + 1), after=py_)
+        ps_ = dma("s", k2 + l2 + z2, 1e5, after=ps_)
+        for c in range(XCH):
+            ps_ = dma("s", xs[c][1], 2 ** 20, after=ps_)
+        sent = exchange(["I"], 1e5)
+        sent = exchange(["Z", "P"], 1e5, after=sent)
+        for c in range(XCH):
+            sent = exchange(["X%d" % c], 2 ** 20 / XCH, after=sent)
+        dma("s", a1 + a2, 2 ** 19, "stX0")
+        sent = exchange(["A"], 2 ** 19, after=sent)
+        dma("y", [(a("Ki"), land("I"))], 1e5)
+        dma("y", [(a("Zi"), land("Z"))], 1e5)
+        dma("y", [(a("Li", p=(0, N)), land("P", 16 * rank, 16 * rank + 16))], 1e5)
+        for c in range(XCH):
+            dma("y", [(a("X", X0 + c * xw, X0 + (c + 1) * xw), land("X%d" % c))], 2 ** 20 / XCH)
+        dma("y", [(a("Si"), land("A"))], 2 ** 19)
 
     def col(i):
         return a("col", i, i + 1)
@@ -238,7 +293,10 @@ def build(g, core, T, topo):
     def small(buf):
         return lambda i, h=None: a(buf, 16 * i, 16 * i + 12) if h is None else a(buf, 16 * i + NB * h, 16 * i + NB * (h + 1))
     sf, si, su, sh = small("sf"), small("si"), small("su"), small("sh")
-    PID, CI_, CQ16, CW, CPW, CQ128, CI16, AM, CP128, CZ8, PC = 0, 1, 2, 3, 4, 5, 6, 7, 8, 9, 16
+
+    def wide(buf, i, h, c0=0, c1=2 * NB):
+        return a(buf, 16 * (i + h) + c0, 16 * (i + h) + c1)
+    PID, CI_, CQ16, CW, CPW, CQ128, CI16, AM, CP128, CZ8, CUP, PC = 0, 1, 2, 3, 4, 5, 6, 7, 8, 9, 10, 16
     iota(a("coli", 0, 1), [[0, 1]], 0, 1)
     iota(a("cJ"), [[1, 256]], 0, 0)
     cp(col(PID), a("coli", 0, 1))
@@ -250,82 +308,85 @@ def build(g, core, T, topo):
     ts(col(CW), col(CI_), 15.0, OP.mult, 7.0, OP.add)
     ts(col(CI16), col(CI_), 16.0, OP.mult)
     ts(col(CZ8), col(PID), 16.0, OP.mult, 128.0, OP.add)
-    mset(col(AM), 2048.0)
-    ts(a("c1"), a("cJ"), col(PID), OP.is_equal)
-    ts(a("c2"), a("cJ"), col(CP128), OP.is_equal)
-    tt(a("ZI"), a("c1"), a("c2"), OP.add)
-    cp(a("ZIh"), a("ZI"))
+    mset(col(AM), 1024.0)
+    for c in range(2):
+        ts(a("ZI", 128 * c, 128 * c + 128), a("cJ", 0, 128), col(PID), OP.is_equal)
+        ts(a("ZW1", 128 * c, 128 * c + 128), a("cJ", 0, 128), col(CQ16), OP.is_equal)
     I = a("ZI", 0, 128)
-    for n, v in (("NI", -1.0), ("NIh", -1.0), ("HI", 0.5), ("CI", CS), ("NCI", -CS), ("I12", 2.0 ** -12)):
+    for n, v in (("NI", -1.0), ("HI", 0.5), ("CI", CS), ("NCI", -CS), ("NF", -2.0 ** 23)):
         ts(a(n), I, v, OP.mult)
     mset(a("CQ"), -0.25)
-    ts(a("C2k"), a("CQ"), 0.0, OP.mult, 2048.0, OP.add)
-    mset(a("c1", 0, 16), 0.5)
-    mset(a("c2", 0, 16), 0.0)
-    add({"v": (FIX, lambda: g.vector.tensor_tensor_scan(T.TBL[:, 0:16], T.c1[:, 0:16], T.c2[:, 0:16], 131072.0, OP.mult, OP.add))},
-        [a("TBL", 0, 16)], [a("c1", 0, 16), a("c2", 0, 16)])
+    mset(a("C3k"), 2048.0 + X0)
+    mset(a("c1", 0, LW), 2.0)
+    mset(a("c2", 0, LW), 0.0)
+    scan(a("PW"), a("c1", 0, LW), a("c2", 0, LW), 2.0 ** 12, OP.mult, OP.add)
+    mset(a("c1", 128, 144), 0.5)
+    scan(a("TBL", 0, 16), a("c1", 128, 144), a("c2", 0, 16), 131072.0, OP.mult, OP.add)
     cp(a("TBL", 16, 32), a("TBL", 0, 16))
-    cp(a("TBN", 0, 31), a("TBL", 1, 32))
-    mset(a("TBN", 31, 32), 1.0)
-    mset(a("TW", 0, 2 * LN), 2.0 ** 20)
     cp(a("TB2", 0, 16), a("cJ", 0, 16))
     cp(a("TB2", 16, 32), a("cJ", 0, 16))
-    ts(a("c1", 0, 16), a("cJ", 0, 16), col(CI_), OP.is_equal, 0.5, OP.mult)
-    tt(a("c2", 0, 16), a("c1", 0, 16), a("TBL", 0, 16), OP.mult)
-    red(col(CPW), a("c2", 0, 16), OP.add)
-    ts(a("c1"), a("cJ"), col(CQ16), OP.is_equal)
-    ts(a("c2"), a("cJ"), col(CQ128), OP.is_equal)
-    tt(a("ZW1"), a("c1"), a("c2"), OP.add)
-    for n, v in (("ZWd", -2.0 ** -12), ("ZWp", col(CPW)), ("ZWw", col(CW)), ("ZW2", 4096.0), ("ZWm", 2048.0 if LV2 else -2048.0), ("ZWh", 1.0)):
-        ts(a(n), a("ZW1"), v, OP.mult)
+    mset(a("TT", 0, CODE), -1.0)
+    mset(a("TT", CODE, 3 * CODE), 2.0 ** 20)
+    cp(a("TT", 2 * CODE, 2 * CODE + 31), a("TBL", 1, 32))
+    ts(a("OH", 0, 16), a("cJ", 0, 16), col(CI_), OP.is_equal)
+    tt(a("c2", 128, 144), a("OH", 0, 16), a("TBL", 0, 16), OP.mult)
+    red(col(CPW), a("c2", 128, 144), OP.add)
+    tt(a("c2", 144, 160), a("OH", 0, 16), a("PW", 0, 16), OP.mult)
+    red(col(CUP), a("c2", 144, 160), OP.add)
+    ts(a("ZWp"), a("ZW1"), col(CPW), OP.mult, 0.5, OP.mult)
+    for n, v in (("ZWd", -2048.0), ("ZW2", 4096.0), ("ZWt", 2048.0), ("ZWw", col(CW))):
+        if (n != "ZWt" or "s" in LEVEL) and (n != "ZWw" or VSUM):
+            ts(a(n), a("ZW1"), v, OP.mult)
     ts(a("Z8"), a("cJ"), col(CZ8), OP.is_equal)
     ts(a("c1", 0, 128), a("cJ", 0, 128), col(CQ16), OP.subtract, 0.0, OP.is_ge)
     ts(a("c2", 0, 128), a("cJ", 0, 128), col(CQ16), OP.subtract, 16.0, OP.is_lt)
     tt(a("BO"), a("c1", 0, 128), a("c2", 0, 128), OP.mult)
-    cp(a("BOh"), a("BO"))
     ts(a("BOw"), a("BO"), col(CW), OP.mult)
-    ts(a("c1", 0, 5), a("cJ", 0, 5), col(CI_), OP.add)
-    ts(a("cI", 0, 5), a("c1", 0, 5), -2.0, OP.add, 0.2, OP.mult)
-    ts(a("c2", 0, 5), a("cI", 0, 5), -5.0, OP.mult)
-    tt(a("c1", 0, 5), a("c1", 0, 5), a("c2", 0, 5), OP.add)
-    ts(a("c1", 0, 5), a("c1", 0, 5), -16.0, OP.mult, col(CP128), OP.add)
-    ts(a("cI", 0, 5), a("c1", 0, 5), -16.0, OP.add)
+    ts(a("c1", 160, 165), a("cJ", 0, 5), col(CI_), OP.add)
+    ts(a("cI", 0, 5), a("c1", 160, 165), -2.0, OP.add, 0.2, OP.mult)
+    ts(a("c2", 160, 165), a("cI", 0, 5), -5.0, OP.mult)
+    tt(a("c1", 160, 165), a("c1", 160, 165), a("c2", 160, 165), OP.add)
+    ts(a("c1", 160, 165), a("c1", 160, 165), -16.0, OP.mult, col(CP128), OP.add)
+    ts(a("cI", 0, 5), a("c1", 160, 165), -16.0, OP.add)
     ts(a("cI", 0, 5), a("cI", 0, 5), 127, OP.bitwise_and)
     cp(a("col", PC, PC + 5), a("cI", 0, 5))
     for c in range(5):
-        ts(a("PERM", 128 * c, 128 * c + 128), a("cJ", 0, 128), col(PC + c), OP.is_equal)
-    iota(a("c1", 0, LW), [[1, 16], [256, NB]], 0, 0)
-    ts(a("CK"), a("c1", 0, LW), col(CI16), OP.add)
-    ts(a("CKs"), a("CK"), 2.0 ** -11, OP.mult)
-    TOF, DUM, HKT, BB, LO, THO, TMP, DUF, MUL = 0, 1, 2, 3, 5, 6, 7, 9, 36
-    ts(sf(TOF), a("cJ", 0, 12), 16.0, OP.mult, col(CI_), OP.add)
-    cp(sh(0), sf(TOF))
-    ts(a("sf", 16 * BB, 16 * BB + 12), sf(TOF), float(W), OP.add)
-    ts(a("sf", 16 * BB + 12, 16 * BB + 24), sf(TOF), -1.0, OP.mult)
-    ts(sf(HKT), sf(TOF), 1.0 / 256, OP.mult, float(HK0), OP.add)
-    ts(a("TFh"), sf(TOF), 1.0 / 256, OP.mult)
-    ts(sf(DUF), sf(TOF), 1.0 + 1.0 / 256, OP.mult, float(W), OP.add)
-    mset(a("sf", 16 * MUL, 16 * MUL + NB), 4.0)
-    mset(a("sf", 16 * MUL + NB, 16 * MUL + 2 * NB), 21.0)
-    ts(si(0, 0), sf(TOF, 0), -(NB - 1) / 2.0, OP.add, 1.0 / NB, OP.mult)
-    ts(sf(TMP, 0), si(0, 0), -float(NB), OP.mult)
-    tt(sf(TMP, 0), sf(TMP, 0), sf(TOF, 0), OP.add)
+        ts(a("PERM", 128 * c, 128 * c + 128), a("cJ", 0, 128), col(PC + c), OP.is_equal, float(CODE), OP.mult)
+    iota(a("rr", 0, LW), [[256, NB], [1, 16]], 0, 0)
+    ts(a("CK"), a("rr", 0, LW), col(CI16), OP.add)
+    DUM, WGT, MUL, THR, TMP, VS, THE, U1, KEY, NN, CC, CNT, CON = 0, 1, 3, 5, 6, 8, 14, 15, 16, 17, 18, 19, 20
+    ts(sf(TMP), a("cJ", 0, 12), 16.0, OP.mult, col(CI_), OP.add)
+    ts(sf(DUM), sf(TMP), float(KDUM), OP.add)
     for h in range(NH):
-        ts(su(0, h), sf(TMP, 0), float(NB * h), OP.add)
-    ts(a("tR"), a("cJ", 0, LN), 1.0 / 256, OP.mult)
-    mset(si(11), 0)
-    mset(a("sf", 16 * THO, 16 * THO + 16), 0.0)
-    for n in ("X", "XN"):
-        mset(a(n, W, W + LN), 0.0)
-    for n in ("S", "SN"):
-        mset(a(n, 0, SOFF), 0.0)
-    ts(a("OH", 0, 16), a("cJ", 0, 16), col(CI_), OP.is_equal)
+        cp(wide("sh", 0, h, 0, NB), sf(TMP, 0))
+    ts(sf(WGT, 0), a("PW", 0, LW, 16), col(CUP), OP.mult, 2.0 ** -13, OP.mult)
+    for j, v in enumerate((4.0, 21.0, 2048.0)):
+        mset(a("sf", 16 * MUL + NB * j, 16 * MUL + NB * (j + 1)), v)
+    cp(su(0), a("cJ", 0, 12))
+    mset(si(0), 0)
+    for h in range(NH):
+        mset(a("WK", 3 * CODE * h + LW, 3 * CODE * (h + 1)), 0)
+    mset(a("YP"), 0.0)
+    mset(a("MW"), 0.0)
+    mset(a("MU"), 0.0)
+    mset(a("sf", 16 * THR, 16 * THR + 16), 0.0)
+    for n in ("ZZ00", "ZZ01", "ZZ10", "ZZ11"):
+        mset(a(n, UA), 0.0)
     c = 16
     while c < BIG:
         cp(a("OH", c, min(2 * c, BIG)), a("OH", 0, min(c, BIG - c)))
         c *= 2
-    for c in range(0, NKEY, 896):
-        iota(a("IO", c, c + 896), [[1, 896]], c, 0, after=sent)
+    ts(a("MK"), a("OH", 0, 3 * LW), -1.0, OP.add, FAR, OP.mult)
+    ts(a("c1", 0, LW), a("OH", 0, LW), 2048.0 + X0, OP.mult)
+    tt(a("MK2"), a("c1", 0, LW), a("MK", 0, LW), OP.add)
+    tt(a("c2", 0, LW), a("OH", 0, LW), a("PW"), OP.mult)
+    ts(a("c2", 128, 128 + LW), a("MK", 0, LW), 0.5 * FAR, OP.mult)
+    tt(a("c2", 0, LW), a("c2", 128, 128 + LW), a("c2", 0, LW), OP.subtract)
+    ts(a("MK3"), a("c2", 0, LW), 2.0, OP.mult)
+    for c in range(0, KDUM, 856):
+        iota(a("IO", c, c + 856), [[1, 856]], c, 0, after=sent)
+    for x, s in (("X", "S"), ("XN", "SN")) if SPARE else ():
+        dma("y", [(a(s, A, NK), a("IO", 0, NK - A)), (a(x, 0, X0), a("OH", 0, X0)), (a(x, KCON, NK), a("OH", 0, NK - KCON))], 2 ** 21)
 
     def SH(n, s):
         return a(n, 128 - 16 * (s % N), 256 - 16 * (s % N))
@@ -333,341 +394,371 @@ def build(g, core, T, topo):
     def WW(n, s, i):
         return a(n, 128 - 16 * (s % N) - i, 256 - 16 * (s % N) - i)
 
-    mset(a("UZ"), 0.0)
-
     def hs(n, h, base=0):
-        if n == "us" and JOIN:
-            return a("UZ", 200 * h, 200 * h + LW)
         return a(n, base + LW * h, base + LW * (h + 1))
 
-    def shift(ps, pc, mat, sign, extra, src, h, acc=False):
-        t0 = LW * h
-        for m in range(5):
-            f = (m - t0) % 5
-            mm(a(ps, pc + f, pc + LW, 5), SH(mat, sign * (1 + m + extra)), a(src, t0 + f, t0 + LW, 5), not acc, not acc or m == 4)
-
-    def osum(out, mat, s, src, c0, c1, first=True, last=True):
+    def osum(out, mat, s, src, h, first=True, last=True):
         for i in range(16):
-            mm(out, WW(mat, s, i), a(src, c0 + i, c1, 16), first and i == 0, last and i == 15)
+            mm(out, WW(mat, s, i), a3(src, LW * h + i, LW * (h + 1), st=16), first and i == 0, last and i == 15)
+
+    def diag(out, ps, r0, r1, terms, mask):
+        mm(a3(ps, r0, r1), I, mask, True, False)
+        for j, (q0, q1, l, r) in enumerate(terms):
+            mm(a3(ps, q0, q1), l, r, False, j == len(terms) - 1)
+        red(out, a3(ps, r0, r1), OP.max)
 
     nb = [0]
 
-    def sub(src, h, kg, zz, pos, neg, keep=False):
+    def sub(src, h, kg, zz, pos, neg):
         nb[0] += 1
-        b = ("PB0", "PB1", "PB2", "PD")[nb[0] % (4 if LV2 else 3)]
+        b = ("PB0", "PB1", "PB2")[nb[0] % 3]
         for kk in range(KG):
-            o = a(b, kk * LW, (kk + 1) * LW)
-            mm(o, pos, a(src, BIG * h + kg * KG + kk, BIG * (h + 1), 16), kk == 0 or not keep, False)
-            mm(o, neg, zz, False, not keep or kk == KG - 1)
-        return a(b, 0, KG * LW)
+            o, k = one(b, 0, LW, kk), kg * KG + kk
+            mm(o, pos, a(src, BIG * h + k, BIG * (h + 1), 16) if len(SCRATCH[src][1]) == 2 else one(src, LW * h, LW * (h + 1), k), True, False)
+            mm(o, neg, zz, False, True)
+        return a3(b, 0, LW)
 
     def big(n, h, kg):
-        return a(n, BIG * h + kg * KG * LW, BIG * h + (kg + 1) * KG * LW)
+        return a3(n, LW * h, LW * (h + 1), kg * KG, (kg + 1) * KG)
 
-    def words(dst, h, lst, base, j):
-        eng, s = GENG[j], "HBC"[j]
+    def words(dst, h, src, lst, base, j, then=None):
+        eng = GENG.split()[NH * j + h]
         w = LW // len(eng)
         for c, e in enumerate(eng):
             c0 = LW * h + c * w
-            o, i = a(dst, 16 * c0, 16 * (c0 + w)), ind(a("X", 0, W), a(lst, base + c0, base + c0 + w))
-            if s in FUSE:
-                tt(o, i, a("zr" + s, 16 * c0, 16 * (c0 + w)), OP.subtract)
+            o, i = a(dst, 16 * c0, 16 * (c0 + w)), ind(a(src, X0, X0 + W), a(lst, base + c * w, base + (c + 1) * w))
+            if then:
+                tt(o, i, a("zr", 16 * c0, 16 * (c0 + w)), OP.subtract)
+                act(a3(then, c0, c0 + w), o, AF.Abs)
             else:
                 cp(o, i, e.replace("x", "vs"))
 
-    def absolute(dst, src, h, kg):
-        for k in range(kg * KG, (kg + 1) * KG):
-            act(a(dst, BIG * h + k * LW, BIG * h + (k + 1) * LW), a(src, BIG * h + k, BIG * (h + 1), 16), AF.Abs)
-
     def halve(out, pm, c, x, y, wy):
         o = a(pm, c, c + LW)
-        mm(o, a("HI"), x, True, False)
+        mm(o, I, a("CQ"), True, False)
         mm(o, wy, y, False, False)
-        mm(o, I, a("CQ"), False, True)
+        mm(o, a("HI"), x, False, True)
         ts(out, o, ROUND, OP.add, ROUND, OP.subtract)
 
-    def thresholds(step, last):
-        if step:
-            ts(sf(TMP), su(3), float(2 * LN), OP.is_ge)
-            tt(sf(LO), sf(LO), sf(TMP), OP.add)
-        cp(su(1), sf(LO))
-        if last:
-            cp(a("Lr"), ind(a("TB2"), su(1)), "vs")
-            return
-        cp(a("TW", 2 * LN, 3 * LN), ind(a("TBN"), su(1)), "vs")
-        cp(a("thrR"), ind(a("TBL"), su(1)), "vs")
-        osum(a("PM0", 0, 12), "ZW1", 0, "thrR", 0, LN)
-        lin(sf(THO), a("PM0", 0, 12), 1.0 / 16, 0.0)
-        for h in HO:
-            cp(hs("thrK", h), ind(a("sf", 16 * THO, 16 * THO + 16), su(0, h)), "vs")
+    def bounds():
+        cp(a("thrK"), ind(a("sf", 16 * THR, 16 * THR + 16), su(0)), "vs")
 
-    def zshift(h):
-        pm, c = "PM%d" % h, 2 * LW * h
-        if JOIN:
-            cp(a("UZ", 200 * h + 100, 200 * h + 100 + LW), hs("Zn", h), "vs")
-        else:
-            shift(pm, 0, "ZI", 1, 0, "Zn", h)
-            shift(pm, LW, "ZI", 1, 1, "Zn", h)
-            cp(a("zs", c, c + 2 * LW), a(pm, 0, 2 * LW), "s")
-        cp(hs("ZC", h), hs("Zn", h), "vs")
-        for s in FUSE:
-            z = {"H": hs("Zn", h), "B": a("zs", c, c + LW), "C": a("zs", c + LW, c + 2 * LW)}[s]
-            for k in range(16):
-                cp(a("zr" + s, BIG * h + k, BIG * (h + 1), 16), z, ZENG[k % len(ZENG)].replace("x", "vs"))
+    def powers():
+        cp(a("thrR"), ind(a("TBL"), su(1)), "vs")
+        diag(sf(THR), "PS0", 0, 12, [(0, 12, I, a("thrR"))], a("MK", 0, LN))
+
+    rnd = [0]
+
+    def zz(h, c0, c1, nxt=0, st=None):
+        return a("ZZ%d%d" % ((rnd[0] + nxt) % 2, h), c0, c1, st)
+
+    def aim(h, nxt=0):
+        if nxt and rnd[0] == RO - 1:
+            return hs("Zf", h)
+        return zz(h, ZA, ZA + LW, nxt)
+
+    def uz(h, c0, c1, st=None):
+        if HOMEH and rnd[0] == 0:
+            return a("MI", MUH * h + c0, MUH * h + c1, st)
+        return zz(h, UA + c0, UA + c1, st=st)
+
+    def yp(h, c0, c1, st=None):
+        return a("YP", 304 * h + c0, 304 * h + c1, st)
+
+    def ds(h, j):
+        return a("Ds", 400 * h + 200 * j, 400 * h + 200 * j + LW)
+
+    def zs(h, j):
+        return a("Ds", 400 * h + 200 * j + 100, 400 * h + 200 * j + 100 + LW)
+
+    def fused(h):
+        return str(h) in FUSE and rnd[0] > 0
 
     cp(a("Lb", p=(0, N)), a("Li", p=(0, N)))
     for i in range(16):
         mm(a("PM0", 0, 12), a("Z8", 128 - i, 256 - i, p=(0, N)), a("Lb", i, LN, 16, p=(0, N)), i == 0, i == 15)
-    cp(sf(LO), a("PM0", 0, 12))
-    cp(a("Ku"), a("KC", LN, 2 * LN))
-    thresholds(False, False)
-    for h in HO:
-        zshift(h)
-    cp(a("S", SOFF, SOFF + A), a("Si"))
+    cp(su(1), a("PM0", 0, 12))
+    cp(a("Ku"), a("Ki"))
+    for h in range(NH):
+        if HOMEH:
+            cp(a("MU", MUH * h + 292, MUH * h + 292 + NB), a("PM0", NB * h, NB * (h + 1)))
+            cp(a("MU", MUH * h + 100, MUH * h + 100 + LW), hs("Zi", h))
+            ts(a("MU", MUH * h + 196, MUH * h + 196 + LW), hs("Ki", h), -2048.0, OP.add)
+        else:
+            cp(wide("sh", 0, h, NB, 2 * NB), a("PM0", NB * h, NB * (h + 1)))
+            cp(aim(h), hs("Zi", h))
+    powers()
+    bounds()
+    if not HOMEH:
+        cp(a("Kf"), a("Ki"))
+    for c in range(2):
+        cp(a("S", 512 * c, 512 * c + 512), a("Si", 512 * c, 512 * c + 512), SX)
 
-    MH, T8, HK, ME, MF, THE, LT, CC, U1, U2, KD, NB2, AA, MN, PEN, RR, CNT = 10, 11, 12, 15, 16, 17, 18, 19, 20, 21, 22, 23, 24, 26, 27, 29, 34
+    def speaker(h, src, xg, z, us):
+        ps, pm = "PS%d" % h, "PM%d" % h
+        words(xg, h, src, "Ku", LW * h, 0)
+        for kg in range(16 // KG):
+            act(big("dx", h, kg), sub(xg, h, kg, z, I, a("NI")), AF.Abs)
+            ts(big("gt", h, kg), big("dx", h, kg), 40.0, OP.is_gt)
+        osum(a(pm, 0, LW), "ZWp", 0, "gt", h)
+        mm(a3(ps, 0, NB), I, a("CK"), True, False)
+        osum(a3(ps, 0, NB), "ZWd", 0, "dx", h, False, False)
+        tt(hs("fit", h), a(pm, 0, LW), hs("thrK", h), OP.is_lt)
+        mm(a3(ps, 0, NB), a("NF"), hs("fit", h), False, True)
+        red(wide("si", 2, h, 0, NB), a3(ps, 0, NB), OP.min)
+        ts(wide("si", 2, h, 8, 8 + NB), wide("si", 2, h, 0, NB), 2047, OP.bitwise_and)
+        cp(su(2, h), wide("si", 2, h, 8, 8 + NB), SX)
+        tt(us, ind(a(xg, BIG * h, BIG * (h + 1)), su(2, h)), z, OP.subtract)
 
-    def pair(buf, i, h):
-        return a(buf, 16 * i + 2 * NB * h, 16 * i + 2 * NB * (h + 1))
-
-    def half(buf, i, h, j):
-        return a(buf, 16 * i + 2 * NB * h + NB * j, 16 * i + 2 * NB * h + NB * (j + 1))
-
-    def least(slot, h, src, c):
-        for b in range(NB):
-            red(a("sf", 16 * slot + NB * h + b, 16 * slot + NB * h + b + 1), a(src, c + b, c + LW, NB), OP.min)
+    def first(h):
+        speaker(h, "XN", "xh", hs("Zi", h), a("MU", MUH * h, MUH * h + LW))
+        u1, u2 = stage("U%d" % h, sbs("MU", MUH * h, MUH * (h + 1)))
+        dma("s", u1 + u2, 1e5)
+        exchange(["U%d" % h], 1e5)
+        dma("s", [(a("MI", MUH * h, MUH * (h + 1)), land("U%d" % h))], 1e5)
+        cp(aim(h), uz(h, 100, 100 + LW), "vs")
+        lin(hs("Kf", h), a("MI", MUH * h + 196, MUH * h + 196 + LW), 1.0, 2048.0)
+        cp(wide("sh", 0, h, NB, 2 * NB), a("MI", MUH * h + 292, MUH * h + 292 + NB), "vs")
+        cp(su(1, h), a("MI", MUH * h + 292, MUH * h + 292 + NB))
+        if h == NH - 1:
+            powers()
+            g1, g2 = stage("G", sbs("xh", 0, 16 * LN))
+            dma("y", g1 + g2, 2 ** 20)
+            exchange(["G"], 2 ** 20)
+            dma("y", [(a("xg"), land("G"))], 2 ** 20)
 
     def home(h, last):
         ps, pm, db = "PS%d" % h, "PM%d" % h, 2 * LW * h
-        words("xg", h, "Ku", 0, 0)
-        for kg in range(16 // KG):
-            if "H" in FUSE:
-                absolute("dx", "xg", h, kg)
-            else:
-                act(big("dx", h, kg), sub("xg", h, kg, hs("Zn", h), I, a("NI")), AF.Abs)
-            ts(big("gt", h, kg), big("dx", h, kg), 40.0, OP.is_gt)
-        cp(hs("KC", h, 2 * LN), hs("KC", h, LN))
-        ts(hs("K20", h), hs("KC", h, LN), 20.0, OP.mult)
-        mm(a(ps, 0, LW), a("I12"), a("CKs"), True, False)
-        osum(a(ps, 0, LW), "ZWd", 0, "dx", BIG * h, BIG * (h + 1), False, True)
-        osum(a(ps, LW, 2 * LW), "ZWp", 0, "gt", BIG * h, BIG * (h + 1))
-        tt(hs("fit", h), a(ps, LW, 2 * LW), hs("thrK", h), OP.is_lt)
-        tt(hs("key", h), a(ps, 0, LW), hs("fit", h), OP.subtract)
-        least(MH, h, "key", LW * h)
-        ts(si(0, h), sf(MH, h), 2.0 ** 23, OP.mult)
-        ts(si(1, h), si(0, h), 2047, OP.bitwise_and)
-        cp(su(2, h), si(1, h))
-        spk = ind(a("xg", BIG * h, BIG * (h + 1)), su(2, h))
-        if "H" in FUSE:
-            cp(hs("us", h), spk, "vs")
+        us = uz(h, 0, LW)
+        if HOMEH and rnd[0] == 0:
+            first(h)
         else:
-            tt(hs("us", h), spk, hs("Zn", h), OP.subtract)
-        if JOIN:
-            for j in range(2):
-                for m in range(5):
-                    f = (m - LW * h) % 5
-                    mm(a(pm, 100 + 200 * j + f, 300 + 200 * j, 5), SH("ZI", 1 + m + j), a("UZ", 200 * h + f, 200 * h + 200, 5))
-            for j in range(2):
-                act(a("Ds", db + LW * j, db + LW * (j + 1)), a(pm, 100 + 200 * j, 100 + 200 * j + LW), AF.Abs)
-            for j in range(2):
-                act(a("PD", db + LW * j, db + LW * (j + 1)), a(pm, 100 + 200 * j, 100 + 200 * j + LW), AF.Abs)
-                cp(a("zs", db + LW * j, db + LW * (j + 1)), a(pm, 200 + 200 * j, 200 + 200 * j + LW), "s")
-        else:
-            shift("PD", db, "ZI", 1, 0, "us", h)
-            shift("PD", db + LW, "ZI", 1, 1, "us", h)
-            pd = a("PD", db, db + 2 * LW)
-            act(a("Ds", db, db + 2 * LW), pd, AF.Abs)
-            act(pd, pd, AF.Abs)
-        osum(a("PS%d" % h, 4 * LW, 4 * LW + 2 * NB) if JOIN else a(pm, 0, 2 * NB), "ZWw", 0, "Ds", db, db + 2 * LW)
-        tt(pair("si", 2, h), a("PS%d" % h, 4 * LW, 4 * LW + 2 * NB) if JOIN else a(pm, 0, 2 * NB), a("sf", 16 * MUL, 16 * MUL + 2 * NB), OP.mult)
-        ts(pair("si", 4, h), pair("si", 2, h), 2, OP.arith_shift_right, A - 1, OP.bitwise_and)
-        cp(pair("su", 4, h), pair("si", 4, h))
+            speaker(h, "X", "xg", aim(h), us)
+        lin(hs("K20", h), hs("Kf", h), 20.0, 0.0)
         for j in range(2):
-            cp(hs("PGu", h, LN * j), ind(a("S", SOFF, SOFF + A), half("su", 4, h, j)))
-        act(hs("D", h), hs("us", h), AF.Abs)
-        if not LV2:
-            osum(a(pm, 16, 16 + NB), "ZW1", 0, "Ds", db, db + LW)
-        mm(a(pm, 32, 32 + LW), a("BOw"), hs("D", h))
-        if not LV2:
-            lin(sf(T8, h), a(pm, 16, 16 + NB), 2048.0, 800.0 * 2048)
-        tt(hs("vi", h), a(pm, 32, 32 + LW), hs("K20", h), OP.add)
-        ts(hs("KC", h), hs("vi", h), 2, OP.arith_shift_right, W - 1, OP.bitwise_and)
-        halve(hs("ZC", h, LN), pm, 128, hs("us", h), hs("Zn", h), I)
-        tt(sf(HK, h), half("si", 4, h, 0), sf(HKT, h), OP.add)
-        ts(hs("Ph", h), hs("PGu", h), -2048.0, OP.add)
-        ts(hs("Gh", h), hs("PGu", h, LN), -2048.0, OP.add)
-        cp(hs("Pf", h), hs("PGu", h))
-        mm(a(pm, 256, 256 + LW), SH("ZIh", -1), hs("Gh", h))
-        cp(hs("GB", h), a(pm, 256, 256 + LW), "s")
+            for m in range(5):
+                f = (m - LW * h) % 5
+                mm(a(pm, 200 * j + f, 200 + 200 * j, 5), SH("ZI", 1 + m + j), uz(h, f, 200, 5))
+        act(a("Ds", 400 * h, 400 * h + 396), a(pm, 0, 396), AF.Abs)
+        lv = LEVEL.split()[h]
+        nv = 2 if lv == "ss" else 3
+        vi = a("si", 16 * (4 + 2 * h), 16 * (4 + 2 * h) + nv * NB)
+        vs = a("sf", 16 * (VS + 2 * h), 16 * (VS + 2 * h) + nv * NB)
+        terms = [(NB, 2 * NB, a("BOw"), ds(h, 0)), (2 * NB, 3 * NB, a("BOw"), ds(h, 1)), (3 * NB, 4 * NB, a("BO"), ds(h, 0))]
+        diag(vs, ps, NB, (1 + nv) * NB, terms[:nv], a("MK", 0, nv * LW))
+        tt(vi, vs, a("sf", 16 * MUL, 16 * MUL + nv * NB), OP.mult)
+        for j in range(2):
+            if lv[j] == "v":
+                mm(a("PD", db + LW * j, db + LW * (j + 1)), I, ds(h, j))
+        ts(wide("si", 8, h), a("si", 16 * (4 + 2 * h), 16 * (4 + 2 * h) + 2 * NB), 2, OP.arith_shift_right, A - 1, OP.bitwise_and)
+        cp(wide("su", 4, h), wide("si", 8, h), SX)
+        cp(a("PGu", db, db + 2 * LW), ind(a("S", 0, A), wide("su", 4, h)), SX)
+        act(hs("D", h), us, AF.Abs)
+        mm(a(pm, 0, LW), a("BOw"), hs("D", h))
+        tt(hs("vi", h), a(pm, 0, LW), hs("K20", h), OP.add)
+        ts(a("WK", 3 * CODE * h, 3 * CODE * h + LW), hs("vi", h), 2, OP.arith_shift_right, W - 1, OP.bitwise_and)
+        halve(zz(h, ZA + CODE, ZA + CODE + LW), pm, 100, us, uz(h, 100, 100 + LW), I)
+        ts(yp(h, 100, 100 + 2 * LW), a("PGu", db, db + 2 * LW), -2048.0, OP.add)
+        lin(hs("Pf", h), yp(h, 100, 100 + LW), 1.0, 2048.0)
+        mm(a(pm, 200, 200 + LW), SH("ZI", -1), yp(h, 100 + LW, 100 + 2 * LW))
+        cp(hs("GB", h), a(pm, 200, 200 + LW), "vs")
 
     def look(h, j):
         ps = "PS%d" % h
         y, aa, mx = (("yB", "aB", "mB"), ("yC", "aC", "mC"))[j]
-        words(y, h, "PGu", LN * j, 1 + j)
         c = 2 * LW * h + LW * j
+        fu, lv = j == 0 and fused(h), LEVEL.split()[h][j]
+        words(y, h, "X", "PGu", c, 1 + j, aa if fu else None)
         for kg in range(16 // KG):
-            if "BC"[j] in FUSE:
-                absolute(aa, y, h, kg)
-            else:
-                b = sub(y, h, kg, a("zs", c, c + LW), I, a("NI"), LV2)
-                if LV2:
-                    act(b, b, AF.Abs)
-                    for kk in range(KG):
-                        mm(a(b["nm"], kk * LW, (kk + 1) * LW), a("NI"), a("Ds", c, c + LW), False, kk == KG - 1)
-                act(big(aa, h, kg), b, AF.Abs)
-            for kk in range(0 if LV2 else KG):
-                c0 = BIG * h + (kg * KG + kk) * LW
-                tt(a(mx, c0, c0 + LW), a(aa, c0, c0 + LW), a("PD", c, c + LW), OP.max)
-        o = a(ps, (2 + j) * LW, (3 + j) * LW)
-        mm(o, a("ZIh", 0, 128), a("CK"), True, False)
-        osum(o, "ZWm", -j, aa, BIG * h, BIG * (h + 1), False, LV2)
-        if not LV2:
-            osum(o, "ZW2", -j, mx, BIG * h, BIG * (h + 1), False, True)
-        least((ME, MF)[j], h, ps, (2 + j) * LW)
+            if not fu:
+                act(big(aa, h, kg), sub(y, h, kg, zs(h, j), I, a("NI")), AF.Abs)
+            if lv == "v":
+                for k in range(kg * KG, (kg + 1) * KG):
+                    tt(one(mx, LW * h, LW * (h + 1), k), one(aa, LW * h, LW * (h + 1), k), a("PD", c, c + LW), OP.max)
+            elif kg > 0:
+                act(big(mx, h, kg - 1), sub(aa, h, kg - 1, ds(h, j), I, a("NI")), AF.Abs)
+        o = a3(ps, (1 + j) * NB, (2 + j) * NB)
+        mm(o, I, a("CK"), True, False)
+        if lv == "v":
+            osum(o, "ZWd", -j, aa, h, False, False)
+            osum(o, "ZW2", -j, mx, h, False, True)
+        else:
+            act(big(mx, h, 3), sub(aa, h, 3, ds(h, j), I, a("NI")), AF.Abs)
+            osum(o, "ZWt", -j, mx, h, False, True)
+        red(wide("si", 10, h, NB * j, NB * (j + 1)), o, OP.min)
+        ts(wide("si", 12, h, NB * j, NB * (j + 1)), wide("si", 10, h, NB * j, NB * (j + 1)), 2047, OP.bitwise_and)
+        cp(wide("su", 6, h, NB * j, NB * (j + 1)), wide("si", 12, h, NB * j, NB * (j + 1)), SX)
+
+    def msg(h, c0, c1):
+        return a("MW", MWH * h + c0, MWH * h + c1)
 
     def partner(h, last):
-        pm = "PM%d" % h
-        cp(si(6, h), sf(ME, h))
-        ts(si(7, h), si(6, h), 2047, OP.bitwise_and)
-        cp(su(6, h), si(7, h))
-        if LV2:
-            ts(sf(LT, h), sf(ME, h), 800.0 * 2048, OP.is_lt)
+        ps, pm, db = "PS%d" % h, "PM%d" % h, 2 * LW * h
+        me, jl = wide("si", 10, h, 0, NB), wide("su", 6, h, 0, NB)
+        lv, true = LEVEL.split()[h], me
+        if lv[0] == "v":
+            true = sf(TMP, h)
+            tt(true, me, a("si", 16 * (4 + 2 * h) + 2 * NB, 16 * (4 + 2 * h) + 3 * NB), OP.subtract)
+        lin(sf(THE, h), true if lv == "vs" else me, 1.0, col(AM), SX)
+        ts(sf(CC, h), true, 800.0 * 2048, OP.is_lt, 1.0, OP.add)
+        ts(sf(TMP + 1, h), true, 800.0 * 2048, OP.is_lt, float(KCON), OP.mult)
+        best = ind(a("yB", BIG * h, BIG * (h + 1)), jl)
+        if fused(h):
+            tt(yp(h, 0, LW), best, zs(h, 0), OP.add)
         else:
-            tt(sf(LT, h), sf(ME, h), sf(T8, h), OP.is_lt)
-        tt(sf(THE, h), sf(ME, h), si(7, h), OP.subtract)
-        ts(sf(THE, h), sf(THE, h), col(AM), OP.add)
-        lin(sf(CC, h), sf(LT, h), float(LN), float(LN))
-        best = ind(a("yB", BIG * h, BIG * (h + 1)), su(6, h))
-        if "B" in FUSE:
-            tt(hs("yj", h), best, a("zs", 2 * LW * h, 2 * LW * h + LW), OP.add)
+            cp(yp(h, 0, LW), best, "vs")
+        cp(hs("ohj", h), ind(a("OH"), jl), "vs")
+        tt(hs("ohP", h), hs("ohj", h), yp(h, 100, 100 + LW), OP.mult)
+        if PJSUM:
+            pj = a(pm, 400, 400 + NB)
+            mm(pj, I, a("C3k"), True, False)
+            for i in range(16):
+                mm(pj, WW("ZW1", 0, i), a("ohP", LW * h + i, LW * (h + 1), 16), False, i == 15)
+            tt(sf(U1, h), pj, sf(TMP + 1, h), OP.max)
         else:
-            cp(hs("yj", h), best, "vs")
-        cp(hs("ohj", h), ind(a("OH"), su(6, h)), "vs")
-        tt(hs("ohP", h), hs("ohj", h), hs("Ph", h), OP.mult)
-        mm(a(pm, 16, 16 + NB), a("ZIh", 0, 128), a("C2k", 0, NB), True, False)
-        mm(a(pm, 16, 16 + NB), a("ZIh", 0, 128), a("TFh", NB * h, NB * (h + 1)), False, False)
-        osum(a(pm, 16, 16 + NB), "ZWh", 0, "ohP", LW * h, LW * (h + 1), False, True)
-        tt(sf(U2, h), sf(DUF, h), sf(LT, h), OP.mult)
-        shift(pm, 128, "ZI", -1, 0, "yj", h)
-        tt(sf(U1, h), a(pm, 16, 16 + NB), sf(U2, h), OP.max)
-        cp(hs("ZC", h, 2 * LN), a(pm, 128, 128 + LW), "vs")
-        tt(sf(KD, h), sf(U1, h), sf(HK, h), OP.subtract)
-        halve(hs("MW" if last else "nw", h), pm, 256, hs("yj", h), a("Ds", 2 * LW * h, 2 * LW * h + LW), a("HI"))
+            diag(sf(U1, h), ps, 4 * NB, 5 * NB, [(4 * NB, 5 * NB, a("BO"), hs("ohP", h))], a("MK2"))
+            tt(sf(U1, h), sf(U1, h), sf(TMP + 1, h), OP.max)
+        for m in range(5):
+            f = (m - LW * h) % 5
+            mm(a(pm, 200 + f, 400, 5), SH("ZI", -1 - m), yp(h, f, 200, 5))
+        cp(zz(h, ZA + 2 * CODE, ZA + 2 * CODE + LW), a(pm, 200, 200 + LW), "vs")
+        lin(a("WK", 3 * CODE * h + 2 * CODE, 3 * CODE * h + 2 * CODE + LW), a(pm, 300, 300 + LW), 1.0, 2048.0, SX)
+        halve(msg(h, 0, LW) if last else hs("nw", h), pm, 0, yp(h, 0, LW), ds(h, 0), a("HI"))
 
     def decide(h, last):
         pm = "PM%d" % h
-        key = a("sf", 16 * AA + NB * h, 16 * AA + NB * (h + 1))
-        tt(sh(1, h), sf(MF, h), sf(THE, h), OP.is_ge)
-        tt(sh(2, h), sf(CC, h), sh(1, h), OP.mult)
-        tt(key, sf(KD, h), sh(1, h), OP.mult)
-        tt(key, key, sf(HK, h), OP.add)
-        ts(su(8, h), key, -0.375, OP.add)
-        tt(hs("kr2", h), ind(a("IO"), su(8, h)), hs("tR", h), OP.add)
-        lin(sf(NB2, h), key, -1.0, -0.375)
-        lin(a("sf", 16 * AA + 12 + NB * h, 16 * AA + 12 + NB * (h + 1)), key, -1.0, float(HK0 - SOFF))
-        mm(a(pm, 0, NB), I, sh(0, h), True, False)
-        for c in range(5):
-            f = (c - NB * h) % 5
-            mm(a(pm, f, NB, 5), a("PERM", 128 * c, 128 * c + 128), a("sh", 32 + NB * h + f, 32 + NB * (h + 1), 5), False, c == 4)
-        cp(su(3, h), a(pm, 0, NB))
-        cp(hs("Zn", h), ind(a("ZC"), su(3, h)), "vs")
-        cp(si(8, h), sf(MF, h))
-        ts(si(9, h), si(8, h), 2047, OP.bitwise_and)
-        cp(su(7, h), si(9, h))
-        cp(hs("ohm", h), ind(a("OH"), su(7, h)), "vs")
-        tt(hs("ohG", h), hs("ohm", h), hs("GB", h), OP.mult)
-        mm(a(pm, 256, 256 + LW), a("BOh"), hs("ohG", h), True, False)
-        mm(a(pm, 256, 256 + LW), a("NIh"), hs("Ph", h), False, True)
-        mm(a(pm, 128, 128 + LW), a("ZIh", 0, 128), a("C2k"), True, False)
-        shift(pm, 128, "ZIh", -1, 0, "Ph", h, True)
-        tt(hs("rr", h), a(pm, 256, 256 + LW), hs("ohj", h), OP.mult)
+        tt(sh(2, h), wide("si", 10, h, NB, 2 * NB), sf(THE, h), OP.is_ge)
+        tt(sh(3, h), sf(CC, h), sh(2, h), OP.mult)
+        tt(sf(KEY, h), sf(U1, h), sh(2, h), OP.mult)
+        tt(sf(KEY, h), sf(KEY, h), wide("si", 8, h, 0, NB), OP.max)
+        cp(su(3, h), sf(KEY, h), SX)
+        cp(hs("kr", h), ind(a("IO"), su(3, h)), SX)
+        mm(a(pm, 400, 400 + 2 * NB), I, wide("sh", 0, h), True, False)
+        for j in range(2):
+            for c in range(5):
+                f = (c - NB * h) % 5
+                mm(a(pm, 400 + NB * j + f, 400 + NB * (j + 1), 5), a("PERM", 128 * c, 128 * c + 128), a("sh", 48 + NB * h + f, 48 + NB * (h + 1), 5),
+                   False, j == 1 and c == 4)
+        cp(wide("su", 8, h), a(pm, 400, 400 + 2 * NB), SX)
+        code = wide("su", 8, h, 0, NB)
+        cp(aim(h, 1), ind(zz(h, ZA, ZA + 3 * CODE), code), "vs")
+        tt(hs("dl", h), ind(a("WK", 3 * CODE * h, 3 * CODE * (h + 1)), code), hs("Kf", h), OP.subtract)
+        cp(hs("To", h), ind(a("TT"), wide("su", 8, h, NB, 2 * NB)), "vs")
+        tt(hs("ohG", h), ind(a("OH"), wide("su", 6, h, NB, 2 * NB)), hs("GB", h), OP.mult)
+        mm(a(pm, 100, 100 + LW), a("NI"), yp(h, 100, 100 + LW), True, False)
+        mm(a(pm, 100, 100 + LW), a("BO"), hs("ohG", h), False, True)
+        tt(hs("rr", h), a(pm, 100, 100 + LW), hs("ohj", h), OP.mult)
         if last:
-            tt(hs("MW", h, LN), hs("rr", h), hs("Pf", h), OP.add)
-        cp(hs("Kp", h), ind(a("KC"), su(3, h)))
-        tt(hs("dPK", h), a(pm, 128, 128 + LW), hs("Kp", h), OP.subtract)
-        cp(hs("To", h), ind(a("TW"), su(3, h)), "vs")
+            tt(msg(h, LW, 2 * LW), hs("rr", h), hs("Pf", h), OP.add)
+        elif str(h) in FUSE:
+            ze = hs("ze", h)
+            for m in range(5):
+                f = (m - LW * h) % 5
+                mm(a(pm, 200 + f, 200 + LW, 5), SH("ZI", 1 + m), zz(h, ZA + f, ZA + LW, 1, 5))
+            cp(ze, a(pm, 200, 200 + LW), "vs")
+            for k in range(16):
+                o = a("zr", BIG * h + k, BIG * (h + 1), 16)
+                o["reg"] = [("zr", BIG * h, BIG * (h + 1), k, k + 1)]
+                gcp(o, ze)
 
     def off(h, last):
-        o = a("PS%d" % h, 4 * LW, 5 * LW)
-        if "H" in FUSE:
-            tt(hs("dl", h), hs("Zn", h), hs("ZC", h), OP.subtract)
+        o = a("PM%d" % h, 300, 300 + LW)
         for kg in range(16 // KG):
-            b = sub("xg", h, kg, hs("dl" if "H" in FUSE else "Zn", h), a("CI"), a("NCI"))
-            if OFFMODE[kg] == "v":
+            b = sub("xg", h, kg, aim(h, 1), a("CI"), a("NCI"))
+            if OFFMODE.split()[h][kg] == "v":
                 ts(big("gt", h, kg), b, MAGIC, OP.add, MAGIC, OP.not_equal)
             else:
                 act(big("ab2", h, kg), b, AF.Abs)
                 ts(big("gt", h, kg), big("ab2", h, kg), 64.0, OP.is_gt)
         for k in range(16):
-            mm(o, WW("ZWp", 0, k), a("gt", BIG * h + k * LW, BIG * h + (k + 1) * LW), k == 0, k == 15)
+            mm(o, WW("ZWp", 0, k), one("gt", LW * h, LW * (h + 1), k), k == 0, k == 15)
         tt(o, o, hs("To", h), OP.is_ge)
-        tt(o, o, hs("dPK", h), OP.mult)
+        tt(o, o, hs("dl", h), OP.mult)
+        tt(hs("Kf", h), o, hs("Kf", h), OP.add)
+        if not last:
+            cp(hs("Ku", h), hs("Kf", h), SX)
+
+    def settle(h, last):
+        ps, terms = "PS%d" % h, []
+        for b in range(NB):
+            e = a("EQ", (NB * h + b) * LW, (NB * h + b) * LW + 16 * (b + 1))
+            ts(e, a("kr", LW * h, LW * h + 16 * (b + 1)), a("sf", 16 * KEY + NB * h + b, 16 * KEY + NB * h + b + 1), OP.is_equal,
+               a("sf", 16 * WGT + b, 16 * WGT + b + 1), OP.mult)
+            terms.append((0, b + 1, a("BO"), e))
+        diag(sf(NN, h), ps, 0, NB, terms, a("MK3"))
+        tt(sf(NN, h), sf(NN, h), sf(DUM, h), OP.min)
         if last:
-            tt(hs("Kf", h), o, hs("Kp", h), OP.add)
+            tt(msg(h, 2 * LW, 2 * LW + NB), sf(NN, h), sf(KEY, h), OP.max)
         else:
-            tt(hs("KC", h, LN), o, hs("Kp", h), OP.add)
-            cp(hs("Ku", h), hs("KC", h, LN))
-            zshift(h)
+            tt(sf(NN, h), sf(NN, h), sf(KEY, h), OP.max)
+            cp(su(10, h), sf(NN, h), SX)
 
-    def settle(last):
-        for b in range(11, -1, -1):
-            o = a("dd", LN * b + 16 * b, LN * (b + 1))
-            act(o, a("kr2", 16 * b, LN), AF.Abs, a("sf", 16 * NB2 + b, 16 * NB2 + b + 1))
-            red(a("sf", 16 * MN + b, 16 * MN + b + 1), o, OP.min)
-        for j in range(2):
-            ts(a("sf", 16 * PEN + 12 * j, 16 * PEN + 12 * j + 12), sf(MN), 0.375, OP.is_lt, 8192.0, OP.mult)
-        r24 = a("sf", 16 * RR, 16 * RR + 24)
-        tt(r24, a("sf", 16 * AA, 16 * AA + 24), a("sf", 16 * PEN, 16 * PEN + 24), OP.add)
-        tt(a("MW", 2 * LN, 2 * LN + 24) if last else r24, r24, a("sf", 16 * BB, 16 * BB + 24), OP.min)
+    def write(h, last):
+        if not last:
+            cp(ind(a("X"), su(10, h)), hs("nw", h))
+            tt(ind(a("S"), su(10, h)), hs("rr", h), hs("Pf", h), OP.add)
+
+    def carry(last):
+        for h in range(NH):
+            ts(sf(CON, h), wide("su", 8, h, 0, NB), float(2 * CODE), OP.is_ge)
+            tt(wide("sh", 0, h, NB, 2 * NB), wide("sh", 0, h, NB, 2 * NB), sf(CON, h), OP.add)
         if last:
-            thresholds(True, True)
+            for h in range(NH):
+                cp(su(1, h), wide("sh", 0, h, NB, 2 * NB))
+            cp(a("Lr"), ind(a("TB2"), su(1)), "vs")
             return
-        ts(su(10), a("sf", 16 * RR, 16 * RR + 12), -0.375, OP.add)
-        ts(su(11), a("sf", 16 * RR + 12, 16 * RR + 24), -1.0, OP.mult, -0.375, OP.add)
-        cp(ind(a("X"), su(10)), a("nw"))
-        tt(ind(a("S"), su(11)), a("rr"), a("Pf"), OP.add)
-        thresholds(True, False)
-        mm(a("PM0", 400, 412), a("BO"), sh(1))
-        red(a("sf", 16 * CNT, 16 * CNT + 1), a("PM0", 400, 412), OP.add)
-        tt(a("si", 16 * 11, 16 * 11 + 1), a("si", 16 * 11, 16 * 11 + 1), a("sf", 16 * CNT, 16 * CNT + 1), OP.subtract)
-        ts(a("si", 16 * 11 + 4, 16 * 11 + 5), a("si", 16 * 11, 16 * 11 + 1), 31, OP.bitwise_and)
-        ts(col(AM), a("si", 16 * 11 + 4, 16 * 11 + 5), 2048.0, OP.mult, 2048.0, OP.add)
+        lin(sf(CON), sf(CON), -0.5, 1.0)
+        tt(sf(THR), sf(THR), sf(CON), OP.mult)
+        ts(sf(CON), sf(THR), 1.5, OP.is_lt, 65535.0, OP.mult)
+        tt(sf(THR), sf(THR), sf(CON), OP.add)
+        bounds()
+        mm(a("PM1", 112, 124), a("BO"), sh(2))
+        red(a("sf", 16 * CNT, 16 * CNT + 1), a("PM1", 112, 124), OP.add)
+        tt(a("si", 0, 1), a("si", 0, 1), a("sf", 16 * CNT, 16 * CNT + 1), OP.subtract)
+        ts(a("si", 4, 5), a("si", 0, 1), 31, OP.bitwise_and)
+        lin(col(AM), a("si", 4, 5), 2048.0, 1024.0, SX)
 
-    steps = {"H": home, "B": lambda h, last: look(h, 0), "C": lambda h, last: look(h, 1), "P": partner, "D": decide, "O": off}
-    for rnd in range(RO):
-        last = rnd == RO - 1
+    steps = {"H": home, "B": lambda h, last: look(h, 0), "C": lambda h, last: look(h, 1), "P": partner, "D": decide, "O": off,
+             "S": settle, "W": write}
+    for r in range(RO):
+        rnd[0] = r
+        last = r == RO - 1
         if last:
-            n1, n2 = stage("N", sbs("X", 0, W))
-            s1, s2 = stage("S", sbs("S", SOFF, SOFF + A))
+            n1, n2 = stage("N", sbs("X", X0, X0 + W))
+            s1, s2 = stage("S", sbs("S", 0, A))
             dma("y", n1, 2 ** 20)
             dma("y", s1, 2 ** 20)
             dma("y", n2 + s2, 2 ** 20)
             exchange(["N"], 2 ** 20)
             exchange(["S"], 2 ** 20)
-            dma("y", [(a("XN", 0, W), land("N"))], 2 ** 20)
-            dma("y", [(a("SN", SOFF, SOFF + A), land("S"))], 2 ** 20)
+            dma("y", [(a("XN", X0, X0 + W), land("N"))], 2 ** 20)
+            dma("y", [(a("SN", 0, A), land("S"))], 2 ** 20)
         for w in ORDER.split():
-            stg[0] += 1
+            stg[0], stg[1] = stg[0] + 1, w
+            seen.clear()
             steps[w[0]](int(w[1]), last)
-        settle(last)
+        stg[1] = "R"
+        carry(last)
 
-    w1, w2 = stage("W", sbs("MW", 0, 408))
+    w1, w2 = stage("W", sbs("MW", 0, NH * MWH))
     dma("y", w1, 2e5)
     dma("y", w2, 2e5)
     exchange(["W"], 2e5)
     k1, k2 = stage("K", sbs("Kf", 0, LN))
-    z1, z2 = stage("L", sbs("Zn", 0, LN), 0, 64)
+    z1, z2 = stage("L", sbs("Zf", 0, LN), 0, 64)
     l1, l2 = stage("L", sbs("Lr", 0, LN), 64, 128)
     dma("s", k1 + z1 + l1, 2e5)
     dma("s", k2 + z2 + l2, 2e5)
     exchange(["K", "L"], 2e5)
     dma("y", [(a("MO"), land("W"))], 2e5)
-    ts(su(10), a("MO", 2 * LN, 2 * LN + 12), -0.375, OP.add)
-    ts(su(11), a("MO", 2 * LN + 12, 2 * LN + 24), -1.0, OP.mult, -0.375, OP.add)
-    cp(ind(a("XN"), su(10)), a("MO", 0, LN))
-    dma("y", [(d(T.yx[:], None), a("XN", 0, W))], 2 ** 20)
-    cp(ind(a("SN"), su(11)), a("MO", LN, 2 * LN))
-    dma("s", [(d(T.ya[:], None), a("SN", SOFF, SOFF + A))], 2 ** 20)
+    for h in range(NH):
+        cp(su(10, h), a("MO", MWH * h + 2 * LW, MWH * h + 2 * LW + NB))
+    for h in range(NH):
+        cp(ind(a("XN"), su(10, h)), a("MO", MWH * h, MWH * h + LW))
+    dma("y", [(d(T.yx[:], None), a("XN", X0, X0 + W))], 2 ** 20)
+    for h in range(NH):
+        cp(ind(a("SN"), su(10, h)), a("MO", MWH * h + LW, MWH * h + 2 * LW))
+    dma("s", [(d(T.ya[:], None), a("SN", 0, A))], 2 ** 20)
     dma("s", [(d(T.yk[:], None), land("K")), (d(T.yz[:], None), land("L", 0, 64))], 2e5)
     dma("g", [(d(T.yl[:], None), land("L", 64, 68))], 1e4)
     return ops, Q
@@ -679,7 +770,9 @@ def depend(ops):
         dp, od = set(), set()
         eng = list(o["alts"])[0] if len(o["alts"]) == 1 else i
         for wr, regs in ((0, o["r"]), (1, o["w"])):
-            for n, c0, c1 in regs:
+            for n, r0, r1, c0, c1 in regs:
+                if n == "zr" and not wr:
+                    c0, c1 = 0, 16
                 if n in SCRATCH and SCRATCH[n][0] == "psum":
                     st = banks.setdefault(n, [None, [], []])
                     if st[0] != eng:
@@ -688,14 +781,14 @@ def depend(ops):
                     if eng == "p":
                         od.update(x[0] for x in st[1][-1:])
                     else:
-                        dp.update(x[0] for x in st[1] if (wr or x[3]) and x[1] < c1 and c0 < x[2])
-                    st[1].append((i, c0, c1, wr))
+                        dp.update(x[0] for x in st[1] if (wr or x[5]) and x[1] < r1 and r0 < x[2] and x[3] < c1 and c0 < x[4])
+                    st[1].append((i, r0, r1, c0, c1, wr))
                     continue
                 lst = recs.setdefault(n, [])
-                dp.update(x[0] for x in lst if (wr or x[3]) and x[1] < c1 and c0 < x[2])
+                dp.update(x[0] for x in lst if (wr or x[5]) and x[1] < r1 and r0 < x[2] and x[3] < c1 and c0 < x[4])
                 if wr:
-                    lst[:] = [x for x in lst if not (c0 <= x[1] and x[2] <= c1)]
-                lst.append((i, c0, c1, wr))
+                    lst[:] = [x for x in lst if not (r0 <= x[1] and x[2] <= r1 and c0 <= x[3] and x[4] <= c1)]
+                lst.append((i, r0, r1, c0, c1, wr))
         dp.discard(i)
         od.discard(i)
         if "after" in o:
@@ -703,55 +796,72 @@ def depend(ops):
         o["dp"], o["od"] = dp, od - dp
 
 
+def place(ops, seq, pre, keep=None):
+    gaps = {}
+    t0, c0, eng = [0.0] * len(ops), [0.0] * len(ops), [None] * len(ops)
+    for i in seq:
+        t = max([t0[j] + c0[j] + w for j, w in pre[i]] + [0.0])
+        best = None
+        for e, al in ops[i]["alts"].items():
+            if keep[i] and keep[i] != e:
+                continue
+            s, c = gaps.setdefault(e, []), al[0]
+            lo, hi = 0, len(s)
+            while lo < hi:
+                mid = (lo + hi) // 2
+                if s[mid][1] <= t:
+                    lo = mid + 1
+                else:
+                    hi = mid
+            x = t
+            while lo < len(s) and s[lo][0] < x + c:
+                x = max(x, s[lo][1])
+                lo += 1
+            v = x + c * (VB if e == "v" else 1)
+            if best is None or v < best[0]:
+                best = (v, e, x, c, lo)
+        if best:
+            _, eng[i], t, c0[i], k = best
+            gaps[eng[i]].insert(k, (t, t + c0[i]))
+        t0[i] = t
+    return t0, c0, eng
+
+
+def ordered(keys, pre):
+    keys = list(keys)
+    for i in pre:
+        for j, w in pre[i]:
+            keys[i] = max(keys[i], keys[j])
+    pos = {i: k for k, i in enumerate(pre)}
+    return sorted(pre, key=lambda i: (keys[i], pos[i]))
+
+
 def schedule(ops):
     n = len(ops)
-    succ = [[] for _ in range(n)]
-    left = [0] * n
+    if REPORT.get("n") != n:
+        pre, post = {i: [] for i in range(n)}, {i: [] for i in range(n - 1, -1, -1)}
+        for i, o in enumerate(ops):
+            for j, w in [(j, HOP + ops[j].get("lat", 0)) for j in o["dp"]] + [(j, 0.0) for j in o["od"]]:
+                pre[i].append((j, w))
+                post[j].append((i, w))
+        prio = [0.0] * n
+        for i in post:
+            c = min([x[0] for x in ops[i]["alts"].values()] or [0])
+            prio[i] = c + max([prio[j] + w for j, w in post[i]] + [ops[i].get("lat", 0)])
+        seq, best = ordered([LAM * o["st"] + LATE.get(o["tag"], 0.0) - prio[i] for i, o in enumerate(ops)], pre), None
+        fix = [("s" if o["name"] in ONS else "v") if "name" in o and ONS is not None else None for o in ops]
+        for _ in range(PASSES):
+            t0, c0, eng = place(ops, seq, pre, fix)
+            end = max(t0[i] + c0[i] + ops[i].get("lat", 0) for i in range(n))
+            if best is None or end < best[0]:
+                best = (end, t0, c0, eng)
+            b0, d0, _e = place(ops, ordered([-t0[i] - c0[i] for i in range(n)], post), post, eng)
+            seq = ordered([-b0[i] - d0[i] for i in range(n)], pre)
+        REPORT.update(n=n, best=best, order=ordered(best[1], pre))
+    end, t0, c0, eng = REPORT["best"]
     for i, o in enumerate(ops):
-        for j in o["dp"] | o["od"]:
-            succ[j].append(i)
-            left[i] += 1
-    prio = [0.0] * n
-    for i in range(n - 1, -1, -1):
-        o = ops[i]
-        c = min([x[0] for x in o["alts"].values()] or [0]) + o.get("lat", 0)
-        prio[i] = c + max([prio[j] + (HOP if i in ops[j]["dp"] else 0) for j in succ[i]] or [0])
-    x = SEED
-    for i in range(n):
-        x = (x * 1103515245 + 12345) % 2147483648
-        prio[i] += NOISE * (x / 2147483648.0) - LAM * ops[i]["st"]
-    free = {"v": 0.0, "s": 0.0, "p": 0.0, "g": 0.0, "y": 0.0}
-    busy = dict(free)
-    issue, done, rdy, order = [0.0] * n, [0.0] * n, {}, []
-    for i in range(n):
-        if left[i] == 0:
-            rdy[i] = 0.0
-    while rdy:
-        cand = []
-        for i, t in rdy.items():
-            al = ops[i]["alts"]
-            if not al:
-                cand.append((-1.0, i, None))
-                continue
-            e = min(al, key=lambda q: max(t, free[q]) + al[q][0] * (VB if q == "v" else 1))
-            cand.append((max(t, free[e]), i, e))
-        t0 = min(c[0] for c in cand)
-        t, i, e = max((c for c in cand if c[0] <= t0 + 1.0), key=lambda c: prio[c[1]])
-        o = ops[i]
-        t = max(t, rdy.pop(i))
-        c = o["alts"][e][0] if e else 0.0
-        if e:
-            free[e] = t + c
-            busy[e] += c
-        o["e"], o["t"] = e, t
-        issue[i], done[i] = t + c, t + c + o.get("lat", 0)
-        order.append(i)
-        for j in succ[i]:
-            left[j] -= 1
-            if left[j] == 0:
-                rdy[j] = max([done[k] + HOP for k in ops[j]["dp"]] + [issue[k] for k in ops[j]["od"]])
-    REPORT.update(end=max(done), busy=busy, ops=ops)
-    return order, succ
+        o["e"], o["t"] = eng[i], t0[i]
+    return REPORT["order"]
 
 
 def rank_program(g, core, T, topo):
@@ -759,7 +869,8 @@ def rank_program(g, core, T, topo):
         return
     ops, Q = build(g, core, T, topo)
     depend(ops)
-    order, succ = schedule(ops)
+    order = schedule(ops)
+    needed = set(j for o in ops for j in o["dp"])
     count, final = {}, {}
     known = {q: {} for q in Q}
     for i in order:
@@ -783,7 +894,7 @@ def rank_program(g, core, T, topo):
         if "sem" in o:
             o["tok"] = o["sem"]
             final[o["sem"][0]] = o["sem"][1]
-        elif any(i in ops[j]["dp"] for j in succ[i]):
+        elif i in needed:
             s = ESEM[e]
             count[s] = count.get(s, 0) + 1
             ins.then_inc(T.sem[s], 1)

@@ -3,9 +3,7 @@ from concourse.mybir import AluOpType as OP, AxisListType, ActivationFunctionTyp
 
 N, W, A, LN, RO = 8, 4096, 1024, 192, 4
 NH = 2
-LW = LN // NH
-NB = LW // 16
-BIG = 16 * LW
+SPLIT = 96
 KG = 4
 XCH = 2
 X0 = A
@@ -13,53 +11,50 @@ KCON = X0 + W
 KDUM = KCON + 16
 NK = KDUM + LN
 CODE = 128
-ZA, UA = 160, 60
-MWH = 200
-MUH = 304
-MAGIC = 1.5 * 2.0 ** 30
+GAP = 100
+ZA = 160
+MUH = 400
 ROUND = 1.5 * 2.0 ** 23
-CS = 1.578125
 FAR = 2.0 ** 60
 H16 = "float16"
-ORDER = "H0 H1 B0 C0 P0 D0 B1 C1 P1 S0 O0 D1 S1 W0 W1 O1"
-OFFMODE = "ssss ssss"
-GENG = "xxx xxx xxx xxx xxx xxx"
-LEVEL = "vv vv"
-FUSE = ""
+ORDER = "H0 H1 B0 C0 P0 D0 B1 C1 P1 S0 O0 K0 D1 S1 W0 W1 O1 K1"
+OFFMODE = "ssss vvvv"
+FUSE = "B0 B1"
+PIECE = 32
 HOMEH = False
-VSUM, PJSUM = False, False
-ONS = None
-LATE = {'W0': -1500, 'D0': -500, 'C1': -1000, 'P0': 2000, 'S0': 4000, 'B0': -2000, 'W1': 2000, 'O1': -500, 'R': -500, 'B1': 500, 'C0': -1000, 'D1': -1000, 'O0': 1000}
-SPARE = False
-SX = "vs"
-CY, PCY, FIX, HOP, GCY, SCY, SA = 0.83, 0.42, 55.0, 130.0, 1.3, 3.2, 60.0
-VB, LAM, PASSES = 1.4, 1000.0, 2
+LATE = {'W0': -1000, 'D0': -6500, 'P0': 2000, 'S0': 6000, 'B0': -2000, 'R': -4500, 'C0': -4500, 'D1': 500, 'O0': 3000, 'H0': -2000, 'P1': -1000,
+        'S1': -1000, 'B0yB': -2000, 'H0sf': 1000, 'P0sf': 1000, 'H0PD': 2500, 'H1fi': 1000, 'H1PS': -2000, 'C1yC': -1000, 'B0su': 500,
+        'H1si': -2000, 'C0PS': 2500, 'B1mB': -1000, 'B1PB': -2000, 'H0vi': 1000, 'C1PB': -2000, 'H1su': 1000, 'O0gt': 500, 'S1su': 2000,
+        'RLr': 1000, 'H1Ds': -2000, 'O1PB': -2000, 'B0PB': 2000, 'H0st': -2000, 'B1PS': 2500, 'B0PS': -500, 'C0yC': 1000, 'D1su': -1000, 'P0oh': 1000, 'H1dx': 2000, 'C0mC': 500,
+        'P0ZZ': 1000, 'B1aB': -1000, 'C1si': 2000, 'D1PM': 1000, 'P0PM': -1000, 'H0PM': -2000, 'H0ZZ': 2000, 'H0PB': -2000, 'H1xh': -2000}
+RUN = 320.0
+CY, PCY, FIX, HOP, NEAR, GCY, SCY, SA = 0.83, 0.5, 55.0, 175.0, 165.0, 1.35, 3.2, 10.0
+VB, LAM, PASSES = 1.8, 1000.0, 4
 
 
 def _sb(n, d):
     return ("sbuf", [128, n], d)
 
 
-SCRATCH = {"CK": _sb(LW, H16), "X": _sb(NK, "bfloat16"), "S": _sb(NK, "float32"), "Si": _sb(A, "int32"),
-           "XN": _sb(NK, "bfloat16"), "SN": _sb(NK, "float32"), "MW": _sb(NH * MWH, "float32"), "MO": _sb(NH * MWH, "float32"),
-           "WK": _sb(NH * 3 * CODE, "int32"), "TT": _sb(3 * CODE, "float32"), "PGu": _sb(2 * LN, "uint16"),
-           "Ds": _sb(NH * 400, "bfloat16"), "Ku": _sb(LN, "uint16"), "YP": _sb(NH * 304, H16),
-           "sf": _sb(16 * 24, "float32"), "si": _sb(16 * 16, "int32"), "su": _sb(16 * 16, "uint16"), "sh": _sb(16 * 4, "bfloat16"),
+SCRATCH = {"CK": _sb(CODE, H16), "X": _sb(NK, "bfloat16"), "S": _sb(NK, "float32"), "Si": _sb(A, "int32"),
+           "XN": _sb(NK, "bfloat16"), "SN": _sb(NK, "float32"), "MW": _sb(400, "float32"), "MO": _sb(400, "float32"),
+           "WK": _sb(NH * 3 * CODE, "int32"), "C2k": _sb(2 * GAP, "bfloat16"), "PGu": _sb(2 * LN, "uint16"),
+           "Ds": _sb(NH * 2 * GAP, "bfloat16"), "Ku": _sb(LN, "uint16"), "YP": _sb(NH * 3 * GAP, H16),
+           "sf": _sb(16 * 16, "float32"), "si": _sb(16 * 16, "int32"), "su": _sb(16 * 16, "uint16"), "sh": _sb(16 * 4, "bfloat16"),
            "cI": _sb(16, "int32"), "col": _sb(32, "float32"), "coli": _sb(16, "int32"), "PERM": _sb(5 * 128, "bfloat16"),
-           "OH": _sb(BIG, "bfloat16"), "IO": _sb(KDUM, "float32"), "MK": _sb(3 * LW, "bfloat16"), "MK2": _sb(LW, "bfloat16"),
-           "MK3": _sb(LW, "bfloat16"), "kr": _sb(LN, "uint16"), "EQ": _sb(NH * NB * LW, "bfloat16"), "PW": _sb(LW, "float32"),
-           "MU": _sb(NH * MUH, H16), "MI": _sb(NH * MUH, H16)}
-for _names, _n, _d in (("xg xh yB yC zr", 16 * LN, "bfloat16"), ("ZZ00 ZZ01 ZZ10 ZZ11", ZA + 3 * CODE, "bfloat16"),
-                       ("Zi Zf D thrR ohj nw fit Lb Lr ze", LN, "bfloat16"), ("Ki vi Li", LN, "int32"), ("ohP ohG GB", LN, H16),
+           "OH": _sb(16 * CODE, "bfloat16"), "IO": _sb(KDUM, "float32"), "MK": _sb(3 * CODE, "bfloat16"),
+           "kr": _sb(LN, "uint16"), "EQ": _sb(12 * CODE, "bfloat16"), "MU": _sb(NH * MUH, H16), "MI": _sb(NH * MUH, H16)}
+for _names, _n, _d in (("xg xh yB yC zrB zrC", 16 * LN, "bfloat16"), ("zeB zeC", LN, "bfloat16"), ("ZZ00 ZZ01 ZZ10 ZZ11", ZA + 3 * CODE, "bfloat16"),
+                       ("Zi Zf D thrR ohj nw fit Lb Lr", LN, "bfloat16"), ("Ki vi Li", LN, "int32"), ("ohP ohG GB", LN, H16),
                        ("K20 thrK To Pf rr dl Kf", LN, "float32"), ("cJ c1 c2", 256, "float32"),
-                       ("ZI ZW1 ZWd ZWp ZW2 ZWt ZWw Z8", 256, "bfloat16"), ("NI CI NCI HI NF BO BOw", 128, "bfloat16"),
-                       ("CQ", LW, "bfloat16"), ("C3k", NB, "bfloat16"), ("TBL TB2", 32, "float32")):
+                       ("ZI ZW1 ZWd ZWp ZWq ZW2 Z8 NI BOw", 256, "bfloat16"), ("HI NF BO B4 B16 B2k CQ MK2 MK3", 128, "bfloat16"),
+                       ("B5", 128, H16), ("TBL TB2 TT", 32, "float32"), ("PW", SPLIT, "float32")):
     for _x in _names.split():
         SCRATCH[_x] = _sb(_n, _d)
 for _x in "dx gt aB mB aC mC ab2".split():
     SCRATCH[_x] = ("sbuf", [128, LN, 16], "bfloat16")
 for _x, _n, _d in [("I", 24, "int32"), ("Z", 24, "bfloat16"), ("A", 128, "int32"), ("N", 512, "bfloat16"), ("S", 128, "float32"),
-                   ("W", NH * MWH // N, "float32"), ("K", 24, "float32"), ("L", 48, "bfloat16"), ("U0", MUH // N, H16), ("U1", MUH // N, H16),
+                   ("W0", 200 // N, "float32"), ("W1", 200 // N, "float32"), ("K", 24, "float32"), ("L", 48, "bfloat16"), ("U0", MUH // N, H16), ("U1", MUH // N, H16),
                    ("G", 2 * LN, "bfloat16")] + [("X%d" % _c, 512 // XCH, "bfloat16") for _c in range(XCH)]:
     SCRATCH["st" + _x] = ("dram", [N, 128, _n], _d)
     SCRATCH["ld" + _x] = ("dram", [N, 128, _n], _d)
@@ -72,7 +67,7 @@ for _b in ("PS0", "PS1"):
 for _b in ("PD", "PM0", "PM1"):
     SCRATCH[_b] = ("psum", [128, 512], "float32")
 ALL = dict(SCRATCH)
-for _x in (("stI ldI stZ ldZ stP ldP" if HOMEH else "stU0 ldU0 stU1 ldU1 stG ldG MI xh") + ("" if FUSE else " zr ze")).split():
+for _x in ("stI ldI stZ ldZ stP ldP" if HOMEH else "stU0 ldU0 stU1 ldU1 stG ldG MI MU xh").split():
     del SCRATCH[_x]
 SEMAPHORES = ["ev", "es", "ep", "eg"] + ["d%d" % _i for _i in range(48)] + ["r%d" % _i for _i in range(12)] + ["l%d" % _i for _i in range(12)]
 ESEM = {"v": "ev", "s": "es", "p": "ep", "g": "eg"}
@@ -81,8 +76,13 @@ REPORT = {}
 
 def build(g, core, T, topo):
     rank = T.rank_of(core)
-    ops, stg, seen = [], [0, ""], {}
+    ops, stg, cut, rnd = [], [0, ""], [0], [0]
     Q = {"v": g.vector, "s": g.scalar, "p": g.tensor, "g": g, "y": g.sync}
+    T0, T1 = [0, SPLIT], [SPLIT, LN]
+    LW = [T1[h] - T0[h] for h in range(NH)]
+    NB = [n // 16 for n in LW]
+    B0 = [n // 16 for n in T0]
+    M0 = [0, 2 * SPLIT + 8]
 
     def dt(n):
         return SCRATCH[n][2]
@@ -110,16 +110,19 @@ def build(g, core, T, topo):
         return x["ap"] if isinstance(x, dict) else x
 
     def add(alts, outs, ins, **k):
-        if len(alts) > 1:
-            name = stg[1] + outs[0]["nm"]
-            seen[name] = seen.get(name, -1) + 1
-            name += str(seen[name])
-            k["name"] = name
-        k["tag"] = stg[1]
         rd = [r for x in ins if isinstance(x, dict) for r in x["reg"] + x.get("xr", [])] + [r for x in outs for r in x.get("xr", [])]
-        o = {"alts": alts, "w": [r for x in outs for r in x["reg"]], "r": rd, "st": stg[0],
+        o = {"alts": alts, "w": [r for x in outs for r in x["reg"]], "r": rd, "st": stg[0], "tag": stg[1],
+             "sub": stg[1] + (outs[0]["nm"] or "" if outs else "")[:2],
              "gn": sum(x["n"] for x in ins if isinstance(x, dict) and "ind" in x), "sn": sum(x["n"] for x in outs if "ind" in x)}
         o.update(k)
+        p = ops[-1] if ops else o
+        if "run" in o and p.get("run") == o["run"] and p["st"] == o["st"]:
+            e = o["run"][0]
+            (c0, f0), (c1, f1) = p["alts"][e], alts[e]
+            if c0 + c1 <= RUN:
+                p["alts"] = {e: (c0 + c1, lambda: f0() + f1())}
+                p["w"], p["r"] = p["w"] + o["w"], p["r"] + o["r"]
+                return len(ops) - 1
         ops.append(o)
         return len(ops) - 1
 
@@ -136,9 +139,9 @@ def build(g, core, T, topo):
     def scost(out, in0):
         return vcost(out, in0, 1) + (15 if "ind" in in0 else SA)
 
-    def tt(out, i0, i1, op):
+    def tt(out, i0, i1, op, **k):
         ps = SCRATCH[i0["nm"]][0] == "psum" or SCRATCH[i1["nm"]][0] == "psum"
-        add({"v": (vcost(out, i0, 1 if ps else 2), lambda: g.vector.tensor_tensor(out["ap"], i0["ap"], i1["ap"], op))}, [out], [i0, i1])
+        add({"v": (vcost(out, i0, 1 if ps else 2), lambda: [g.vector.tensor_tensor(out["ap"], i0["ap"], i1["ap"], op)])}, [out], [i0, i1], **k)
 
     def ts(out, i0, s1, op0, s2=None, op1=None):
         if s2 is None:
@@ -147,24 +150,18 @@ def build(g, core, T, topo):
             f = lambda: g.vector.tensor_scalar(out["ap"], i0["ap"], val(s1), val(s2), op0, op1)
         add({"v": (vcost(out, i0, 0.5 if two(out, i0) else 1), f)}, [out], [i0, s1, s2])
 
-    def cp(out, i0, eng="v"):
-        alts = {}
-        if "v" in eng:
-            alts["v"] = (vcost(out, i0, 0.5 if two(out, i0) else 1), lambda: g.vector.tensor_copy(out["ap"], i0["ap"]))
+    def cp(out, i0, eng="vs"):
+        alts = {"v": (vcost(out, i0, 0.5 if two(out, i0) else 1), lambda: g.vector.tensor_copy(out["ap"], i0["ap"]))}
         if "s" in eng:
             alts["s"] = (scost(out, i0), lambda: g.scalar.activation(out["ap"], i0["ap"], AF.Copy))
         add(alts, [out], [i0])
 
-    def act(out, i0, fn):
-        add({"s": (scost(out, i0), lambda: g.scalar.activation(out["ap"], i0["ap"], fn))}, [out], [i0])
+    def act(out, i0, fn, bias=0.0):
+        add({"s": (scost(out, i0), lambda: g.scalar.activation(out["ap"], i0["ap"], fn, bias=val(bias)))}, [out], [i0, bias])
 
-    def lin(out, i0, sc, bi, eng="vs"):
-        alts = {}
-        if "v" in eng:
-            alts["v"] = (vcost(out, i0, 0.5 if two(out, i0) else 1), lambda: g.vector.tensor_scalar(out["ap"], i0["ap"], sc, val(bi), OP.mult, OP.add))
-        if "s" in eng:
-            alts["s"] = (scost(out, i0), lambda: g.scalar.activation(out["ap"], i0["ap"], AF.Identity, bias=val(bi), scale=sc))
-        add(alts, [out], [i0, bi])
+    def lin(out, i0, sc, bi):
+        add({"v": (vcost(out, i0, 0.5 if two(out, i0) else 1), lambda: g.vector.tensor_scalar(out["ap"], i0["ap"], sc, val(bi), OP.mult, OP.add)),
+             "s": (scost(out, i0), lambda: g.scalar.activation(out["ap"], i0["ap"], AF.Identity, bias=val(bi), scale=sc))}, [out], [i0, bi])
 
     def red(out, i0, op):
         add({"v": (vcost(out, i0, 1), lambda: g.vector.tensor_reduce(out["ap"], i0["ap"], AxisListType.X, op))}, [out], [i0])
@@ -176,7 +173,7 @@ def build(g, core, T, topo):
         add({"v": (vcost(out, out, 0.5 if two(out) else 1), lambda: g.vector.memset(out["ap"], v))}, [out], [])
 
     def mm(out, l, r, st=True, sp=True):
-        add({"p": (max(64, r["n"]) * PCY, lambda: g.tensor.matmul(out["ap"], l["ap"], r["ap"], st, sp))}, [out], [l, r])
+        add({"p": (max(64, r["n"]) * PCY, lambda: [g.tensor.matmul(out["ap"], l["ap"], r["ap"], st, sp)])}, [out], [l, r], run=("p", out["nm"], cut[0]))
 
     def iota(out, pat, base, cm, **k):
         if dt(out["nm"]) == "int32":
@@ -184,9 +181,6 @@ def build(g, core, T, topo):
         else:
             f = lambda: g.iota(out["ap"], pat, base, cm, allow_small_or_imprecise_dtypes=True)
         add({"g": (130 + 2 * CY * out["n"], f)}, [out], [], **k)
-
-    def gcp(out, i0):
-        add({"g": (170 + 2 * CY * i0["n"], lambda: g.affine_select(out["ap"], i0["ap"], [[0, i0["n"]]], OP.is_ge, 0.0, 1, 0))}, [out], [i0])
 
     nd = [0]
 
@@ -255,13 +249,13 @@ def build(g, core, T, topo):
         for c in range(XCH):
             prev = dma("y", xs[c][0] + xs[c][1], 2 ** 20 + 2 ** 20 / XCH * (c + 1), after=prev)
         prev = dma("y", a1 + a2, 2.5 * 2 ** 20, after=prev)
-        sent = exchange(["X0"], 2 ** 20 / XCH)
+        sent = exchange(["X0"], 2 ** 19)
         for c in range(1, XCH):
-            sent = exchange(["X%d" % c], 2 ** 20 / XCH, after=sent)
+            sent = exchange(["X%d" % c], 2 ** 19, after=sent)
         sent = exchange(["A"], 2 ** 19, after=sent)
         for c in range(XCH):
             prev = dma("y", [(a("X", X0 + c * xw, X0 + (c + 1) * xw), land("X%d" % c))], 2 ** 20 / XCH, after=prev)
-        dma("y", [(a("Si"), land("A"))], 2 ** 19, after=prev)
+        landed = dma("y", [(a("Si"), land("A"))], 2 ** 19, after=prev)
     else:
         k1, k2 = stage("I", inp(T.kw, 0, LN))
         l1, l2 = [(d(T.stP[:], "stP"), d(T.l0[:], None))], [(d(T.ldP[rank], "ldP"), d(T.l0[:], None))]
@@ -275,9 +269,9 @@ def build(g, core, T, topo):
         for c in range(XCH):
             ps_ = dma("s", xs[c][1], 2 ** 20, after=ps_)
         sent = exchange(["I"], 1e5)
-        sent = exchange(["Z", "P"], 1e5, after=sent)
         for c in range(XCH):
             sent = exchange(["X%d" % c], 2 ** 20 / XCH, after=sent)
+        sent = exchange(["Z", "P"], 1e5, after=sent)
         dma("s", a1 + a2, 2 ** 19, "stX0")
         sent = exchange(["A"], 2 ** 19, after=sent)
         dma("y", [(a("Ki"), land("I"))], 1e5)
@@ -291,19 +285,18 @@ def build(g, core, T, topo):
         return a("col", i, i + 1)
 
     def small(buf):
-        return lambda i, h=None: a(buf, 16 * i, 16 * i + 12) if h is None else a(buf, 16 * i + NB * h, 16 * i + NB * (h + 1))
+        return lambda i, h=None: a(buf, 16 * i, 16 * i + 12) if h is None else a(buf, 16 * i + B0[h], 16 * i + B0[h] + NB[h])
     sf, si, su, sh = small("sf"), small("si"), small("su"), small("sh")
 
-    def wide(buf, i, h, c0=0, c1=2 * NB):
-        return a(buf, 16 * (i + h) + c0, 16 * (i + h) + c1)
-    PID, CI_, CQ16, CW, CPW, CQ128, CI16, AM, CP128, CZ8, CUP, PC = 0, 1, 2, 3, 4, 5, 6, 7, 8, 9, 10, 16
+    def wide(buf, i, h, j0, j1, per=1):
+        return a(buf, 16 * (i + per * h) + j0 * NB[h], 16 * (i + per * h) + j1 * NB[h])
+    PID, CI_, CQ16, CW, CPW, CI16, AM, CP128, CZ8, CUP, C40, CPQ, PC = 0, 1, 2, 3, 4, 6, 7, 8, 9, 10, 11, 12, 16
     iota(a("coli", 0, 1), [[0, 1]], 0, 1)
     iota(a("cJ"), [[1, 256]], 0, 0)
-    cp(col(PID), a("coli", 0, 1))
+    cp(col(PID), a("coli", 0, 1), "v")
     ts(a("coli", 1, 2), a("coli", 0, 1), 15, OP.bitwise_and)
-    cp(col(CI_), a("coli", 1, 2))
+    cp(col(CI_), a("coli", 1, 2), "v")
     tt(col(CQ16), col(PID), col(CI_), OP.subtract)
-    ts(col(CQ128), col(CQ16), 128.0, OP.add)
     ts(col(CP128), col(PID), 128.0, OP.add)
     ts(col(CW), col(CI_), 15.0, OP.mult, 7.0, OP.add)
     ts(col(CI16), col(CI_), 16.0, OP.mult)
@@ -313,35 +306,45 @@ def build(g, core, T, topo):
         ts(a("ZI", 128 * c, 128 * c + 128), a("cJ", 0, 128), col(PID), OP.is_equal)
         ts(a("ZW1", 128 * c, 128 * c + 128), a("cJ", 0, 128), col(CQ16), OP.is_equal)
     I = a("ZI", 0, 128)
-    for n, v in (("NI", -1.0), ("HI", 0.5), ("CI", CS), ("NCI", -CS), ("NF", -2.0 ** 23)):
+    ts(a("NI"), a("ZI"), -1.0, OP.mult)
+    NI = a("NI", 0, 128)
+    for n, v in (("HI", 0.5), ("NF", -2.0 ** 23)):
         ts(a(n), I, v, OP.mult)
     mset(a("CQ"), -0.25)
-    mset(a("C3k"), 2048.0 + X0)
-    mset(a("c1", 0, LW), 2.0)
-    mset(a("c2", 0, LW), 0.0)
-    scan(a("PW"), a("c1", 0, LW), a("c2", 0, LW), 2.0 ** 12, OP.mult, OP.add)
+    ts(a("OH", 0, 16), a("cJ", 0, 16), col(CI_), OP.is_equal)
+    mset(a("c1", 0, SPLIT), 2.0)
+    mset(a("c2", 0, SPLIT), 0.0)
+    scan(a("PW"), a("c1", 0, SPLIT), a("c2", 0, SPLIT), 2.0 ** 12, OP.mult, OP.add)
     mset(a("c1", 128, 144), 0.5)
     scan(a("TBL", 0, 16), a("c1", 128, 144), a("c2", 0, 16), 131072.0, OP.mult, OP.add)
-    cp(a("TBL", 16, 32), a("TBL", 0, 16))
-    cp(a("TB2", 0, 16), a("cJ", 0, 16))
-    cp(a("TB2", 16, 32), a("cJ", 0, 16))
-    mset(a("TT", 0, CODE), -1.0)
-    mset(a("TT", CODE, 3 * CODE), 2.0 ** 20)
-    cp(a("TT", 2 * CODE, 2 * CODE + 31), a("TBL", 1, 32))
-    ts(a("OH", 0, 16), a("cJ", 0, 16), col(CI_), OP.is_equal)
+    cp(a("TBL", 16, 32), a("TBL", 0, 16), "v")
+    cp(a("TB2", 0, 16), a("cJ", 0, 16), "v")
+    cp(a("TB2", 16, 32), a("cJ", 0, 16), "v")
+    mset(col(C40), -40.0)
+    mset(a("c1", 144, 160), 2.0 ** -8)
+    scan(a("TT", 0, 16), a("c1", 144, 160), a("c2", 0, 16), 2.0 ** 68, OP.mult, OP.add)
+    tt(a("c2", 176, 192), a("OH", 0, 16), a("TT", 0, 16), OP.mult)
+    red(col(CPQ), a("c2", 176, 192), OP.add)
+    mset(a("TT", 15, 16), 2.0 ** 68)
+    cp(a("TT", 16, 32), a("TT", 0, 16), "v")
+    mset(a("C2k", 0, GAP), 0.0)
+    mset(a("C2k", GAP, 2 * GAP), 2048.0)
     tt(a("c2", 128, 144), a("OH", 0, 16), a("TBL", 0, 16), OP.mult)
     red(col(CPW), a("c2", 128, 144), OP.add)
     tt(a("c2", 144, 160), a("OH", 0, 16), a("PW", 0, 16), OP.mult)
     red(col(CUP), a("c2", 144, 160), OP.add)
     ts(a("ZWp"), a("ZW1"), col(CPW), OP.mult, 0.5, OP.mult)
-    for n, v in (("ZWd", -2048.0), ("ZW2", 4096.0), ("ZWt", 2048.0), ("ZWw", col(CW))):
-        if (n != "ZWt" or "s" in LEVEL) and (n != "ZWw" or VSUM):
-            ts(a(n), a("ZW1"), v, OP.mult)
+    for n, v in (("ZWd", -2048.0), ("ZW2", 4096.0), ("ZWq", col(CPQ))):
+        ts(a(n), a("ZW1"), v, OP.mult)
     ts(a("Z8"), a("cJ"), col(CZ8), OP.is_equal)
     ts(a("c1", 0, 128), a("cJ", 0, 128), col(CQ16), OP.subtract, 0.0, OP.is_ge)
     ts(a("c2", 0, 128), a("cJ", 0, 128), col(CQ16), OP.subtract, 16.0, OP.is_lt)
     tt(a("BO"), a("c1", 0, 128), a("c2", 0, 128), OP.mult)
-    ts(a("BOw"), a("BO"), col(CW), OP.mult)
+    for c in range(2):
+        ts(a("BOw", 128 * c, 128 * c + 128), a("BO"), col(CW), OP.mult)
+    for n, c, v in (("B4", 0, 4.0), ("B16", 112, 16.0), ("B5", 112, 5.0)):
+        ts(a(n), a("BOw", c, c + 128), v, OP.mult)
+    ts(a("B2k"), a("BO"), 2048.0, OP.mult)
     ts(a("c1", 160, 165), a("cJ", 0, 5), col(CI_), OP.add)
     ts(a("cI", 0, 5), a("c1", 160, 165), -2.0, OP.add, 0.2, OP.mult)
     ts(a("c2", 160, 165), a("cI", 0, 5), -5.0, OP.mult)
@@ -349,44 +352,45 @@ def build(g, core, T, topo):
     ts(a("c1", 160, 165), a("c1", 160, 165), -16.0, OP.mult, col(CP128), OP.add)
     ts(a("cI", 0, 5), a("c1", 160, 165), -16.0, OP.add)
     ts(a("cI", 0, 5), a("cI", 0, 5), 127, OP.bitwise_and)
-    cp(a("col", PC, PC + 5), a("cI", 0, 5))
+    cp(a("col", PC, PC + 5), a("cI", 0, 5), "v")
     for c in range(5):
         ts(a("PERM", 128 * c, 128 * c + 128), a("cJ", 0, 128), col(PC + c), OP.is_equal, float(CODE), OP.mult)
-    iota(a("rr", 0, LW), [[256, NB], [1, 16]], 0, 0)
-    ts(a("CK"), a("rr", 0, LW), col(CI16), OP.add)
-    DUM, WGT, MUL, THR, TMP, VS, THE, U1, KEY, NN, CC, CNT, CON = 0, 1, 3, 5, 6, 8, 14, 15, 16, 17, 18, 19, 20
+    iota(a("rr", 0, CODE), [[256, CODE // 16], [1, 16]], 0, 0)
+    ts(a("CK"), a("rr", 0, CODE), col(CI16), OP.add)
+    DUM, THR, TMP, THE, U1, KEY, NN, CC, CNT, CON, LL, WGT = 0, 1, 2, 4, 5, 6, 7, 8, 9, 10, 11, 12
     ts(sf(TMP), a("cJ", 0, 12), 16.0, OP.mult, col(CI_), OP.add)
     ts(sf(DUM), sf(TMP), float(KDUM), OP.add)
-    for h in range(NH):
-        cp(wide("sh", 0, h, 0, NB), sf(TMP, 0))
-    ts(sf(WGT, 0), a("PW", 0, LW, 16), col(CUP), OP.mult, 2.0 ** -13, OP.mult)
-    for j, v in enumerate((4.0, 21.0, 2048.0)):
-        mset(a("sf", 16 * MUL + NB * j, 16 * MUL + NB * (j + 1)), v)
-    cp(su(0), a("cJ", 0, 12))
+    cp(sh(0), sf(TMP), "v")
+    cp(su(0), a("cJ", 0, 12), "v")
     mset(si(0), 0)
     for h in range(NH):
-        mset(a("WK", 3 * CODE * h + LW, 3 * CODE * (h + 1)), 0)
+        for c in range(3 if LW[h] < CODE else 0):
+            mset(a("WK", CODE * (3 * h + c) + LW[h], CODE * (3 * h + c + 1)), 0)
     mset(a("YP"), 0.0)
     mset(a("MW"), 0.0)
-    mset(a("MU"), 0.0)
+    if HOMEH:
+        mset(a("MU"), 0.0)
     mset(a("sf", 16 * THR, 16 * THR + 16), 0.0)
     for n in ("ZZ00", "ZZ01", "ZZ10", "ZZ11"):
-        mset(a(n, UA), 0.0)
+        mset(a(n, ZA - GAP), 0.0)
     c = 16
-    while c < BIG:
-        cp(a("OH", c, min(2 * c, BIG)), a("OH", 0, min(c, BIG - c)))
+    while c < 16 * CODE:
+        cp(a("OH", c, 2 * c), a("OH", 0, c), "v")
         c *= 2
-    ts(a("MK"), a("OH", 0, 3 * LW), -1.0, OP.add, FAR, OP.mult)
-    ts(a("c1", 0, LW), a("OH", 0, LW), 2048.0 + X0, OP.mult)
-    tt(a("MK2"), a("c1", 0, LW), a("MK", 0, LW), OP.add)
-    tt(a("c2", 0, LW), a("OH", 0, LW), a("PW"), OP.mult)
-    ts(a("c2", 128, 128 + LW), a("MK", 0, LW), 0.5 * FAR, OP.mult)
-    tt(a("c2", 0, LW), a("c2", 128, 128 + LW), a("c2", 0, LW), OP.subtract)
-    ts(a("MK3"), a("c2", 0, LW), 2.0, OP.mult)
-    for c in range(0, KDUM, 856):
-        iota(a("IO", c, c + 856), [[1, 856]], c, 0, after=sent)
-    for x, s in (("X", "S"), ("XN", "SN")) if SPARE else ():
-        dma("y", [(a(s, A, NK), a("IO", 0, NK - A)), (a(x, 0, X0), a("OH", 0, X0)), (a(x, KCON, NK), a("OH", 0, NK - KCON))], 2 ** 21)
+    ts(a("MK"), a("OH", 0, 3 * CODE), -1.0, OP.add, FAR, OP.mult)
+    ts(a("c1", 0, CODE), a("OH", 0, CODE), 2048.0 + X0, OP.mult)
+    tt(a("MK2"), a("c1", 0, CODE), a("MK", 0, CODE), OP.add)
+    tt(a("c2", 0, SPLIT), a("OH", 0, SPLIT), a("PW"), OP.mult)
+    ts(a("c2", 128, 128 + SPLIT), a("MK", 0, SPLIT), 0.5 * FAR, OP.mult)
+    tt(a("c2", 0, SPLIT), a("c2", 128, 128 + SPLIT), a("c2", 0, SPLIT), OP.subtract)
+    ts(a("MK3", 0, SPLIT), a("c2", 0, SPLIT), 2.0, OP.mult)
+    ts(sf(WGT, 0), a("PW", 0, SPLIT, 16), col(CUP), OP.mult, 2.0 ** -13, OP.mult)
+
+    def numbers(after):
+        for c in range(0, KDUM, 856):
+            iota(a("IO", c, c + 856), [[1, 856]], c, 0, after=after)
+    if not HOMEH:
+        numbers(sent)
 
     def SH(n, s):
         return a(n, 128 - 16 * (s % N), 256 - 16 * (s % N))
@@ -394,18 +398,29 @@ def build(g, core, T, topo):
     def WW(n, s, i):
         return a(n, 128 - 16 * (s % N) - i, 256 - 16 * (s % N) - i)
 
-    def hs(n, h, base=0):
-        return a(n, base + LW * h, base + LW * (h + 1))
+    def hs(n, h):
+        return a(n, T0[h], T1[h])
+
+    def all16(n, h):
+        return a(n, 16 * T0[h], 16 * T1[h])
 
     def osum(out, mat, s, src, h, first=True, last=True):
+        cut[0] += 1
         for i in range(16):
-            mm(out, WW(mat, s, i), a3(src, LW * h + i, LW * (h + 1), st=16), first and i == 0, last and i == 15)
+            mm(out, WW(mat, s, i), a3(src, T0[h] + i, T1[h], st=16), first and i == 0, last and i == 15)
+        cut[0] += 1
 
     def diag(out, ps, r0, r1, terms, mask):
         mm(a3(ps, r0, r1), I, mask, True, False)
         for j, (q0, q1, l, r) in enumerate(terms):
+            cut[0] += j == 0 or (r["nm"] == "EQ" and l["nm"] == "BO")
             mm(a3(ps, q0, q1), l, r, False, j == len(terms) - 1)
         red(out, a3(ps, r0, r1), OP.max)
+
+    def shift(pm, c, sign, src, n, h, first=True):
+        for m in range(5):
+            f = (m - T0[h]) % 5
+            mm(a(pm, c + f, c + n, 5), SH("ZI", sign * (1 + m)), src(f, n, 5), first, first or m == 4)
 
     nb = [0]
 
@@ -413,300 +428,282 @@ def build(g, core, T, topo):
         nb[0] += 1
         b = ("PB0", "PB1", "PB2")[nb[0] % 3]
         for kk in range(KG):
-            o, k = one(b, 0, LW, kk), kg * KG + kk
-            mm(o, pos, a(src, BIG * h + k, BIG * (h + 1), 16) if len(SCRATCH[src][1]) == 2 else one(src, LW * h, LW * (h + 1), k), True, False)
+            o, k = one(b, 0, LW[h], kk), kg * KG + kk
+            mm(o, pos, a(src, 16 * T0[h] + k, 16 * T1[h], 16), True, False)
             mm(o, neg, zz, False, True)
-        return a3(b, 0, LW)
+        return a3(b, 0, LW[h])
 
     def big(n, h, kg):
-        return a3(n, LW * h, LW * (h + 1), kg * KG, (kg + 1) * KG)
+        return a3(n, T0[h], T1[h], kg * KG, (kg + 1) * KG)
 
-    def words(dst, h, src, lst, base, j, then=None):
-        eng = GENG.split()[NH * j + h]
-        w = LW // len(eng)
-        for c, e in enumerate(eng):
-            c0 = LW * h + c * w
-            o, i = a(dst, 16 * c0, 16 * (c0 + w)), ind(a(src, X0, X0 + W), a(lst, base + c * w, base + (c + 1) * w))
+    def words(dst, h, src, lst, base, then=None):
+        for c in range(0, LW[h], PIECE):
+            c0, c1 = T0[h] + c, T0[h] + c + PIECE
+            o, i = a(dst, 16 * c0, 16 * c1), ind(a(src, X0, X0 + W), a(lst, base + c, base + c + PIECE))
             if then:
-                tt(o, i, a("zr", 16 * c0, 16 * (c0 + w)), OP.subtract)
-                act(a3(then, c0, c0 + w), o, AF.Abs)
+                tt(o, i, a("zr" + then[1], 16 * c0, 16 * c1), OP.subtract)
+                act(a3(then, c0, c1), o, AF.Abs)
             else:
-                cp(o, i, e.replace("x", "vs"))
+                cp(o, i)
 
-    def halve(out, pm, c, x, y, wy):
-        o = a(pm, c, c + LW)
-        mm(o, I, a("CQ"), True, False)
+    def fused(h, j):
+        return "BC"[j] + str(h) in FUSE and (rnd[0] > 0 or not HOMEH)
+
+    def repeat(h, j, nxt=1):
+        pm, x, zw = "PM%d" % h, "BC"[j], "ZZ%d%d" % ((rnd[0] + nxt) % 2, h)
+        for m in range(5):
+            f = (m - T0[h]) % 5
+            mm(a(pm, f, LW[h], 5), SH("ZI", 1 + j + m), a(zw, ZA + f, ZA + LW[h], 5))
+        cp(hs("ze" + x, h), a(pm, 0, LW[h]))
+        for k in range(16):
+            o, i = a("zr" + x, 16 * T0[h] + k, 16 * T1[h], 16), hs("ze" + x, h)
+            o["reg"] = [("zr" + x, 16 * T0[h], 16 * T1[h], k, k + 1)]
+            add({"g": (170 + 2 * CY * LW[h], lambda o=o, i=i: g.affine_select(o["ap"], i["ap"], [[0, LW[h]]], OP.is_ge, 0.0, 1, 0))}, [o], [i], after=sent)
+
+    def halve(out, pm, c, x, y, wy, h):
+        o = a(pm, c, c + LW[h])
+        mm(o, I, a("CQ", 0, LW[h]), True, False)
         mm(o, wy, y, False, False)
+        cut[0] += 1
         mm(o, a("HI"), x, False, True)
         ts(out, o, ROUND, OP.add, ROUND, OP.subtract)
 
     def bounds():
-        cp(a("thrK"), ind(a("sf", 16 * THR, 16 * THR + 16), su(0)), "vs")
+        cp(a("thrK"), ind(a("sf", 16 * THR, 16 * THR + 16), su(0)))
 
     def powers():
-        cp(a("thrR"), ind(a("TBL"), su(1)), "vs")
+        cp(a("thrR"), ind(a("TBL"), su(1)))
         diag(sf(THR), "PS0", 0, 12, [(0, 12, I, a("thrR"))], a("MK", 0, LN))
 
-    rnd = [0]
-
-    def zz(h, c0, c1, nxt=0, st=None):
-        return a("ZZ%d%d" % ((rnd[0] + nxt) % 2, h), c0, c1, st)
-
-    def aim(h, nxt=0):
+    def zz(h, c, nxt=0):
         if nxt and rnd[0] == RO - 1:
             return hs("Zf", h)
-        return zz(h, ZA, ZA + LW, nxt)
+        return a("ZZ%d%d" % ((rnd[0] + nxt) % 2, h), ZA + c * CODE, ZA + c * CODE + LW[h])
 
     def uz(h, c0, c1, st=None):
         if HOMEH and rnd[0] == 0:
             return a("MI", MUH * h + c0, MUH * h + c1, st)
-        return zz(h, UA + c0, UA + c1, st=st)
+        return a("ZZ%d%d" % (rnd[0] % 2, h), ZA - GAP + c0, ZA - GAP + c1, st)
 
     def yp(h, c0, c1, st=None):
-        return a("YP", 304 * h + c0, 304 * h + c1, st)
+        return a("YP", 3 * GAP * h + c0, 3 * GAP * h + c1, st)
 
-    def ds(h, j):
-        return a("Ds", 400 * h + 200 * j, 400 * h + 200 * j + LW)
+    def wk(h, c):
+        return a("WK", CODE * (3 * h + c), CODE * (3 * h + c) + LW[h])
 
-    def zs(h, j):
-        return a("Ds", 400 * h + 200 * j + 100, 400 * h + 200 * j + 100 + LW)
+    def ds(h, c=0):
+        if c and fused(h, 0):
+            return hs("zeB", h)
+        return a("Ds", 2 * GAP * h + GAP * c, 2 * GAP * h + GAP * c + LW[h])
 
-    def fused(h):
-        return str(h) in FUSE and rnd[0] > 0
+    def mu(n, h, c, w):
+        return a(n, MUH * h + c, MUH * h + c + w)
 
-    cp(a("Lb", p=(0, N)), a("Li", p=(0, N)))
+    cp(a("Lb", p=(0, N)), a("Li", p=(0, N)), "v")
     for i in range(16):
         mm(a("PM0", 0, 12), a("Z8", 128 - i, 256 - i, p=(0, N)), a("Lb", i, LN, 16, p=(0, N)), i == 0, i == 15)
-    cp(su(1), a("PM0", 0, 12))
-    cp(a("Ku"), a("Ki"))
+    cp(su(1), a("PM0", 0, 12), "v")
+    cp(a("Ku"), a("Ki"), "v")
+    if not HOMEH:
+        cp(sf(LL), a("PM0", 0, 12), "v")
+        cp(a("To"), ind(a("TT"), su(1)))
     for h in range(NH):
         if HOMEH:
-            cp(a("MU", MUH * h + 292, MUH * h + 292 + NB), a("PM0", NB * h, NB * (h + 1)))
-            cp(a("MU", MUH * h + 100, MUH * h + 100 + LW), hs("Zi", h))
-            ts(a("MU", MUH * h + 196, MUH * h + 196 + LW), hs("Ki", h), -2048.0, OP.add)
+            cp(mu("MU", h, 3 * GAP, NB[h]), a("PM0", B0[h], B0[h] + NB[h]), "v")
+            cp(mu("MU", h, GAP, LW[h]), hs("Zi", h), "v")
+            ts(mu("MU", h, 2 * GAP, LW[h]), hs("Ki", h), -2048.0, OP.add)
         else:
-            cp(wide("sh", 0, h, NB, 2 * NB), a("PM0", NB * h, NB * (h + 1)))
-            cp(aim(h), hs("Zi", h))
+            cp(wk(h, 1), hs("Ki", h), "v")
+            cp(zz(h, 0), hs("Zi", h), "v")
+            for j in range(2):
+                if fused(h, j):
+                    repeat(h, j, 0)
     powers()
     bounds()
-    if not HOMEH:
-        cp(a("Kf"), a("Ki"))
     for c in range(2):
-        cp(a("S", 512 * c, 512 * c + 512), a("Si", 512 * c, 512 * c + 512), SX)
+        cp(a("S", 512 * c, 512 * c + 512), a("Si", 512 * c, 512 * c + 512))
 
     def speaker(h, src, xg, z, us):
-        ps, pm = "PS%d" % h, "PM%d" % h
-        words(xg, h, src, "Ku", LW * h, 0)
+        ps, pm, n = "PS%d" % h, "PM%d" % h, NB[h]
+        words(xg, h, src, "Ku", T0[h])
         for kg in range(16 // KG):
-            act(big("dx", h, kg), sub(xg, h, kg, z, I, a("NI")), AF.Abs)
+            act(big("dx", h, kg), sub(xg, h, kg, z, I, NI), AF.Abs)
             ts(big("gt", h, kg), big("dx", h, kg), 40.0, OP.is_gt)
-        osum(a(pm, 0, LW), "ZWp", 0, "gt", h)
-        mm(a3(ps, 0, NB), I, a("CK"), True, False)
-        osum(a3(ps, 0, NB), "ZWd", 0, "dx", h, False, False)
-        tt(hs("fit", h), a(pm, 0, LW), hs("thrK", h), OP.is_lt)
-        mm(a3(ps, 0, NB), a("NF"), hs("fit", h), False, True)
-        red(wide("si", 2, h, 0, NB), a3(ps, 0, NB), OP.min)
-        ts(wide("si", 2, h, 8, 8 + NB), wide("si", 2, h, 0, NB), 2047, OP.bitwise_and)
-        cp(su(2, h), wide("si", 2, h, 8, 8 + NB), SX)
-        tt(us, ind(a(xg, BIG * h, BIG * (h + 1)), su(2, h)), z, OP.subtract)
+        osum(a(pm, 0, LW[h]), "ZWp", 0, "gt", h)
+        mm(a3(ps, 0, n), I, a("CK", 0, LW[h]), True, False)
+        osum(a3(ps, 0, n), "ZWd", 0, "dx", h, False, False)
+        tt(hs("fit", h), a(pm, 0, LW[h]), hs("thrK", h), OP.is_lt)
+        mm(a3(ps, 0, n), a("NF"), hs("fit", h), False, True)
+        red(wide("si", 2, h, 0, 1), a3(ps, 0, n), OP.min)
+        ts(wide("si", 2, h, 1, 2), wide("si", 2, h, 0, 1), 2047, OP.bitwise_and)
+        cp(su(2, h), wide("si", 2, h, 1, 2))
+        tt(us, ind(all16(xg, h), su(2, h)), z, OP.subtract)
+
+    told = [sent]
 
     def first(h):
-        speaker(h, "XN", "xh", hs("Zi", h), a("MU", MUH * h, MUH * h + LW))
+        speaker(h, "XN", "xh", hs("Zi", h), mu("MU", h, 0, LW[h]))
         u1, u2 = stage("U%d" % h, sbs("MU", MUH * h, MUH * (h + 1)))
         dma("s", u1 + u2, 1e5)
-        exchange(["U%d" % h], 1e5)
-        dma("s", [(a("MI", MUH * h, MUH * (h + 1)), land("U%d" % h))], 1e5)
-        cp(aim(h), uz(h, 100, 100 + LW), "vs")
-        lin(hs("Kf", h), a("MI", MUH * h + 196, MUH * h + 196 + LW), 1.0, 2048.0)
-        cp(wide("sh", 0, h, NB, 2 * NB), a("MI", MUH * h + 292, MUH * h + 292 + NB), "vs")
-        cp(su(1, h), a("MI", MUH * h + 292, MUH * h + 292 + NB))
-        if h == NH - 1:
+        told[0] = exchange(["U%d" % h], 1e5, after=told[0])
+        dma("s", [(mu("MI", h, 0, MUH), land("U%d" % h))], 1e5)
+        cp(zz(h, 0), uz(h, GAP, GAP + LW[h]))
+        lin(wk(h, 1), mu("MI", h, 2 * GAP, LW[h]), 1.0, 2048.0)
+        cp(sf(LL, h), mu("MI", h, 3 * GAP, NB[h]))
+        cp(su(1, h), mu("MI", h, 3 * GAP, NB[h]), "v")
+        if "H%d" % h == [w for w in ORDER.split() if w[0] == "H"][-1]:
+            cp(a("To"), ind(a("TT"), su(1)))
             powers()
             g1, g2 = stage("G", sbs("xh", 0, 16 * LN))
-            dma("y", g1 + g2, 2 ** 20)
-            exchange(["G"], 2 ** 20)
+            dma("y", g1 + g2, 2 ** 20, after=landed)
+            exchange(["G"], 2 ** 20, after=told[0])
+            numbers(told[0])
             dma("y", [(a("xg"), land("G"))], 2 ** 20)
 
     def home(h, last):
-        ps, pm, db = "PS%d" % h, "PM%d" % h, 2 * LW * h
-        us = uz(h, 0, LW)
+        ps, pm, db, n, lw = "PS%d" % h, "PM%d" % h, 2 * T0[h], NB[h], LW[h]
+        us = uz(h, 0, lw)
         if HOMEH and rnd[0] == 0:
             first(h)
         else:
-            speaker(h, "X", "xg", aim(h), us)
-        lin(hs("K20", h), hs("Kf", h), 20.0, 0.0)
+            speaker(h, "X", "xg", zz(h, 0), us)
+        lin(hs("K20", h), wk(h, 1), 20.0, 0.0)
+        w = lw if fused(h, 0) else GAP + lw
+        shift(pm, 0, 1, lambda c0, c1, st: uz(h, c0, c1, st), w, h)
+        act(a("Ds", 2 * GAP * h, 2 * GAP * h + w), a(pm, 0, w), AF.Abs)
+        terms = [(n, 2 * n, a("B4"), ds(h)), (2 * n, 3 * n, a("B16"), ds(h)), (2 * n, 3 * n, a("B5"), ds(h)), (3 * n, 4 * n, a("B2k"), ds(h))]
+        diag(wide("si", 4, h, 0, 3, 2), ps, n, 4 * n, terms, a("MK", 0, 3 * lw))
         for j in range(2):
-            for m in range(5):
-                f = (m - LW * h) % 5
-                mm(a(pm, 200 * j + f, 200 + 200 * j, 5), SH("ZI", 1 + m + j), uz(h, f, 200, 5))
-        act(a("Ds", 400 * h, 400 * h + 396), a(pm, 0, 396), AF.Abs)
-        lv = LEVEL.split()[h]
-        nv = 2 if lv == "ss" else 3
-        vi = a("si", 16 * (4 + 2 * h), 16 * (4 + 2 * h) + nv * NB)
-        vs = a("sf", 16 * (VS + 2 * h), 16 * (VS + 2 * h) + nv * NB)
-        terms = [(NB, 2 * NB, a("BOw"), ds(h, 0)), (2 * NB, 3 * NB, a("BOw"), ds(h, 1)), (3 * NB, 4 * NB, a("BO"), ds(h, 0))]
-        diag(vs, ps, NB, (1 + nv) * NB, terms[:nv], a("MK", 0, nv * LW))
-        tt(vi, vs, a("sf", 16 * MUL, 16 * MUL + nv * NB), OP.mult)
-        for j in range(2):
-            if lv[j] == "v":
-                mm(a("PD", db + LW * j, db + LW * (j + 1)), I, ds(h, j))
-        ts(wide("si", 8, h), a("si", 16 * (4 + 2 * h), 16 * (4 + 2 * h) + 2 * NB), 2, OP.arith_shift_right, A - 1, OP.bitwise_and)
-        cp(wide("su", 4, h), wide("si", 8, h), SX)
-        cp(a("PGu", db, db + 2 * LW), ind(a("S", 0, A), wide("su", 4, h)), SX)
+            mm(a("PD", db + lw * j, db + lw * (j + 1)), SH("ZI", j), ds(h))
+        ts(wide("si", 8, h, 0, 2), wide("si", 4, h, 0, 2, 2), 2, OP.arith_shift_right, A - 1, OP.bitwise_and)
+        cp(wide("su", 4, h, 0, 2), wide("si", 8, h, 0, 2))
+        cp(a("PGu", db, db + 2 * lw), ind(a("S" if rnd[0] else "Si", 0, A), wide("su", 4, h, 0, 2)), "vs" if rnd[0] else "v")
         act(hs("D", h), us, AF.Abs)
-        mm(a(pm, 0, LW), a("BOw"), hs("D", h))
-        tt(hs("vi", h), a(pm, 0, LW), hs("K20", h), OP.add)
-        ts(a("WK", 3 * CODE * h, 3 * CODE * h + LW), hs("vi", h), 2, OP.arith_shift_right, W - 1, OP.bitwise_and)
-        halve(zz(h, ZA + CODE, ZA + CODE + LW), pm, 100, us, uz(h, 100, 100 + LW), I)
-        ts(yp(h, 100, 100 + 2 * LW), a("PGu", db, db + 2 * LW), -2048.0, OP.add)
-        lin(hs("Pf", h), yp(h, 100, 100 + LW), 1.0, 2048.0)
-        mm(a(pm, 200, 200 + LW), SH("ZI", -1), yp(h, 100 + LW, 100 + 2 * LW))
-        cp(hs("GB", h), a(pm, 200, 200 + LW), "vs")
+        mm(a(pm, 0, lw), SH("BOw", 0), hs("D", h))
+        tt(hs("vi", h), a(pm, 0, lw), hs("K20", h), OP.add)
+        ts(wk(h, 0), hs("vi", h), 2, OP.arith_shift_right, W - 1, OP.bitwise_and)
+        halve(zz(h, 1), pm, GAP, us, uz(h, GAP, GAP + lw), I, h)
+        ts(yp(h, GAP, GAP + 2 * lw), a("PGu", db, db + 2 * lw), -2048.0, OP.add)
+        lin(hs("Pf", h), yp(h, GAP, GAP + lw), 1.0, 2048.0)
+        mm(a(pm, 2 * GAP, 2 * GAP + lw), SH("ZI", -1), yp(h, GAP + lw, GAP + 2 * lw))
+        cp(hs("GB", h), a(pm, 2 * GAP, 2 * GAP + lw))
 
     def look(h, j):
-        ps = "PS%d" % h
+        ps, n = "PS%d" % h, NB[h]
         y, aa, mx = (("yB", "aB", "mB"), ("yC", "aC", "mC"))[j]
-        c = 2 * LW * h + LW * j
-        fu, lv = j == 0 and fused(h), LEVEL.split()[h][j]
-        words(y, h, "X", "PGu", c, 1 + j, aa if fu else None)
+        c = 2 * T0[h] + LW[h] * j
+        words(y, h, "X", "PGu", c, aa if fused(h, j) else None)
         for kg in range(16 // KG):
-            if not fu:
-                act(big(aa, h, kg), sub(y, h, kg, zs(h, j), I, a("NI")), AF.Abs)
-            if lv == "v":
-                for k in range(kg * KG, (kg + 1) * KG):
-                    tt(one(mx, LW * h, LW * (h + 1), k), one(aa, LW * h, LW * (h + 1), k), a("PD", c, c + LW), OP.max)
-            elif kg > 0:
-                act(big(mx, h, kg - 1), sub(aa, h, kg - 1, ds(h, j), I, a("NI")), AF.Abs)
-        o = a3(ps, (1 + j) * NB, (2 + j) * NB)
-        mm(o, I, a("CK"), True, False)
-        if lv == "v":
-            osum(o, "ZWd", -j, aa, h, False, False)
-            osum(o, "ZW2", -j, mx, h, False, True)
-        else:
-            act(big(mx, h, 3), sub(aa, h, 3, ds(h, j), I, a("NI")), AF.Abs)
-            osum(o, "ZWt", -j, mx, h, False, True)
-        red(wide("si", 10, h, NB * j, NB * (j + 1)), o, OP.min)
-        ts(wide("si", 12, h, NB * j, NB * (j + 1)), wide("si", 10, h, NB * j, NB * (j + 1)), 2047, OP.bitwise_and)
-        cp(wide("su", 6, h, NB * j, NB * (j + 1)), wide("si", 12, h, NB * j, NB * (j + 1)), SX)
+            if not fused(h, j):
+                act(big(aa, h, kg), sub(y, h, kg, ds(h, 1), I, SH("NI", j)), AF.Abs)
+            for k in range(kg * KG, (kg + 1) * KG):
+                tt(one(mx, T0[h], T1[h], k), one(aa, T0[h], T1[h], k), a("PD", c, c + LW[h]), OP.max, run=("v", mx, kg))
+        o = a3(ps, (1 + j) * n, (2 + j) * n)
+        mm(o, I, a("CK", 0, LW[h]), True, False)
+        osum(o, "ZWd", -j, aa, h, False, False)
+        osum(o, "ZW2", -j, mx, h, False, True)
+        red(wide("si", 10, h, j, j + 1), o, OP.min)
+        ts(wide("si", 12, h, j, j + 1), wide("si", 10, h, j, j + 1), 2047, OP.bitwise_and)
+        cp(wide("su", 6, h, j, j + 1), wide("si", 12, h, j, j + 1))
 
     def msg(h, c0, c1):
-        return a("MW", MWH * h + c0, MWH * h + c1)
+        return a("MW", M0[h] + c0, M0[h] + c1)
 
     def partner(h, last):
-        ps, pm, db = "PS%d" % h, "PM%d" % h, 2 * LW * h
-        me, jl = wide("si", 10, h, 0, NB), wide("su", 6, h, 0, NB)
-        lv, true = LEVEL.split()[h], me
-        if lv[0] == "v":
-            true = sf(TMP, h)
-            tt(true, me, a("si", 16 * (4 + 2 * h) + 2 * NB, 16 * (4 + 2 * h) + 3 * NB), OP.subtract)
-        lin(sf(THE, h), true if lv == "vs" else me, 1.0, col(AM), SX)
-        ts(sf(CC, h), true, 800.0 * 2048, OP.is_lt, 1.0, OP.add)
-        ts(sf(TMP + 1, h), true, 800.0 * 2048, OP.is_lt, float(KCON), OP.mult)
-        best = ind(a("yB", BIG * h, BIG * (h + 1)), jl)
-        if fused(h):
-            tt(yp(h, 0, LW), best, zs(h, 0), OP.add)
+        ps, pm, n, lw = "PS%d" % h, "PM%d" % h, NB[h], LW[h]
+        me, jl = wide("si", 10, h, 0, 1), wide("su", 6, h, 0, 1)
+        tt(sf(TMP, h), me, wide("si", 4, h, 2, 3, 2), OP.subtract)
+        lin(sf(THE, h), me, 1.0, col(AM))
+        ts(sf(CC, h), sf(TMP, h), 800.0 * 2048, OP.is_lt, 1.0, OP.add)
+        ts(sf(TMP + 1, h), sf(TMP, h), 800.0 * 2048, OP.is_lt, float(KCON), OP.mult)
+        if fused(h, 0):
+            tt(yp(h, 0, lw), ind(all16("yB", h), jl), ds(h, 1), OP.add)
         else:
-            cp(yp(h, 0, LW), best, "vs")
-        cp(hs("ohj", h), ind(a("OH"), jl), "vs")
-        tt(hs("ohP", h), hs("ohj", h), yp(h, 100, 100 + LW), OP.mult)
-        if PJSUM:
-            pj = a(pm, 400, 400 + NB)
-            mm(pj, I, a("C3k"), True, False)
-            for i in range(16):
-                mm(pj, WW("ZW1", 0, i), a("ohP", LW * h + i, LW * (h + 1), 16), False, i == 15)
-            tt(sf(U1, h), pj, sf(TMP + 1, h), OP.max)
-        else:
-            diag(sf(U1, h), ps, 4 * NB, 5 * NB, [(4 * NB, 5 * NB, a("BO"), hs("ohP", h))], a("MK2"))
-            tt(sf(U1, h), sf(U1, h), sf(TMP + 1, h), OP.max)
-        for m in range(5):
-            f = (m - LW * h) % 5
-            mm(a(pm, 200 + f, 400, 5), SH("ZI", -1 - m), yp(h, f, 200, 5))
-        cp(zz(h, ZA + 2 * CODE, ZA + 2 * CODE + LW), a(pm, 200, 200 + LW), "vs")
-        lin(a("WK", 3 * CODE * h + 2 * CODE, 3 * CODE * h + 2 * CODE + LW), a(pm, 300, 300 + LW), 1.0, 2048.0, SX)
-        halve(msg(h, 0, LW) if last else hs("nw", h), pm, 0, yp(h, 0, LW), ds(h, 0), a("HI"))
+            cp(yp(h, 0, lw), ind(all16("yB", h), jl))
+        cp(hs("ohj", h), ind(a("OH"), jl))
+        tt(hs("ohP", h), hs("ohj", h), yp(h, GAP, GAP + lw), OP.mult)
+        diag(sf(U1, h), ps, 3 * n, 4 * n, [(3 * n, 4 * n, a("BO"), hs("ohP", h))], a("MK2", 0, lw))
+        tt(sf(U1, h), sf(U1, h), sf(TMP + 1, h), OP.max)
+        c = 512 - 2 * GAP
+        mm(a(pm, c, c + GAP + lw), I, a("C2k", 0, GAP + lw), True, False)
+        shift(pm, c, -1, lambda c0, c1, st: yp(h, c0, c1, st), GAP + lw, h, False)
+        cp(zz(h, 2), a(pm, c, c + lw))
+        tt(hs("dl", h), a(pm, c + GAP, c + GAP + lw), wk(h, 1), OP.subtract)
+        halve(msg(h, 0, lw) if last else hs("nw", h), pm, 0, yp(h, 0, lw), ds(h), a("HI"), h)
 
     def decide(h, last):
-        pm = "PM%d" % h
-        tt(sh(2, h), wide("si", 10, h, NB, 2 * NB), sf(THE, h), OP.is_ge)
+        pm, n, lw = "PM%d" % h, NB[h], LW[h]
+        tt(sh(2, h), wide("si", 10, h, 1, 2), sf(THE, h), OP.is_ge)
         tt(sh(3, h), sf(CC, h), sh(2, h), OP.mult)
-        tt(sf(KEY, h), sf(U1, h), sh(2, h), OP.mult)
-        tt(sf(KEY, h), sf(KEY, h), wide("si", 8, h, 0, NB), OP.max)
-        cp(su(3, h), sf(KEY, h), SX)
-        cp(hs("kr", h), ind(a("IO"), su(3, h)), SX)
-        mm(a(pm, 400, 400 + 2 * NB), I, wide("sh", 0, h), True, False)
-        for j in range(2):
-            for c in range(5):
-                f = (c - NB * h) % 5
-                mm(a(pm, 400 + NB * j + f, 400 + NB * (j + 1), 5), a("PERM", 128 * c, 128 * c + 128), a("sh", 48 + NB * h + f, 48 + NB * (h + 1), 5),
-                   False, j == 1 and c == 4)
-        cp(wide("su", 8, h), a(pm, 400, 400 + 2 * NB), SX)
-        code = wide("su", 8, h, 0, NB)
-        cp(aim(h, 1), ind(zz(h, ZA, ZA + 3 * CODE), code), "vs")
-        tt(hs("dl", h), ind(a("WK", 3 * CODE * h, 3 * CODE * (h + 1)), code), hs("Kf", h), OP.subtract)
-        cp(hs("To", h), ind(a("TT"), wide("su", 8, h, NB, 2 * NB)), "vs")
-        tt(hs("ohG", h), ind(a("OH"), wide("su", 6, h, NB, 2 * NB)), hs("GB", h), OP.mult)
-        mm(a(pm, 100, 100 + LW), a("NI"), yp(h, 100, 100 + LW), True, False)
-        mm(a(pm, 100, 100 + LW), a("BO"), hs("ohG", h), False, True)
-        tt(hs("rr", h), a(pm, 100, 100 + LW), hs("ohj", h), OP.mult)
+        tt(sf(U1, h), sf(U1, h), sh(2, h), OP.mult)
+        tt(su(3, h), sf(U1, h), wide("si", 8, h, 0, 1), OP.max)
+        tt(sf(KEY, h), sf(U1, h), wide("si", 8, h, 0, 1), OP.max)
+        cp(hs("kr", h), ind(a("IO"), su(3, h)))
+        c0 = 2 * GAP
+        mm(a(pm, c0, c0 + n), I, a("sh", 0, n), True, False)
+        cls = [c for c in range(5) if (c - B0[h]) % 5 < n]
+        for c in cls:
+            f = (c - B0[h]) % 5
+            mm(a(pm, c0 + f, c0 + n, 5), a("PERM", 128 * c, 128 * c + 128), a("sh", 48 + B0[h] + f, 48 + B0[h] + n, 5), False, c == cls[-1])
+        cp(su(8, h), a(pm, c0, c0 + n))
+        zw = "ZZ%d%d" % (rnd[0] % 2, h)
+        cp(zz(h, 0, 1), ind(a(zw, ZA, ZA + 3 * CODE), su(8, h)))
+        tt(hs("ohG", h), ind(a("OH"), wide("su", 6, h, 1, 2)), hs("GB", h), OP.mult)
+        mm(a(pm, GAP, GAP + lw), NI, yp(h, GAP, GAP + lw), True, False)
+        mm(a(pm, GAP, GAP + lw), a("BO"), hs("ohG", h), False, True)
+        tt(hs("rr", h), a(pm, GAP, GAP + lw), hs("ohj", h), OP.mult)
         if last:
-            tt(msg(h, LW, 2 * LW), hs("rr", h), hs("Pf", h), OP.add)
-        elif str(h) in FUSE:
-            ze = hs("ze", h)
-            for m in range(5):
-                f = (m - LW * h) % 5
-                mm(a(pm, 200 + f, 200 + LW, 5), SH("ZI", 1 + m), zz(h, ZA + f, ZA + LW, 1, 5))
-            cp(ze, a(pm, 200, 200 + LW), "vs")
-            for k in range(16):
-                o = a("zr", BIG * h + k, BIG * (h + 1), 16)
-                o["reg"] = [("zr", BIG * h, BIG * (h + 1), k, k + 1)]
-                gcp(o, ze)
+            tt(msg(h, lw, 2 * lw), hs("rr", h), hs("Pf", h), OP.add)
+        for j in range(0 if last else 2):
+            if "BC"[j] + str(h) in FUSE:
+                repeat(h, j)
 
     def off(h, last):
-        o = a("PM%d" % h, 300, 300 + LW)
+        o = a("PM%d" % h, 384, 384 + LW[h])
         for kg in range(16 // KG):
-            b = sub("xg", h, kg, aim(h, 1), a("CI"), a("NCI"))
+            act(big("ab2", h, kg), sub("xg", h, kg, zz(h, 2), I, NI), AF.Abs)
             if OFFMODE.split()[h][kg] == "v":
-                ts(big("gt", h, kg), b, MAGIC, OP.add, MAGIC, OP.not_equal)
+                ts(big("gt", h, kg), big("ab2", h, kg), 40.0, OP.is_gt)
             else:
-                act(big("ab2", h, kg), b, AF.Abs)
-                ts(big("gt", h, kg), big("ab2", h, kg), 64.0, OP.is_gt)
+                act(big("gt", h, kg), big("ab2", h, kg), AF.Relu, col(C40))
         for k in range(16):
-            mm(o, WW("ZWp", 0, k), one("gt", LW * h, LW * (h + 1), k), k == 0, k == 15)
+            mm(o, WW("ZWq", 0, k), one("gt", T0[h], T1[h], k), k == 0, k == 15)
         tt(o, o, hs("To", h), OP.is_ge)
         tt(o, o, hs("dl", h), OP.mult)
-        tt(hs("Kf", h), o, hs("Kf", h), OP.add)
+        tt(wk(h, 2), o, wk(h, 1), OP.add)
+
+    def players(h, last):
+        cp(hs("Kf" if last else "Ku", h), ind(a("WK", 3 * CODE * h, 3 * CODE * (h + 1)), su(8, h)), "v")
         if not last:
-            cp(hs("Ku", h), hs("Kf", h), SX)
+            cp(wk(h, 1), hs("Ku", h), "v")
 
     def settle(h, last):
-        ps, terms = "PS%d" % h, []
-        for b in range(NB):
-            e = a("EQ", (NB * h + b) * LW, (NB * h + b) * LW + 16 * (b + 1))
-            ts(e, a("kr", LW * h, LW * h + 16 * (b + 1)), a("sf", 16 * KEY + NB * h + b, 16 * KEY + NB * h + b + 1), OP.is_equal,
-               a("sf", 16 * WGT + b, 16 * WGT + b + 1), OP.mult)
-            terms.append((0, b + 1, a("BO"), e))
-        diag(sf(NN, h), ps, 0, NB, terms, a("MK3"))
+        ps, terms, n, lw = "PS%d" % h, [], NB[h], LW[h]
+        for b in range(n):
+            e = CODE * (B0[h] + b)
+            ts(a("EQ", e, e + 16 * (b + 1)), a("kr", T0[h], T0[h] + 16 * (b + 1)), a("sf", 16 * KEY + B0[h] + b, 16 * KEY + B0[h] + b + 1),
+               OP.is_equal, a("sf", 16 * WGT + b, 16 * WGT + b + 1), OP.mult)
+            terms.append((0, b + 1, a("BO"), a("EQ", e, e + 16 * (b + 1))))
+        diag(sf(NN, h), ps, 0, n, terms, a("MK3", 0, lw))
         tt(sf(NN, h), sf(NN, h), sf(DUM, h), OP.min)
         if last:
-            tt(msg(h, 2 * LW, 2 * LW + NB), sf(NN, h), sf(KEY, h), OP.max)
+            tt(msg(h, 2 * lw, 2 * lw + n), sf(NN, h), sf(KEY, h), OP.max)
         else:
-            tt(sf(NN, h), sf(NN, h), sf(KEY, h), OP.max)
-            cp(su(10, h), sf(NN, h), SX)
+            tt(su(10, h), sf(NN, h), sf(KEY, h), OP.max)
 
     def write(h, last):
         if not last:
-            cp(ind(a("X"), su(10, h)), hs("nw", h))
+            cp(ind(a("X"), su(10, h)), hs("nw", h), "v")
             tt(ind(a("S"), su(10, h)), hs("rr", h), hs("Pf", h), OP.add)
 
     def carry(last):
-        for h in range(NH):
-            ts(sf(CON, h), wide("su", 8, h, 0, NB), float(2 * CODE), OP.is_ge)
-            tt(wide("sh", 0, h, NB, 2 * NB), wide("sh", 0, h, NB, 2 * NB), sf(CON, h), OP.add)
+        ts(sf(CON), su(8), float(2 * CODE), OP.is_ge)
+        tt(sf(LL), sf(LL), sf(CON), OP.add)
+        cp(su(1), sf(LL))
         if last:
-            for h in range(NH):
-                cp(su(1, h), wide("sh", 0, h, NB, 2 * NB))
-            cp(a("Lr"), ind(a("TB2"), su(1)), "vs")
+            cp(a("Lr"), ind(a("TB2"), su(1)))
             return
+        cp(a("To"), ind(a("TT"), su(1)))
         lin(sf(CON), sf(CON), -0.5, 1.0)
         tt(sf(THR), sf(THR), sf(CON), OP.mult)
         ts(sf(CON), sf(THR), 1.5, OP.is_lt, 65535.0, OP.mult)
@@ -716,14 +713,15 @@ def build(g, core, T, topo):
         red(a("sf", 16 * CNT, 16 * CNT + 1), a("PM1", 112, 124), OP.add)
         tt(a("si", 0, 1), a("si", 0, 1), a("sf", 16 * CNT, 16 * CNT + 1), OP.subtract)
         ts(a("si", 4, 5), a("si", 0, 1), 31, OP.bitwise_and)
-        lin(col(AM), a("si", 4, 5), 2048.0, 1024.0, SX)
+        lin(col(AM), a("si", 4, 5), 2048.0, 1024.0)
 
     steps = {"H": home, "B": lambda h, last: look(h, 0), "C": lambda h, last: look(h, 1), "P": partner, "D": decide, "O": off,
-             "S": settle, "W": write}
+             "S": settle, "W": write, "K": players}
     for r in range(RO):
         rnd[0] = r
         last = r == RO - 1
         if last:
+            stg[1] = "X"
             n1, n2 = stage("N", sbs("X", X0, X0 + W))
             s1, s2 = stage("S", sbs("S", 0, A))
             dma("y", n1, 2 ** 20)
@@ -735,29 +733,30 @@ def build(g, core, T, topo):
             dma("y", [(a("SN", 0, A), land("S"))], 2 ** 20)
         for w in ORDER.split():
             stg[0], stg[1] = stg[0] + 1, w
-            seen.clear()
             steps[w[0]](int(w[1]), last)
         stg[1] = "R"
         carry(last)
 
-    w1, w2 = stage("W", sbs("MW", 0, NH * MWH))
-    dma("y", w1, 2e5)
-    dma("y", w2, 2e5)
-    exchange(["W"], 2e5)
+    stg[1] = "E"
+    for h in range(NH):
+        w1, w2 = stage("W%d" % h, sbs("MW", M0[h], M0[h] + 200))
+        dma("y", w1, 1e5)
+        dma("y", w2, 1e5)
+        exchange(["W%d" % h], 1e5)
+        dma("y", [(a("MO", M0[h], M0[h] + 200), land("W%d" % h))], 1e5)
     k1, k2 = stage("K", sbs("Kf", 0, LN))
     z1, z2 = stage("L", sbs("Zf", 0, LN), 0, 64)
     l1, l2 = stage("L", sbs("Lr", 0, LN), 64, 128)
     dma("s", k1 + z1 + l1, 2e5)
     dma("s", k2 + z2 + l2, 2e5)
     exchange(["K", "L"], 2e5)
-    dma("y", [(a("MO"), land("W"))], 2e5)
     for h in range(NH):
-        cp(su(10, h), a("MO", MWH * h + 2 * LW, MWH * h + 2 * LW + NB))
+        cp(su(10, h), a("MO", M0[h] + 2 * LW[h], M0[h] + 2 * LW[h] + NB[h]), "v")
     for h in range(NH):
-        cp(ind(a("XN"), su(10, h)), a("MO", MWH * h, MWH * h + LW))
+        cp(ind(a("XN"), su(10, h)), a("MO", M0[h], M0[h] + LW[h]), "v")
     dma("y", [(d(T.yx[:], None), a("XN", X0, X0 + W))], 2 ** 20)
     for h in range(NH):
-        cp(ind(a("SN"), su(10, h)), a("MO", MWH * h + LW, MWH * h + 2 * LW))
+        cp(ind(a("SN"), su(10, h)), a("MO", M0[h] + LW[h], M0[h] + 2 * LW[h]), "v")
     dma("s", [(d(T.ya[:], None), a("SN", 0, A))], 2 ** 20)
     dma("s", [(d(T.yk[:], None), land("K")), (d(T.yz[:], None), land("L", 0, 64))], 2e5)
     dma("g", [(d(T.yl[:], None), land("L", 64, 68))], 1e4)
@@ -771,8 +770,8 @@ def depend(ops):
         eng = list(o["alts"])[0] if len(o["alts"]) == 1 else i
         for wr, regs in ((0, o["r"]), (1, o["w"])):
             for n, r0, r1, c0, c1 in regs:
-                if n == "zr" and not wr:
-                    c0, c1 = 0, 16
+                if n[:2] == "zr" and not wr:
+                    c1 = 16
                 if n in SCRATCH and SCRATCH[n][0] == "psum":
                     st = banks.setdefault(n, [None, [], []])
                     if st[0] != eng:
@@ -796,15 +795,17 @@ def depend(ops):
         o["dp"], o["od"] = dp, od - dp
 
 
-def place(ops, seq, pre, keep=None):
+def place(ops, seq, pre, keep):
     gaps = {}
     t0, c0, eng = [0.0] * len(ops), [0.0] * len(ops), [None] * len(ops)
     for i in seq:
-        t = max([t0[j] + c0[j] + w for j, w in pre[i]] + [0.0])
-        best = None
+        t, best = 0.0, None
+        if not ops[i]["alts"]:
+            t = max([t0[j] + c0[j] + w for j, w in pre[i]] + [0.0])
         for e, al in ops[i]["alts"].items():
             if keep[i] and keep[i] != e:
                 continue
+            t = max([t0[j] + c0[j] + (NEAR if w == HOP and eng[j] == e else w) for j, w in pre[i]] + [0.0])
             s, c = gaps.setdefault(e, []), al[0]
             lo, hi = 0, len(s)
             while lo < hi:
@@ -848,10 +849,9 @@ def schedule(ops):
         for i in post:
             c = min([x[0] for x in ops[i]["alts"].values()] or [0])
             prio[i] = c + max([prio[j] + w for j, w in post[i]] + [ops[i].get("lat", 0)])
-        seq, best = ordered([LAM * o["st"] + LATE.get(o["tag"], 0.0) - prio[i] for i, o in enumerate(ops)], pre), None
-        fix = [("s" if o["name"] in ONS else "v") if "name" in o and ONS is not None else None for o in ops]
+        seq, best = ordered([LAM * o["st"] + LATE.get(o["tag"], 0.0) + LATE.get(o["sub"], 0.0) - prio[i] for i, o in enumerate(ops)], pre), None
         for _ in range(PASSES):
-            t0, c0, eng = place(ops, seq, pre, fix)
+            t0, c0, eng = place(ops, seq, pre, [None] * n)
             end = max(t0[i] + c0[i] + ops[i].get("lat", 0) for i in range(n))
             if best is None or end < best[0]:
                 best = (end, t0, c0, eng)
@@ -896,8 +896,9 @@ def rank_program(g, core, T, topo):
             final[o["sem"][0]] = o["sem"][1]
         elif i in needed:
             s = ESEM[e]
-            count[s] = count.get(s, 0) + 1
-            ins.then_inc(T.sem[s], 1)
+            for x in ins if isinstance(ins, list) else [ins]:
+                count[s] = count.get(s, 0) + 1
+                x.then_inc(T.sem[s], 1)
             o["tok"] = (s, count[s])
             final[s] = count[s]
     for s, v in final.items():

from concourse.bass import DstId, RemoteDMATransfer
from concourse.mybir import AluOpType as OP, AxisListType, ActivationFunctionType as AF

N, W, A, LN, RO = 8, 4096, 1024, 192, 4
NH = 2
SPLIT = 96
KG = 4
XCH = 2
X0 = A
KCON = X0 + W
KDUM = KCON + 16
NK = KDUM + LN
CODE = 128
GAP = 100
ZA = 160
MUH = 400
ROUND = 1.5 * 2.0 ** 23
FAR = 2.0 ** 60
H16 = "float16"
ORDER = "H0 H1 B0 C0 P0 D0 B1 C1 P1 S0 O0 K0 D1 S1 W0 W1 O1 K1"
OFFMODE = "ssss vvvv"
FUSE = "B0 B1"
PIECE = 32
HOMEH = False
LATE = {'W0': -1000, 'D0': -6500, 'P0': 2000, 'S0': 6000, 'B0': -2000, 'R': -4500, 'C0': -4500, 'D1': 500, 'O0': 3000, 'H0': -2000, 'P1': -1000,
        'S1': -1000, 'B0yB': -2000, 'H0sf': 1000, 'P0sf': 1000, 'H0PD': 2500, 'H1fi': 1000, 'H1PS': -2000, 'C1yC': -1000, 'B0su': 500,
        'H1si': -2000, 'C0PS': 2500, 'B1mB': -1000, 'B1PB': -2000, 'H0vi': 1000, 'C1PB': -2000, 'H1su': 1000, 'O0gt': 500, 'S1su': 2000,
        'RLr': 1000, 'H1Ds': -2000, 'O1PB': -2000, 'B0PB': 2000, 'H0st': -2000, 'B1PS': 2500, 'B0PS': -500, 'C0yC': 1000, 'D1su': -1000, 'P0oh': 1000, 'H1dx': 2000, 'C0mC': 500,
        'P0ZZ': 1000, 'B1aB': -1000, 'C1si': 2000, 'D1PM': 1000, 'P0PM': -1000, 'H0PM': -2000, 'H0ZZ': 2000, 'H0PB': -2000, 'H1xh': -2000}
RUN = 320.0
CY, PCY, FIX, HOP, NEAR, GCY, SCY, SA = 0.83, 0.5, 55.0, 175.0, 165.0, 1.35, 3.2, 10.0
VB, LAM, PASSES = 1.8, 1000.0, 4


def _sb(n, d):
    return ("sbuf", [128, n], d)


SCRATCH = {"CK": _sb(CODE, H16), "X": _sb(NK, "bfloat16"), "S": _sb(NK, "float32"), "Si": _sb(A, "int32"),
           "XN": _sb(NK, "bfloat16"), "SN": _sb(NK, "float32"), "MW": _sb(400, "float32"), "MO": _sb(400, "float32"),
           "WK": _sb(NH * 3 * CODE, "int32"), "C2k": _sb(2 * GAP, "bfloat16"), "PGu": _sb(2 * LN, "uint16"),
           "Ds": _sb(NH * 2 * GAP, "bfloat16"), "Ku": _sb(LN, "uint16"), "YP": _sb(NH * 3 * GAP, H16),
           "sf": _sb(16 * 16, "float32"), "si": _sb(16 * 16, "int32"), "su": _sb(16 * 16, "uint16"), "sh": _sb(16 * 4, "bfloat16"),
           "cI": _sb(16, "int32"), "col": _sb(32, "float32"), "coli": _sb(16, "int32"), "PERM": _sb(5 * 128, "bfloat16"),
           "OH": _sb(16 * CODE, "bfloat16"), "IO": _sb(KDUM, "float32"), "MK": _sb(3 * CODE, "bfloat16"),
           "kr": _sb(LN, "uint16"), "EQ": _sb(12 * CODE, "bfloat16"), "MU": _sb(NH * MUH, H16), "MI": _sb(NH * MUH, H16)}
for _names, _n, _d in (("xg xh yB yC zrB zrC", 16 * LN, "bfloat16"), ("zeB zeC", LN, "bfloat16"), ("ZZ00 ZZ01 ZZ10 ZZ11", ZA + 3 * CODE, "bfloat16"),
                       ("Zi Zf D thrR ohj nw fit Lb Lr", LN, "bfloat16"), ("Ki vi Li", LN, "int32"), ("ohP ohG GB", LN, H16),
                       ("K20 thrK To Pf rr dl Kf", LN, "float32"), ("cJ c1 c2", 256, "float32"),
                       ("ZI ZW1 ZWd ZWp ZWq ZW2 Z8 NI BOw", 256, "bfloat16"), ("HI NF BO B4 B16 B2k CQ MK2 MK3", 128, "bfloat16"),
                       ("B5", 128, H16), ("TBL TB2 TT", 32, "float32"), ("PW", SPLIT, "float32")):
    for _x in _names.split():
        SCRATCH[_x] = _sb(_n, _d)
for _x in "dx gt aB mB aC mC ab2".split():
    SCRATCH[_x] = ("sbuf", [128, LN, 16], "bfloat16")
for _x, _n, _d in [("I", 24, "int32"), ("Z", 24, "bfloat16"), ("A", 128, "int32"), ("N", 512, "bfloat16"), ("S", 128, "float32"),
                   ("W0", 200 // N, "float32"), ("W1", 200 // N, "float32"), ("K", 24, "float32"), ("L", 48, "bfloat16"), ("U0", MUH // N, H16), ("U1", MUH // N, H16),
                   ("G", 2 * LN, "bfloat16")] + [("X%d" % _c, 512 // XCH, "bfloat16") for _c in range(XCH)]:
    SCRATCH["st" + _x] = ("dram", [N, 128, _n], _d)
    SCRATCH["ld" + _x] = ("dram", [N, 128, _n], _d)
SCRATCH["stP"] = ("dram", [128, 12], "int32")
SCRATCH["ldP"] = ("dram", [N, 128, 12], "int32")
for _b in ("PB0", "PB1", "PB2"):
    SCRATCH[_b] = ("psum", [128, 128, KG], "float32")
for _b in ("PS0", "PS1"):
    SCRATCH[_b] = ("psum", [128, 32, 16], "float32")
for _b in ("PD", "PM0", "PM1"):
    SCRATCH[_b] = ("psum", [128, 512], "float32")
ALL = dict(SCRATCH)
for _x in ("stI ldI stZ ldZ stP ldP" if HOMEH else "stU0 ldU0 stU1 ldU1 stG ldG MI MU xh").split():
    del SCRATCH[_x]
SEMAPHORES = ["ev", "es", "ep", "eg"] + ["d%d" % _i for _i in range(48)] + ["r%d" % _i for _i in range(12)] + ["l%d" % _i for _i in range(12)]
ESEM = {"v": "ev", "s": "es", "p": "ep", "g": "eg"}
REPORT = {}


def build(g, core, T, topo):
    rank = T.rank_of(core)
    ops, stg, cut, rnd = [], [0, ""], [0], [0]
    Q = {"v": g.vector, "s": g.scalar, "p": g.tensor, "g": g, "y": g.sync}
    T0, T1 = [0, SPLIT], [SPLIT, LN]
    LW = [T1[h] - T0[h] for h in range(NH)]
    NB = [n // 16 for n in LW]
    B0 = [n // 16 for n in T0]
    M0 = [0, 2 * SPLIT + 8]

    def dt(n):
        return SCRATCH[n][2]

    def a(n, c0=0, c1=None, st=None, p=None):
        c1 = SCRATCH[n][1][1] if c1 is None else c1
        ps = slice(None) if p is None else slice(p[0], p[1])
        cs = slice(c0, c1) if st is None else slice(c0, c1, st)
        return {"ap": T[n][ps, cs], "reg": [(n, c0, c1, 0, 1)], "n": len(range(c0, c1, st or 1)), "nm": n}

    def a3(n, r0, r1, c0=0, c1=None, st=1):
        c1 = SCRATCH[n][1][2] if c1 is None else c1
        return {"ap": T[n][:, r0:r1:st, c0:c1], "reg": [(n, r0, r1, c0, c1)], "n": len(range(r0, r1, st)) * (c1 - c0), "nm": n}

    def one(n, r0, r1, c):
        return {"ap": T[n][:, r0:r1, c], "reg": [(n, r0, r1, c, c + 1)], "n": r1 - r0, "nm": n}

    def ind(w, o):
        return {"ap": w["ap"].indirect(o["ap"]), "reg": w["reg"], "xr": o["reg"], "n": 16 * o["n"], "nm": w["nm"], "ind": 1}

    def d(ap, n):
        return {"ap": ap, "reg": [(n, 0, N, 0, 1)] if n else [], "n": 0, "nm": n}

    def val(x):
        return x["ap"] if isinstance(x, dict) else x

    def add(alts, outs, ins, **k):
        rd = [r for x in ins if isinstance(x, dict) for r in x["reg"] + x.get("xr", [])] + [r for x in outs for r in x.get("xr", [])]
        o = {"alts": alts, "w": [r for x in outs for r in x["reg"]], "r": rd, "st": stg[0], "tag": stg[1],
             "sub": stg[1] + (outs[0]["nm"] or "" if outs else "")[:2],
             "gn": sum(x["n"] for x in ins if isinstance(x, dict) and "ind" in x), "sn": sum(x["n"] for x in outs if "ind" in x)}
        o.update(k)
        p = ops[-1] if ops else o
        if "run" in o and p.get("run") == o["run"] and p["st"] == o["st"]:
            e = o["run"][0]
            (c0, f0), (c1, f1) = p["alts"][e], alts[e]
            if c0 + c1 <= RUN:
                p["alts"] = {e: (c0 + c1, lambda: f0() + f1())}
                p["w"], p["r"] = p["w"] + o["w"], p["r"] + o["r"]
                return len(ops) - 1
        ops.append(o)
        return len(ops) - 1

    def two(*xs):
        return all(dt(x["nm"]) in ("bfloat16", "float16", "uint16") for x in xs)

    def vcost(out, in0, per):
        if "ind" in in0:
            return 50 + GCY * in0["n"]
        if "ind" in out:
            return 50 + SCY * out["n"]
        return max(FIX, per * CY * in0["n"])

    def scost(out, in0):
        return vcost(out, in0, 1) + (15 if "ind" in in0 else SA)

    def tt(out, i0, i1, op, **k):
        ps = SCRATCH[i0["nm"]][0] == "psum" or SCRATCH[i1["nm"]][0] == "psum"
        add({"v": (vcost(out, i0, 1 if ps else 2), lambda: [g.vector.tensor_tensor(out["ap"], i0["ap"], i1["ap"], op)])}, [out], [i0, i1], **k)

    def ts(out, i0, s1, op0, s2=None, op1=None):
        if s2 is None:
            f = lambda: g.vector.tensor_scalar(out["ap"], i0["ap"], val(s1), None, op0)
        else:
            f = lambda: g.vector.tensor_scalar(out["ap"], i0["ap"], val(s1), val(s2), op0, op1)
        add({"v": (vcost(out, i0, 0.5 if two(out, i0) else 1), f)}, [out], [i0, s1, s2])

    def cp(out, i0, eng="vs"):
        alts = {"v": (vcost(out, i0, 0.5 if two(out, i0) else 1), lambda: g.vector.tensor_copy(out["ap"], i0["ap"]))}
        if "s" in eng:
            alts["s"] = (scost(out, i0), lambda: g.scalar.activation(out["ap"], i0["ap"], AF.Copy))
        add(alts, [out], [i0])

    def act(out, i0, fn, bias=0.0):
        add({"s": (scost(out, i0), lambda: g.scalar.activation(out["ap"], i0["ap"], fn, bias=val(bias)))}, [out], [i0, bias])

    def lin(out, i0, sc, bi):
        add({"v": (vcost(out, i0, 0.5 if two(out, i0) else 1), lambda: g.vector.tensor_scalar(out["ap"], i0["ap"], sc, val(bi), OP.mult, OP.add)),
             "s": (scost(out, i0), lambda: g.scalar.activation(out["ap"], i0["ap"], AF.Identity, bias=val(bi), scale=sc))}, [out], [i0, bi])

    def red(out, i0, op):
        add({"v": (vcost(out, i0, 1), lambda: g.vector.tensor_reduce(out["ap"], i0["ap"], AxisListType.X, op))}, [out], [i0])

    def scan(out, d0, d1, init, op0, op1):
        add({"v": (vcost(out, d0, 1), lambda: g.vector.tensor_tensor_scan(out["ap"], d0["ap"], d1["ap"], init, op0, op1))}, [out], [d0, d1])

    def mset(out, v):
        add({"v": (vcost(out, out, 0.5 if two(out) else 1), lambda: g.vector.memset(out["ap"], v))}, [out], [])

    def mm(out, l, r, st=True, sp=True):
        add({"p": (max(64, r["n"]) * PCY, lambda: [g.tensor.matmul(out["ap"], l["ap"], r["ap"], st, sp)])}, [out], [l, r], run=("p", out["nm"], cut[0]))

    def iota(out, pat, base, cm, **k):
        if dt(out["nm"]) == "int32":
            f = lambda: g.iota(out["ap"], pat, base, cm)
        else:
            f = lambda: g.iota(out["ap"], pat, base, cm, allow_small_or_imprecise_dtypes=True)
        add({"g": (130 + 2 * CY * out["n"], f)}, [out], [], **k)

    nd = [0]

    def dma(q, pairs, nbytes, behind=None, **k):
        sem = "d%d" % nd[0]
        nd[0] += 1

        def f():
            for o, i in pairs:
                Q[q].dma_start(o["ap"], i["ap"]).then_inc(T.sem[sem], 16)
        return add({q: ((600 if q == "g" else 160), f)}, [o for o, i in pairs] + ([d(None, behind)] if behind else []), [i for o, i in pairs],
                   sem=(sem, 16 * len(pairs)), lat=1800 + nbytes / 250.0, **k)

    peers = [r for r in range(N) if r != rank]
    far = [r for r in peers if topo.die(T.cores[r]) != topo.die(core)]
    near = [r for r in peers if r not in far]
    nr = [0]

    def exchange(names, nbytes, **kw):
        k = nr[0]
        nr[0] += 1
        per = 2 // len(names)
        trs = []
        for j, x in enumerate(names):
            st, ld = "st" + x, "ld" + x
            for cls, lst in ((0, far), (1, near)):
                for i, r in enumerate(lst):
                    en = topo.engines(core, T.cores[r])[cls::2]
                    m = 0
                    for e in en[2 * i + j * per:2 * i + (j + 1) * per]:
                        m |= 1 << e
                    rid, pid, _ = topo.addr(T.cores[r])
                    trs.append(RemoteDMATransfer(dst_ids=[DstId(rid=rid, pnc=pid)], dma_engine_mask=m, remote_sem=T.sem["r%d" % k],
                                                 src=T[st][r] if len(SCRATCH[st][1]) == 3 else T[st][:], dst=T[ld][rank]))
        tot = per * len(trs)
        s = add({"g": (1000, lambda: g.remote_dma_fused(trs, local_sem=T.sem["l%d" % k]))}, [], [d(None, "st" + x) for x in names],
                sem=("l%d" % k, tot), lat=2200 + nbytes / 200.0, **kw)
        add({}, [d(None, "ld" + x + "R") for x in names], [], sem=("r%d" % k, tot), lat=2500 + nbytes / 200.0, after=s)
        return s

    def land(x, r0=0, r1=128):
        y = d(T["ld" + x][:, r0:r1, :], "ld" + x)
        y["reg"] = y["reg"] + [("ld" + x + "R", 0, N, 0, 1)]
        return y

    def stage(x, src, r0=0, r1=128):
        st, ld, pr = "st" + x, "ld" + x, []
        if rank > 0:
            pr.append((d(T[st][0:rank, r0:r1, :], st), src(0, 16 * rank)))
        if rank < N - 1:
            pr.append((d(T[st][rank + 1:N, r0:r1, :], st), src(16 * (rank + 1), 16 * N)))
        return pr, [(d(T[ld][rank, r0:r1, :], ld), src(16 * rank, 16 * (rank + 1)))]

    def inp(t, c0, c1):
        return lambda r0, r1: d(t[r0:r1, c0:c1], None)

    def sbs(n, c0, c1):
        return lambda r0, r1: a(n, c0, c1, p=(r0, r1))

    xw = W // XCH
    xs = [stage("X%d" % c, inp(T.x0, c * xw, (c + 1) * xw)) for c in range(XCH)]
    a1, a2 = stage("A", inp(T.asc, 0, A))
    if HOMEH:
        dma("s", [(a("Ki"), d(T.kw[:], None)), (a("Zi"), d(T.z0[:], None)), (a("Li", p=(0, N)), d(T.l0[:], None))], 1e5)
        prev = dma("y", [(a("XN", X0, X0 + W), d(T.x0[:], None))], 2 ** 20)
        for c in range(XCH):
            prev = dma("y", xs[c][0] + xs[c][1], 2 ** 20 + 2 ** 20 / XCH * (c + 1), after=prev)
        prev = dma("y", a1 + a2, 2.5 * 2 ** 20, after=prev)
        sent = exchange(["X0"], 2 ** 19)
        for c in range(1, XCH):
            sent = exchange(["X%d" % c], 2 ** 19, after=sent)
        sent = exchange(["A"], 2 ** 19, after=sent)
        for c in range(XCH):
            prev = dma("y", [(a("X", X0 + c * xw, X0 + (c + 1) * xw), land("X%d" % c))], 2 ** 20 / XCH, after=prev)
        landed = dma("y", [(a("Si"), land("A"))], 2 ** 19, after=prev)
    else:
        k1, k2 = stage("I", inp(T.kw, 0, LN))
        l1, l2 = [(d(T.stP[:], "stP"), d(T.l0[:], None))], [(d(T.ldP[rank], "ldP"), d(T.l0[:], None))]
        z1, z2 = stage("Z", inp(T.z0, 0, LN))
        ps_ = dma("s", k1, 1e5)
        py_ = dma("y", xs[0][0], 2 ** 20 / XCH)
        ps_ = dma("s", l1 + z1, 1e5, after=ps_)
        for c in range(1, XCH):
            py_ = dma("y", xs[c][0], 2 ** 20 / XCH * (c + 1), after=py_)
        ps_ = dma("s", k2 + l2 + z2, 1e5, after=ps_)
        for c in range(XCH):
            ps_ = dma("s", xs[c][1], 2 ** 20, after=ps_)
        sent = exchange(["I"], 1e5)
        for c in range(XCH):
            sent = exchange(["X%d" % c], 2 ** 20 / XCH, after=sent)
        sent = exchange(["Z", "P"], 1e5, after=sent)
        dma("s", a1 + a2, 2 ** 19, "stX0")
        sent = exchange(["A"], 2 ** 19, after=sent)
        dma("y", [(a("Ki"), land("I"))], 1e5)
        dma("y", [(a("Zi"), land("Z"))], 1e5)
        dma("y", [(a("Li", p=(0, N)), land("P", 16 * rank, 16 * rank + 16))], 1e5)
        for c in range(XCH):
            dma("y", [(a("X", X0 + c * xw, X0 + (c + 1) * xw), land("X%d" % c))], 2 ** 20 / XCH)
        dma("y", [(a("Si"), land("A"))], 2 ** 19)

    def col(i):
        return a("col", i, i + 1)

    def small(buf):
        return lambda i, h=None: a(buf, 16 * i, 16 * i + 12) if h is None else a(buf, 16 * i + B0[h], 16 * i + B0[h] + NB[h])
    sf, si, su, sh = small("sf"), small("si"), small("su"), small("sh")

    def wide(buf, i, h, j0, j1, per=1):
        return a(buf, 16 * (i + per * h) + j0 * NB[h], 16 * (i + per * h) + j1 * NB[h])
    PID, CI_, CQ16, CW, CPW, CI16, AM, CP128, CZ8, CUP, C40, CPQ, PC = 0, 1, 2, 3, 4, 6, 7, 8, 9, 10, 11, 12, 16
    iota(a("coli", 0, 1), [[0, 1]], 0, 1)
    iota(a("cJ"), [[1, 256]], 0, 0)
    cp(col(PID), a("coli", 0, 1), "v")
    ts(a("coli", 1, 2), a("coli", 0, 1), 15, OP.bitwise_and)
    cp(col(CI_), a("coli", 1, 2), "v")
    tt(col(CQ16), col(PID), col(CI_), OP.subtract)
    ts(col(CP128), col(PID), 128.0, OP.add)
    ts(col(CW), col(CI_), 15.0, OP.mult, 7.0, OP.add)
    ts(col(CI16), col(CI_), 16.0, OP.mult)
    ts(col(CZ8), col(PID), 16.0, OP.mult, 128.0, OP.add)
    mset(col(AM), 1024.0)
    for c in range(2):
        ts(a("ZI", 128 * c, 128 * c + 128), a("cJ", 0, 128), col(PID), OP.is_equal)
        ts(a("ZW1", 128 * c, 128 * c + 128), a("cJ", 0, 128), col(CQ16), OP.is_equal)
    I = a("ZI", 0, 128)
    ts(a("NI"), a("ZI"), -1.0, OP.mult)
    NI = a("NI", 0, 128)
    for n, v in (("HI", 0.5), ("NF", -2.0 ** 23)):
        ts(a(n), I, v, OP.mult)
    mset(a("CQ"), -0.25)
    ts(a("OH", 0, 16), a("cJ", 0, 16), col(CI_), OP.is_equal)
    mset(a("c1", 0, SPLIT), 2.0)
    mset(a("c2", 0, SPLIT), 0.0)
    scan(a("PW"), a("c1", 0, SPLIT), a("c2", 0, SPLIT), 2.0 ** 12, OP.mult, OP.add)
    mset(a("c1", 128, 144), 0.5)
    scan(a("TBL", 0, 16), a("c1", 128, 144), a("c2", 0, 16), 131072.0, OP.mult, OP.add)
    cp(a("TBL", 16, 32), a("TBL", 0, 16), "v")
    cp(a("TB2", 0, 16), a("cJ", 0, 16), "v")
    cp(a("TB2", 16, 32), a("cJ", 0, 16), "v")
    mset(col(C40), -40.0)
    mset(a("c1", 144, 160), 2.0 ** -8)
    scan(a("TT", 0, 16), a("c1", 144, 160), a("c2", 0, 16), 2.0 ** 68, OP.mult, OP.add)
    tt(a("c2", 176, 192), a("OH", 0, 16), a("TT", 0, 16), OP.mult)
    red(col(CPQ), a("c2", 176, 192), OP.add)
    mset(a("TT", 15, 16), 2.0 ** 68)
    cp(a("TT", 16, 32), a("TT", 0, 16), "v")
    mset(a("C2k", 0, GAP), 0.0)
    mset(a("C2k", GAP, 2 * GAP), 2048.0)
    tt(a("c2", 128, 144), a("OH", 0, 16), a("TBL", 0, 16), OP.mult)
    red(col(CPW), a("c2", 128, 144), OP.add)
    tt(a("c2", 144, 160), a("OH", 0, 16), a("PW", 0, 16), OP.mult)
    red(col(CUP), a("c2", 144, 160), OP.add)
    ts(a("ZWp"), a("ZW1"), col(CPW), OP.mult, 0.5, OP.mult)
    for n, v in (("ZWd", -2048.0), ("ZW2", 4096.0), ("ZWq", col(CPQ))):
        ts(a(n), a("ZW1"), v, OP.mult)
    ts(a("Z8"), a("cJ"), col(CZ8), OP.is_equal)
    ts(a("c1", 0, 128), a("cJ", 0, 128), col(CQ16), OP.subtract, 0.0, OP.is_ge)
    ts(a("c2", 0, 128), a("cJ", 0, 128), col(CQ16), OP.subtract, 16.0, OP.is_lt)
    tt(a("BO"), a("c1", 0, 128), a("c2", 0, 128), OP.mult)
    for c in range(2):
        ts(a("BOw", 128 * c, 128 * c + 128), a("BO"), col(CW), OP.mult)
    for n, c, v in (("B4", 0, 4.0), ("B16", 112, 16.0), ("B5", 112, 5.0)):
        ts(a(n), a("BOw", c, c + 128), v, OP.mult)
    ts(a("B2k"), a("BO"), 2048.0, OP.mult)
    ts(a("c1", 160, 165), a("cJ", 0, 5), col(CI_), OP.add)
    ts(a("cI", 0, 5), a("c1", 160, 165), -2.0, OP.add, 0.2, OP.mult)
    ts(a("c2", 160, 165), a("cI", 0, 5), -5.0, OP.mult)
    tt(a("c1", 160, 165), a("c1", 160, 165), a("c2", 160, 165), OP.add)
    ts(a("c1", 160, 165), a("c1", 160, 165), -16.0, OP.mult, col(CP128), OP.add)
    ts(a("cI", 0, 5), a("c1", 160, 165), -16.0, OP.add)
    ts(a("cI", 0, 5), a("cI", 0, 5), 127, OP.bitwise_and)
    cp(a("col", PC, PC + 5), a("cI", 0, 5), "v")
    for c in range(5):
        ts(a("PERM", 128 * c, 128 * c + 128), a("cJ", 0, 128), col(PC + c), OP.is_equal, float(CODE), OP.mult)
    iota(a("rr", 0, CODE), [[256, CODE // 16], [1, 16]], 0, 0)
    ts(a("CK"), a("rr", 0, CODE), col(CI16), OP.add)
    DUM, THR, TMP, THE, U1, KEY, NN, CC, CNT, CON, LL, WGT = 0, 1, 2, 4, 5, 6, 7, 8, 9, 10, 11, 12
    ts(sf(TMP), a("cJ", 0, 12), 16.0, OP.mult, col(CI_), OP.add)
    ts(sf(DUM), sf(TMP), float(KDUM), OP.add)
    cp(sh(0), sf(TMP), "v")
    cp(su(0), a("cJ", 0, 12), "v")
    mset(si(0), 0)
    for h in range(NH):
        for c in range(3 if LW[h] < CODE else 0):
            mset(a("WK", CODE * (3 * h + c) + LW[h], CODE * (3 * h + c + 1)), 0)
    mset(a("YP"), 0.0)
    mset(a("MW"), 0.0)
    if HOMEH:
        mset(a("MU"), 0.0)
    mset(a("sf", 16 * THR, 16 * THR + 16), 0.0)
    for n in ("ZZ00", "ZZ01", "ZZ10", "ZZ11"):
        mset(a(n, ZA - GAP), 0.0)
    c = 16
    while c < 16 * CODE:
        cp(a("OH", c, 2 * c), a("OH", 0, c), "v")
        c *= 2
    ts(a("MK"), a("OH", 0, 3 * CODE), -1.0, OP.add, FAR, OP.mult)
    ts(a("c1", 0, CODE), a("OH", 0, CODE), 2048.0 + X0, OP.mult)
    tt(a("MK2"), a("c1", 0, CODE), a("MK", 0, CODE), OP.add)
    tt(a("c2", 0, SPLIT), a("OH", 0, SPLIT), a("PW"), OP.mult)
    ts(a("c2", 128, 128 + SPLIT), a("MK", 0, SPLIT), 0.5 * FAR, OP.mult)
    tt(a("c2", 0, SPLIT), a("c2", 128, 128 + SPLIT), a("c2", 0, SPLIT), OP.subtract)
    ts(a("MK3", 0, SPLIT), a("c2", 0, SPLIT), 2.0, OP.mult)
    ts(sf(WGT, 0), a("PW", 0, SPLIT, 16), col(CUP), OP.mult, 2.0 ** -13, OP.mult)

    def numbers(after):
        for c in range(0, KDUM, 856):
            iota(a("IO", c, c + 856), [[1, 856]], c, 0, after=after)
    if not HOMEH:
        numbers(sent)

    def SH(n, s):
        return a(n, 128 - 16 * (s % N), 256 - 16 * (s % N))

    def WW(n, s, i):
        return a(n, 128 - 16 * (s % N) - i, 256 - 16 * (s % N) - i)

    def hs(n, h):
        return a(n, T0[h], T1[h])

    def all16(n, h):
        return a(n, 16 * T0[h], 16 * T1[h])

    def osum(out, mat, s, src, h, first=True, last=True):
        cut[0] += 1
        for i in range(16):
            mm(out, WW(mat, s, i), a3(src, T0[h] + i, T1[h], st=16), first and i == 0, last and i == 15)
        cut[0] += 1

    def diag(out, ps, r0, r1, terms, mask):
        mm(a3(ps, r0, r1), I, mask, True, False)
        for j, (q0, q1, l, r) in enumerate(terms):
            cut[0] += j == 0 or (r["nm"] == "EQ" and l["nm"] == "BO")
            mm(a3(ps, q0, q1), l, r, False, j == len(terms) - 1)
        red(out, a3(ps, r0, r1), OP.max)

    def shift(pm, c, sign, src, n, h, first=True):
        for m in range(5):
            f = (m - T0[h]) % 5
            mm(a(pm, c + f, c + n, 5), SH("ZI", sign * (1 + m)), src(f, n, 5), first, first or m == 4)

    nb = [0]

    def sub(src, h, kg, zz, pos, neg):
        nb[0] += 1
        b = ("PB0", "PB1", "PB2")[nb[0] % 3]
        for kk in range(KG):
            o, k = one(b, 0, LW[h], kk), kg * KG + kk
            mm(o, pos, a(src, 16 * T0[h] + k, 16 * T1[h], 16), True, False)
            mm(o, neg, zz, False, True)
        return a3(b, 0, LW[h])

    def big(n, h, kg):
        return a3(n, T0[h], T1[h], kg * KG, (kg + 1) * KG)

    def words(dst, h, src, lst, base, then=None):
        for c in range(0, LW[h], PIECE):
            c0, c1 = T0[h] + c, T0[h] + c + PIECE
            o, i = a(dst, 16 * c0, 16 * c1), ind(a(src, X0, X0 + W), a(lst, base + c, base + c + PIECE))
            if then:
                tt(o, i, a("zr" + then[1], 16 * c0, 16 * c1), OP.subtract)
                act(a3(then, c0, c1), o, AF.Abs)
            else:
                cp(o, i)

    def fused(h, j):
        return "BC"[j] + str(h) in FUSE and (rnd[0] > 0 or not HOMEH)

    def repeat(h, j, nxt=1):
        pm, x, zw = "PM%d" % h, "BC"[j], "ZZ%d%d" % ((rnd[0] + nxt) % 2, h)
        for m in range(5):
            f = (m - T0[h]) % 5
            mm(a(pm, f, LW[h], 5), SH("ZI", 1 + j + m), a(zw, ZA + f, ZA + LW[h], 5))
        cp(hs("ze" + x, h), a(pm, 0, LW[h]))
        for k in range(16):
            o, i = a("zr" + x, 16 * T0[h] + k, 16 * T1[h], 16), hs("ze" + x, h)
            o["reg"] = [("zr" + x, 16 * T0[h], 16 * T1[h], k, k + 1)]
            add({"g": (170 + 2 * CY * LW[h], lambda o=o, i=i: g.affine_select(o["ap"], i["ap"], [[0, LW[h]]], OP.is_ge, 0.0, 1, 0))}, [o], [i], after=sent)

    def halve(out, pm, c, x, y, wy, h):
        o = a(pm, c, c + LW[h])
        mm(o, I, a("CQ", 0, LW[h]), True, False)
        mm(o, wy, y, False, False)
        cut[0] += 1
        mm(o, a("HI"), x, False, True)
        ts(out, o, ROUND, OP.add, ROUND, OP.subtract)

    def bounds():
        cp(a("thrK"), ind(a("sf", 16 * THR, 16 * THR + 16), su(0)))

    def powers():
        cp(a("thrR"), ind(a("TBL"), su(1)))
        diag(sf(THR), "PS0", 0, 12, [(0, 12, I, a("thrR"))], a("MK", 0, LN))

    def zz(h, c, nxt=0):
        if nxt and rnd[0] == RO - 1:
            return hs("Zf", h)
        return a("ZZ%d%d" % ((rnd[0] + nxt) % 2, h), ZA + c * CODE, ZA + c * CODE + LW[h])

    def uz(h, c0, c1, st=None):
        if HOMEH and rnd[0] == 0:
            return a("MI", MUH * h + c0, MUH * h + c1, st)
        return a("ZZ%d%d" % (rnd[0] % 2, h), ZA - GAP + c0, ZA - GAP + c1, st)

    def yp(h, c0, c1, st=None):
        return a("YP", 3 * GAP * h + c0, 3 * GAP * h + c1, st)

    def wk(h, c):
        return a("WK", CODE * (3 * h + c), CODE * (3 * h + c) + LW[h])

    def ds(h, c=0):
        if c and fused(h, 0):
            return hs("zeB", h)
        return a("Ds", 2 * GAP * h + GAP * c, 2 * GAP * h + GAP * c + LW[h])

    def mu(n, h, c, w):
        return a(n, MUH * h + c, MUH * h + c + w)

    cp(a("Lb", p=(0, N)), a("Li", p=(0, N)), "v")
    for i in range(16):
        mm(a("PM0", 0, 12), a("Z8", 128 - i, 256 - i, p=(0, N)), a("Lb", i, LN, 16, p=(0, N)), i == 0, i == 15)
    cp(su(1), a("PM0", 0, 12), "v")
    cp(a("Ku"), a("Ki"), "v")
    if not HOMEH:
        cp(sf(LL), a("PM0", 0, 12), "v")
        cp(a("To"), ind(a("TT"), su(1)))
    for h in range(NH):
        if HOMEH:
            cp(mu("MU", h, 3 * GAP, NB[h]), a("PM0", B0[h], B0[h] + NB[h]), "v")
            cp(mu("MU", h, GAP, LW[h]), hs("Zi", h), "v")
            ts(mu("MU", h, 2 * GAP, LW[h]), hs("Ki", h), -2048.0, OP.add)
        else:
            cp(wk(h, 1), hs("Ki", h), "v")
            cp(zz(h, 0), hs("Zi", h), "v")
            for j in range(2):
                if fused(h, j):
                    repeat(h, j, 0)
    powers()
    bounds()
    for c in range(2):
        cp(a("S", 512 * c, 512 * c + 512), a("Si", 512 * c, 512 * c + 512))

    def speaker(h, src, xg, z, us):
        ps, pm, n = "PS%d" % h, "PM%d" % h, NB[h]
        words(xg, h, src, "Ku", T0[h])
        for kg in range(16 // KG):
            act(big("dx", h, kg), sub(xg, h, kg, z, I, NI), AF.Abs)
            ts(big("gt", h, kg), big("dx", h, kg), 40.0, OP.is_gt)
        osum(a(pm, 0, LW[h]), "ZWp", 0, "gt", h)
        mm(a3(ps, 0, n), I, a("CK", 0, LW[h]), True, False)
        osum(a3(ps, 0, n), "ZWd", 0, "dx", h, False, False)
        tt(hs("fit", h), a(pm, 0, LW[h]), hs("thrK", h), OP.is_lt)
        mm(a3(ps, 0, n), a("NF"), hs("fit", h), False, True)
        red(wide("si", 2, h, 0, 1), a3(ps, 0, n), OP.min)
        ts(wide("si", 2, h, 1, 2), wide("si", 2, h, 0, 1), 2047, OP.bitwise_and)
        cp(su(2, h), wide("si", 2, h, 1, 2))
        tt(us, ind(all16(xg, h), su(2, h)), z, OP.subtract)

    told = [sent]

    def first(h):
        speaker(h, "XN", "xh", hs("Zi", h), mu("MU", h, 0, LW[h]))
        u1, u2 = stage("U%d" % h, sbs("MU", MUH * h, MUH * (h + 1)))
        dma("s", u1 + u2, 1e5)
        told[0] = exchange(["U%d" % h], 1e5, after=told[0])
        dma("s", [(mu("MI", h, 0, MUH), land("U%d" % h))], 1e5)
        cp(zz(h, 0), uz(h, GAP, GAP + LW[h]))
        lin(wk(h, 1), mu("MI", h, 2 * GAP, LW[h]), 1.0, 2048.0)
        cp(sf(LL, h), mu("MI", h, 3 * GAP, NB[h]))
        cp(su(1, h), mu("MI", h, 3 * GAP, NB[h]), "v")
        if "H%d" % h == [w for w in ORDER.split() if w[0] == "H"][-1]:
            cp(a("To"), ind(a("TT"), su(1)))
            powers()
            g1, g2 = stage("G", sbs("xh", 0, 16 * LN))
            dma("y", g1 + g2, 2 ** 20, after=landed)
            exchange(["G"], 2 ** 20, after=told[0])
            numbers(told[0])
            dma("y", [(a("xg"), land("G"))], 2 ** 20)

    def home(h, last):
        ps, pm, db, n, lw = "PS%d" % h, "PM%d" % h, 2 * T0[h], NB[h], LW[h]
        us = uz(h, 0, lw)
        if HOMEH and rnd[0] == 0:
            first(h)
        else:
            speaker(h, "X", "xg", zz(h, 0), us)
        lin(hs("K20", h), wk(h, 1), 20.0, 0.0)
        w = lw if fused(h, 0) else GAP + lw
        shift(pm, 0, 1, lambda c0, c1, st: uz(h, c0, c1, st), w, h)
        act(a("Ds", 2 * GAP * h, 2 * GAP * h + w), a(pm, 0, w), AF.Abs)
        terms = [(n, 2 * n, a("B4"), ds(h)), (2 * n, 3 * n, a("B16"), ds(h)), (2 * n, 3 * n, a("B5"), ds(h)), (3 * n, 4 * n, a("B2k"), ds(h))]
        diag(wide("si", 4, h, 0, 3, 2), ps, n, 4 * n, terms, a("MK", 0, 3 * lw))
        for j in range(2):
            mm(a("PD", db + lw * j, db + lw * (j + 1)), SH("ZI", j), ds(h))
        ts(wide("si", 8, h, 0, 2), wide("si", 4, h, 0, 2, 2), 2, OP.arith_shift_right, A - 1, OP.bitwise_and)
        cp(wide("su", 4, h, 0, 2), wide("si", 8, h, 0, 2))
        cp(a("PGu", db, db + 2 * lw), ind(a("S" if rnd[0] else "Si", 0, A), wide("su", 4, h, 0, 2)), "vs" if rnd[0] else "v")
        act(hs("D", h), us, AF.Abs)
        mm(a(pm, 0, lw), SH("BOw", 0), hs("D", h))
        tt(hs("vi", h), a(pm, 0, lw), hs("K20", h), OP.add)
        ts(wk(h, 0), hs("vi", h), 2, OP.arith_shift_right, W - 1, OP.bitwise_and)
        halve(zz(h, 1), pm, GAP, us, uz(h, GAP, GAP + lw), I, h)
        ts(yp(h, GAP, GAP + 2 * lw), a("PGu", db, db + 2 * lw), -2048.0, OP.add)
        lin(hs("Pf", h), yp(h, GAP, GAP + lw), 1.0, 2048.0)
        mm(a(pm, 2 * GAP, 2 * GAP + lw), SH("ZI", -1), yp(h, GAP + lw, GAP + 2 * lw))
        cp(hs("GB", h), a(pm, 2 * GAP, 2 * GAP + lw))

    def look(h, j):
        ps, n = "PS%d" % h, NB[h]
        y, aa, mx = (("yB", "aB", "mB"), ("yC", "aC", "mC"))[j]
        c = 2 * T0[h] + LW[h] * j
        words(y, h, "X", "PGu", c, aa if fused(h, j) else None)
        for kg in range(16 // KG):
            if not fused(h, j):
                act(big(aa, h, kg), sub(y, h, kg, ds(h, 1), I, SH("NI", j)), AF.Abs)
            for k in range(kg * KG, (kg + 1) * KG):
                tt(one(mx, T0[h], T1[h], k), one(aa, T0[h], T1[h], k), a("PD", c, c + LW[h]), OP.max, run=("v", mx, kg))
        o = a3(ps, (1 + j) * n, (2 + j) * n)
        mm(o, I, a("CK", 0, LW[h]), True, False)
        osum(o, "ZWd", -j, aa, h, False, False)
        osum(o, "ZW2", -j, mx, h, False, True)
        red(wide("si", 10, h, j, j + 1), o, OP.min)
        ts(wide("si", 12, h, j, j + 1), wide("si", 10, h, j, j + 1), 2047, OP.bitwise_and)
        cp(wide("su", 6, h, j, j + 1), wide("si", 12, h, j, j + 1))

    def msg(h, c0, c1):
        return a("MW", M0[h] + c0, M0[h] + c1)

    def partner(h, last):
        ps, pm, n, lw = "PS%d" % h, "PM%d" % h, NB[h], LW[h]
        me, jl = wide("si", 10, h, 0, 1), wide("su", 6, h, 0, 1)
        tt(sf(TMP, h), me, wide("si", 4, h, 2, 3, 2), OP.subtract)
        lin(sf(THE, h), me, 1.0, col(AM))
        ts(sf(CC, h), sf(TMP, h), 800.0 * 2048, OP.is_lt, 1.0, OP.add)
        ts(sf(TMP + 1, h), sf(TMP, h), 800.0 * 2048, OP.is_lt, float(KCON), OP.mult)
        if fused(h, 0):
            tt(yp(h, 0, lw), ind(all16("yB", h), jl), ds(h, 1), OP.add)
        else:
            cp(yp(h, 0, lw), ind(all16("yB", h), jl))
        cp(hs("ohj", h), ind(a("OH"), jl))
        tt(hs("ohP", h), hs("ohj", h), yp(h, GAP, GAP + lw), OP.mult)
        diag(sf(U1, h), ps, 3 * n, 4 * n, [(3 * n, 4 * n, a("BO"), hs("ohP", h))], a("MK2", 0, lw))
        tt(sf(U1, h), sf(U1, h), sf(TMP + 1, h), OP.max)
        c = 512 - 2 * GAP
        mm(a(pm, c, c + GAP + lw), I, a("C2k", 0, GAP + lw), True, False)
        shift(pm, c, -1, lambda c0, c1, st: yp(h, c0, c1, st), GAP + lw, h, False)
        cp(zz(h, 2), a(pm, c, c + lw))
        tt(hs("dl", h), a(pm, c + GAP, c + GAP + lw), wk(h, 1), OP.subtract)
        halve(msg(h, 0, lw) if last else hs("nw", h), pm, 0, yp(h, 0, lw), ds(h), a("HI"), h)

    def decide(h, last):
        pm, n, lw = "PM%d" % h, NB[h], LW[h]
        tt(sh(2, h), wide("si", 10, h, 1, 2), sf(THE, h), OP.is_ge)
        tt(sh(3, h), sf(CC, h), sh(2, h), OP.mult)
        tt(sf(U1, h), sf(U1, h), sh(2, h), OP.mult)
        tt(su(3, h), sf(U1, h), wide("si", 8, h, 0, 1), OP.max)
        tt(sf(KEY, h), sf(U1, h), wide("si", 8, h, 0, 1), OP.max)
        cp(hs("kr", h), ind(a("IO"), su(3, h)))
        c0 = 2 * GAP
        mm(a(pm, c0, c0 + n), I, a("sh", 0, n), True, False)
        cls = [c for c in range(5) if (c - B0[h]) % 5 < n]
        for c in cls:
            f = (c - B0[h]) % 5
            mm(a(pm, c0 + f, c0 + n, 5), a("PERM", 128 * c, 128 * c + 128), a("sh", 48 + B0[h] + f, 48 + B0[h] + n, 5), False, c == cls[-1])
        cp(su(8, h), a(pm, c0, c0 + n))
        zw = "ZZ%d%d" % (rnd[0] % 2, h)
        cp(zz(h, 0, 1), ind(a(zw, ZA, ZA + 3 * CODE), su(8, h)))
        tt(hs("ohG", h), ind(a("OH"), wide("su", 6, h, 1, 2)), hs("GB", h), OP.mult)
        mm(a(pm, GAP, GAP + lw), NI, yp(h, GAP, GAP + lw), True, False)
        mm(a(pm, GAP, GAP + lw), a("BO"), hs("ohG", h), False, True)
        tt(hs("rr", h), a(pm, GAP, GAP + lw), hs("ohj", h), OP.mult)
        if last:
            tt(msg(h, lw, 2 * lw), hs("rr", h), hs("Pf", h), OP.add)
        for j in range(0 if last else 2):
            if "BC"[j] + str(h) in FUSE:
                repeat(h, j)

    def off(h, last):
        o = a("PM%d" % h, 384, 384 + LW[h])
        for kg in range(16 // KG):
            act(big("ab2", h, kg), sub("xg", h, kg, zz(h, 2), I, NI), AF.Abs)
            if OFFMODE.split()[h][kg] == "v":
                ts(big("gt", h, kg), big("ab2", h, kg), 40.0, OP.is_gt)
            else:
                act(big("gt", h, kg), big("ab2", h, kg), AF.Relu, col(C40))
        for k in range(16):
            mm(o, WW("ZWq", 0, k), one("gt", T0[h], T1[h], k), k == 0, k == 15)
        tt(o, o, hs("To", h), OP.is_ge)
        tt(o, o, hs("dl", h), OP.mult)
        tt(wk(h, 2), o, wk(h, 1), OP.add)

    def players(h, last):
        cp(hs("Kf" if last else "Ku", h), ind(a("WK", 3 * CODE * h, 3 * CODE * (h + 1)), su(8, h)), "v")
        if not last:
            cp(wk(h, 1), hs("Ku", h), "v")

    def settle(h, last):
        ps, terms, n, lw = "PS%d" % h, [], NB[h], LW[h]
        for b in range(n):
            e = CODE * (B0[h] + b)
            ts(a("EQ", e, e + 16 * (b + 1)), a("kr", T0[h], T0[h] + 16 * (b + 1)), a("sf", 16 * KEY + B0[h] + b, 16 * KEY + B0[h] + b + 1),
               OP.is_equal, a("sf", 16 * WGT + b, 16 * WGT + b + 1), OP.mult)
            terms.append((0, b + 1, a("BO"), a("EQ", e, e + 16 * (b + 1))))
        diag(sf(NN, h), ps, 0, n, terms, a("MK3", 0, lw))
        tt(sf(NN, h), sf(NN, h), sf(DUM, h), OP.min)
        if last:
            tt(msg(h, 2 * lw, 2 * lw + n), sf(NN, h), sf(KEY, h), OP.max)
        else:
            tt(su(10, h), sf(NN, h), sf(KEY, h), OP.max)

    def write(h, last):
        if not last:
            cp(ind(a("X"), su(10, h)), hs("nw", h), "v")
            tt(ind(a("S"), su(10, h)), hs("rr", h), hs("Pf", h), OP.add)

    def carry(last):
        ts(sf(CON), su(8), float(2 * CODE), OP.is_ge)
        tt(sf(LL), sf(LL), sf(CON), OP.add)
        cp(su(1), sf(LL))
        if last:
            cp(a("Lr"), ind(a("TB2"), su(1)))
            return
        cp(a("To"), ind(a("TT"), su(1)))
        lin(sf(CON), sf(CON), -0.5, 1.0)
        tt(sf(THR), sf(THR), sf(CON), OP.mult)
        ts(sf(CON), sf(THR), 1.5, OP.is_lt, 65535.0, OP.mult)
        tt(sf(THR), sf(THR), sf(CON), OP.add)
        bounds()
        mm(a("PM1", 112, 124), a("BO"), sh(2))
        red(a("sf", 16 * CNT, 16 * CNT + 1), a("PM1", 112, 124), OP.add)
        tt(a("si", 0, 1), a("si", 0, 1), a("sf", 16 * CNT, 16 * CNT + 1), OP.subtract)
        ts(a("si", 4, 5), a("si", 0, 1), 31, OP.bitwise_and)
        lin(col(AM), a("si", 4, 5), 2048.0, 1024.0)

    steps = {"H": home, "B": lambda h, last: look(h, 0), "C": lambda h, last: look(h, 1), "P": partner, "D": decide, "O": off,
             "S": settle, "W": write, "K": players}
    for r in range(RO):
        rnd[0] = r
        last = r == RO - 1
        if last:
            stg[1] = "X"
            n1, n2 = stage("N", sbs("X", X0, X0 + W))
            s1, s2 = stage("S", sbs("S", 0, A))
            dma("y", n1, 2 ** 20)
            dma("y", s1, 2 ** 20)
            dma("y", n2 + s2, 2 ** 20)
            exchange(["N"], 2 ** 20)
            exchange(["S"], 2 ** 20)
            dma("y", [(a("XN", X0, X0 + W), land("N"))], 2 ** 20)
            dma("y", [(a("SN", 0, A), land("S"))], 2 ** 20)
        for w in ORDER.split():
            stg[0], stg[1] = stg[0] + 1, w
            steps[w[0]](int(w[1]), last)
        stg[1] = "R"
        carry(last)

    stg[1] = "E"
    for h in range(NH):
        w1, w2 = stage("W%d" % h, sbs("MW", M0[h], M0[h] + 200))
        dma("y", w1, 1e5)
        dma("y", w2, 1e5)
        exchange(["W%d" % h], 1e5)
        dma("y", [(a("MO", M0[h], M0[h] + 200), land("W%d" % h))], 1e5)
    k1, k2 = stage("K", sbs("Kf", 0, LN))
    z1, z2 = stage("L", sbs("Zf", 0, LN), 0, 64)
    l1, l2 = stage("L", sbs("Lr", 0, LN), 64, 128)
    dma("s", k1 + z1 + l1, 2e5)
    dma("s", k2 + z2 + l2, 2e5)
    exchange(["K", "L"], 2e5)
    for h in range(NH):
        cp(su(10, h), a("MO", M0[h] + 2 * LW[h], M0[h] + 2 * LW[h] + NB[h]), "v")
    for h in range(NH):
        cp(ind(a("XN"), su(10, h)), a("MO", M0[h], M0[h] + LW[h]), "v")
    dma("y", [(d(T.yx[:], None), a("XN", X0, X0 + W))], 2 ** 20)
    for h in range(NH):
        cp(ind(a("SN"), su(10, h)), a("MO", M0[h] + LW[h], M0[h] + 2 * LW[h]), "v")
    dma("s", [(d(T.ya[:], None), a("SN", 0, A))], 2 ** 20)
    dma("s", [(d(T.yk[:], None), land("K")), (d(T.yz[:], None), land("L", 0, 64))], 2e5)
    dma("g", [(d(T.yl[:], None), land("L", 64, 68))], 1e4)
    return ops, Q


def depend(ops):
    recs, banks = {}, {}
    for i, o in enumerate(ops):
        dp, od = set(), set()
        eng = list(o["alts"])[0] if len(o["alts"]) == 1 else i
        for wr, regs in ((0, o["r"]), (1, o["w"])):
            for n, r0, r1, c0, c1 in regs:
                if n[:2] == "zr" and not wr:
                    c1 = 16
                if n in SCRATCH and SCRATCH[n][0] == "psum":
                    st = banks.setdefault(n, [None, [], []])
                    if st[0] != eng:
                        st[0], st[1], st[2] = eng, [], [x[0] for x in st[1]]
                    dp.update(st[2])
                    if eng == "p":
                        od.update(x[0] for x in st[1][-1:])
                    else:
                        dp.update(x[0] for x in st[1] if (wr or x[5]) and x[1] < r1 and r0 < x[2] and x[3] < c1 and c0 < x[4])
                    st[1].append((i, r0, r1, c0, c1, wr))
                    continue
                lst = recs.setdefault(n, [])
                dp.update(x[0] for x in lst if (wr or x[5]) and x[1] < r1 and r0 < x[2] and x[3] < c1 and c0 < x[4])
                if wr:
                    lst[:] = [x for x in lst if not (r0 <= x[1] and x[2] <= r1 and c0 <= x[3] and x[4] <= c1)]
                lst.append((i, r0, r1, c0, c1, wr))
        dp.discard(i)
        od.discard(i)
        if "after" in o:
            od.add(o["after"])
        o["dp"], o["od"] = dp, od - dp


def place(ops, seq, pre, keep):
    gaps = {}
    t0, c0, eng = [0.0] * len(ops), [0.0] * len(ops), [None] * len(ops)
    for i in seq:
        t, best = 0.0, None
        if not ops[i]["alts"]:
            t = max([t0[j] + c0[j] + w for j, w in pre[i]] + [0.0])
        for e, al in ops[i]["alts"].items():
            if keep[i] and keep[i] != e:
                continue
            t = max([t0[j] + c0[j] + (NEAR if w == HOP and eng[j] == e else w) for j, w in pre[i]] + [0.0])
            s, c = gaps.setdefault(e, []), al[0]
            lo, hi = 0, len(s)
            while lo < hi:
                mid = (lo + hi) // 2
                if s[mid][1] <= t:
                    lo = mid + 1
                else:
                    hi = mid
            x = t
            while lo < len(s) and s[lo][0] < x + c:
                x = max(x, s[lo][1])
                lo += 1
            v = x + c * (VB if e == "v" else 1)
            if best is None or v < best[0]:
                best = (v, e, x, c, lo)
        if best:
            _, eng[i], t, c0[i], k = best
            gaps[eng[i]].insert(k, (t, t + c0[i]))
        t0[i] = t
    return t0, c0, eng


def ordered(keys, pre):
    keys = list(keys)
    for i in pre:
        for j, w in pre[i]:
            keys[i] = max(keys[i], keys[j])
    pos = {i: k for k, i in enumerate(pre)}
    return sorted(pre, key=lambda i: (keys[i], pos[i]))


def schedule(ops):
    n = len(ops)
    if REPORT.get("n") != n:
        pre, post = {i: [] for i in range(n)}, {i: [] for i in range(n - 1, -1, -1)}
        for i, o in enumerate(ops):
            for j, w in [(j, HOP + ops[j].get("lat", 0)) for j in o["dp"]] + [(j, 0.0) for j in o["od"]]:
                pre[i].append((j, w))
                post[j].append((i, w))
        prio = [0.0] * n
        for i in post:
            c = min([x[0] for x in ops[i]["alts"].values()] or [0])
            prio[i] = c + max([prio[j] + w for j, w in post[i]] + [ops[i].get("lat", 0)])
        seq, best = ordered([LAM * o["st"] + LATE.get(o["tag"], 0.0) + LATE.get(o["sub"], 0.0) - prio[i] for i, o in enumerate(ops)], pre), None
        for _ in range(PASSES):
            t0, c0, eng = place(ops, seq, pre, [None] * n)
            end = max(t0[i] + c0[i] + ops[i].get("lat", 0) for i in range(n))
            if best is None or end < best[0]:
                best = (end, t0, c0, eng)
            b0, d0, _e = place(ops, ordered([-t0[i] - c0[i] for i in range(n)], post), post, eng)
            seq = ordered([-b0[i] - d0[i] for i in range(n)], pre)
        REPORT.update(n=n, best=best, order=ordered(best[1], pre))
    end, t0, c0, eng = REPORT["best"]
    for i, o in enumerate(ops):
        o["e"], o["t"] = eng[i], t0[i]
    return REPORT["order"]


def rank_program(g, core, T, topo):
    if T.rank_of(core) is None:
        return
    ops, Q = build(g, core, T, topo)
    depend(ops)
    order = schedule(ops)
    needed = set(j for o in ops for j in o["dp"])
    count, final = {}, {}
    known = {q: {} for q in Q}
    for i in order:
        o = ops[i]
        e = o["e"]
        if e is None:
            o["tok"], o["clk"] = o["sem"], {}
            final[o["sem"][0]] = o["sem"][1]
            continue
        kn = known[e]
        for j in sorted(o["dp"], key=lambda k: -ops[k]["t"]):
            s, v = ops[j]["tok"]
            if kn.get(s, 0) < v:
                Q[e].wait_ge(T.sem[s], v)
                kn[s] = v
            for s2, v2 in ops[j]["clk"].items():
                if kn.get(s2, 0) < v2:
                    kn[s2] = v2
        o["clk"] = dict(kn)
        ins = o["alts"][e][1]()
        if "sem" in o:
            o["tok"] = o["sem"]
            final[o["sem"][0]] = o["sem"][1]
        elif i in needed:
            s = ESEM[e]
            for x in ins if isinstance(ins, list) else [ins]:
                count[s] = count.get(s, 0) + 1
                x.then_inc(T.sem[s], 1)
            o["tok"] = (s, count[s])
            final[s] = count[s]
    for s, v in final.items():
        if known["g"].get(s, 0) < v:
            g.wait_ge(T.sem[s], v)
